import numpy as np, ml_dtypes
CORES = [35,38,43,46]
N = 4
import mx_ref
BF = ml_dtypes.bfloat16
def gentries(a):
    return np.ascontiguousarray(a.reshape(8, 16, -1).transpose(0, 2, 1)).reshape(8, -1)
def gtable(e):
    e = np.asarray(e); return np.ascontiguousarray(e.reshape(8, -1, 16).transpose(0, 2, 1)).reshape(128, -1).astype(np.int32)
def gcols(t, e):
    v = np.concatenate([t.reshape(8, 16, -1, 4), np.zeros((8, 16, 1, 4), BF)], axis=2)
    return np.ascontiguousarray(np.stack([v[g][:, e[g]] for g in range(8)])).reshape(128, -1)
def gpick(z, e):
    return np.concatenate([z[16 * g:16 * g + 16][:, e[g]] for g in range(8)])
def tile(rs):
    return np.stack(rs, axis=2).reshape(128, -1).astype(BF)
def pick(q, e):
    c = np.concatenate([q[0].reshape(128, -1, 4), np.zeros((128, 1, 4), np.uint8)], axis=1); s = np.concatenate([q[1], np.ones((16, 1), np.uint8)], axis=1)
    return (np.ascontiguousarray(c[:, e].reshape(128, -1)), np.ascontiguousarray(s[:, e]))
def join(*qs):
    return (np.concatenate([q[0] for q in qs], axis=1), np.concatenate([q[1] for q in qs], axis=1))
def put(q, e, v):
    c, s = q[0].reshape(128, -1, 4).copy(), q[1].copy(); c[:, e] = v[0].reshape(128, -1, 4); s[:, e] = v[1]
    return (c.reshape(128, -1), s)
def pk(c, s):
    return (np.ascontiguousarray(c), mx_ref.live(s))
def emit(q):
    return q[0], q[1]
def packed(v, rng):
    q = [mx_ref.quantize(np.ascontiguousarray(v[r])) for r in range(N)]
    return np.stack([a for a, b in q]), np.stack([mx_ref.plane(b, rng) for a, b in q])
def values_of_codes():
    e, c = np.zeros((128, 128, 4), np.float32), np.zeros((128, 2, 4), np.uint8)
    e[np.arange(128), np.arange(128), 0] = 1
    c[:127, :, 0] = np.arange(256).reshape(2, 128).T[:127]
    return mx_ref.matmul(mx_ref.quantize(e.reshape(128, 512).astype(BF)), (c.reshape(128, 8), np.full((16, 2), 127, np.uint8))).T.reshape(-1).astype(np.float64)
CODE_VALUE, SCALE_VALUE = values_of_codes(), 2.0 ** (np.arange(256) - 127.0)
def decode(q):
    return (CODE_VALUE[q[0]].reshape(16, 8, -1, 4) * SCALE_VALUE[q[1]][:, None, :, None] + 0.0).reshape(128, -1).astype(np.float32)
def f(rng, *shape):
    return mx_ref.flush((rng.standard_normal(shape, dtype=np.float32) * np.exp2(rng.integers(-2, 3, shape[:-1] + (1,)))).astype(BF))
def wide(rng, *shape, cols=0):
    v = rng.standard_normal(shape, dtype=np.float32) * np.exp2(rng.integers(-12, 13, shape)).astype(np.float32)
    if cols: v *= np.repeat(np.exp2(rng.integers(-cols, cols + 1, shape[:-2] + (1, shape[-1] // 4))) * (rng.random(shape[:-2] + (1, shape[-1] // 4)) > 0.0625), 4, axis=-1).astype(np.float32)
    return mx_ref.flush(v.astype(BF))
C = 384
STEP = [2, 3, 1]
def numbers_of(rng):
    return {"x": np.array(f(rng, N, 128, 4 * C)), "u": np.array(f(rng, N, 128, 512)), "v": np.array(f(rng, N, 128, 512))}
def orders(rng):
    return rng.permuted(np.tile(np.arange(C), (N, 8, 1)), axis=2), rng.permuted(np.tile(np.arange(8)[:, None], (N, 1, C)), axis=1)
def stored(p, o):
    return {"pg": np.stack([gtable(p[r]) for r in range(N)]), "og": np.stack([gtable(o[r]) for r in range(N)])}
def layers(rng, still=[]):
    w = np.array(f(rng, N, 128, 2048)).reshape(N, 8, 16, 4, 8, 16, 4)
    for i in still:
        w[:, :, i] = 0
        w[:, :, :, :, :, i] = 0
    return w
def weights(rng, w):
    c, s = packed(np.ascontiguousarray(w).reshape(N, 128, 2048), rng)
    return {"wc": c, "ws": s}
def setup_inputs(rng):
    return {**numbers_of(rng), **stored(*orders(rng)), **weights(rng, layers(rng))}
def setup_inputs_ties(rng):
    d = numbers_of(rng)
    n = rng.permutation(N)
    k = rng.integers(0, 4, (N, 8, C))
    k[n[1]] -= 4
    k[n[2]] = np.arange(8)[:, None]
    x = d["x"].reshape(N, 8, 16, C, 4)
    x[:, :, 0] = 0
    x[:, :, 0, :, 0] = k.astype(np.float32).astype(BF)
    u = d["u"].reshape(N, 128, 128, 4)
    u[:, :, ::16] = 0
    for r in range(N):
        for h in range(0, 128, 16): u[r, h, h, 0] = 0.0 if r == n[0] else 1.0
    p, o = orders(rng)
    o[n[2]] = 7 - np.arange(8)[:, None]
    return {"x": x.reshape(N, 128, 4 * C), "u": u.reshape(N, 128, 512), "v": d["v"], **stored(p, o), **weights(rng, layers(rng, [0]))}
def setup_inputs_near(rng):
    d = numbers_of(rng)
    x = d["x"].astype(np.float32).reshape(N, 8, 16, C, 4)
    x[:, :, 0] = 0
    x[:, :, 8:] = 0
    u = d["u"].reshape(N, 128, 128, 4)
    u[:, :, ::16] = 0
    w = layers(rng, [0, 8, 9, 10, 11, 12, 13, 14, 15])
    kind, size, least = np.zeros(N, np.int64), np.ones(N), 2.0 ** -30
    turn = rng.integers(2)
    for i, r in enumerate(rng.permutation([r for r in range(N) if r < r ^ STEP[0]])):
        both = [r, r ^ STEP[0]]
        kind[both] = 2 if i == 0 else rng.permutation(2)
        size[both] = least if (i + turn) % 2 else 1.0
    for r in range(N):
        s = rng.integers(0, 16, (8, C))
        digits = ((s[:, :, None] >> np.arange(4)) & 1) * np.exp2(np.arange(4) - 23.0)
        if kind[r] == 0:
            x[r, :, 0, :, 0] = rng.choice([-1.0, 1.0])
            x[r, :, 8] = digits
            x[r, :, 11, :, 0] = 2.0 ** -10
        if kind[r] == 1: x[r, :, 8] = digits * rng.choice([-1.0, 1.0], (8, C, 1))
        if kind[r] == 2:
            e = rng.integers(-1, 2, (8, C)) * least
            x[r, :, 8, :, 0] = 1.25 * e
            x[r, :, 9, :, 0] = -1.125 * e
            x[r, :, 13, :, 0] = rng.choice([-1.0, 1.0], (8, C)) * least
            for g in range(8): w[r, g, 13, 0, g, 12, 0] = 2.0 ** -8
        for g, j in zip(rng.permutation(8)[:4], [0, C - 1, int(rng.integers(C)), int(rng.integers(C))]): x[r, g, 0, j, 0] = 2.0 ** 29 * rng.choice([-1.0, 1.0])
        k = size[r] if kind[r] == 0 else least
        for h in range(0, 128, 16):
            u[r, h, h, 0] = k if kind[r] == 0 else 1.0
            if kind[r] == 0: u[r, h + 11, h, 0] = k
            if kind[r] < 2: u[r, h + 8, h] = k
            else:
                u[r, h + 8, h, 0] = k
                u[r, h + 9, h, 0] = 1.125 * k
                u[r, h + 12, h, 0] = k
    return {"x": x.reshape(N, 128, 4 * C).astype(BF), "u": u.reshape(N, 128, 512), "v": d["v"], **stored(*orders(rng)), **weights(rng, w)}
def setup_inputs_odd(rng):
    d = numbers_of(rng)
    x = (1.0 + (2 * rng.integers(0, 64, (N, 16, 8, C, 4)) + 1) * 2.0 ** -7) * np.exp2(-rng.integers(0, 7, (N, 16, 8, C, 4)).astype(np.float64)) * rng.choice([-1.0, 1.0], (N, 16, 8, C, 4))
    x[:, :, 0, :, 0] = 1.96875 * 2.0 ** 8 * rng.choice([-1.0, 1.0], (16, 1))
    u = d["u"].reshape(N, 16, 8, 128, 4)
    u[:, :, 0, ::16] = 0
    w = layers(rng, [0, 8])
    for g in range(8):
        for i in (0, 8): w[:, g, i, 0, g, i, 0] = -0.5
    return {"x": x.astype(np.float32).reshape(N, 128, 4 * C).astype(BF), "u": u.reshape(N, 128, 512), "v": d["v"], **stored(*orders(rng)), **weights(rng, w)}
def setup_inputs_ends(rng):
    d = numbers_of(rng)
    n, e, c = [rng.permutation(N) % 4 for _ in range(3)]
    low, tiny = 2.0 ** 29, 2.0 ** -30
    def small(*s): return (1 + 0.125 * rng.integers(0, 8, s)) * tiny
    x = np.zeros((N, 8, 16, C, 4))
    u = d["u"].astype(np.float32).reshape(N, 8, 16, 128, 4)
    v = d["v"].astype(np.float32)
    w = np.zeros((N, 128, 4, 128, 4), np.float32)
    i = np.arange(128)
    p, o = orders(rng)
    for r in range(N):
        h = rng.permutation(8)
        a = np.where(h < 2, 0.0, h % 2 * 2.0 - 1.0)[:, None]
        k = np.full(16, 4.0)
        k[15] = 0
        if n[r] < 2:
            x[r] = -(1 + 0.125 * rng.integers(0, 4, (8, 16, C, 4))) * low
            if n[r] == 1: x[r] *= rng.choice([-1.0, 1.0], (C, 1))
            x[r, :, 15] = 2.0 ** 16 * rng.choice([-1.0, 1.0], (8, C, 4))
            u[r, :, :, ::16] = a * 2.0 ** 30
            v[r] = rng.choice([-1.0, 1.0], (128, 512)) * (1 + 0.125 * rng.integers(4, 9, (128, 512))) * low
        elif n[r] == 2:
            x[r] = -small(8, 16, C, 4)
            u[r, :, :, ::16] = a * small(8, 16, 8, 4)
            u[r, :, 14:, ::16] = 0
            v[r] = rng.choice([-1.0, 1.0], (128, 512)) * small(128, 512)
            k[:] = 0
            k[14], k[15] = 2.0 ** -8, 2.0 ** 8
        else:
            x[r] = d["x"][r].astype(np.float32).reshape(8, 16, C, 4)[:, :, :1]
            u[r, :, :, ::16] *= np.abs(a).astype(np.float32)
        for b in range(4): w[r, i, b, i, b] = np.tile(k, 8)
        if e[r] < 3: p[r] = [np.arange(C), np.arange(C)[::-1], (np.arange(C) + 1) % C][e[r]]
        up = np.arange(8)[:, None]
        if c[r] < 3: o[r] = np.where([np.ones(C, bool), np.zeros(C, bool), rng.random(C) < 0.5][c[r]], up, 7 - up)
    return {"x": x.astype(np.float32).reshape(N, 128, 4 * C).astype(BF), "u": u.reshape(N, 128, 512).astype(BF), "v": v.astype(BF), **stored(p, o), **weights(rng, w.astype(BF))}
def setup_inputs_spread(rng):
    d = setup_inputs(rng)
    d["x"] = wide(rng, N, 128, 4 * C, cols=6)
    return d
def check_inputs(d):
    b = []
    for k in ("x", "u", "v"):
        a = np.abs(d[k].astype(np.float32))
        if not (np.isfinite(a).all() and ((a == 0) | (a >= 2.0 ** -30) & (a <= 2.0 ** 30)).all()): b.append("a value of " + k)
    none, least, most = [emit(mx_ref.quantize(np.full((128, 16), k, np.float32).astype(BF)))[1][0, 0] for k in (0.0, 2.0 ** -8, 2.0 ** 8)]
    for r in range(N):
        if not (np.sort(gentries(d["pg"][r]), axis=1) == np.arange(C)).all(): b.append("pg: a group's entries aren't all columns")
        if not (np.sort(gentries(d["og"][r]), axis=0) == np.arange(8)[:, None]).all(): b.append("og: a column's entries aren't all groups")
        if ((d["wc"][r] == 0x7F) | (d["wc"][r] == 0xFF)).any(): b.append("wc: a code that is no number")
        s = mx_ref.live(d["ws"][r])
        if ((s != none) & ((s < least) | (s > most))).any(): b.append("ws: a scale out of range")
        if (((d["wc"][r].reshape(16, 8, 512, 4) & 0x7F) != 0) & (s == none)[:, None, :, None]).any(): b.append("wc: a code other than zero under the scale of zeros")
    return b
def walk(p, o):
    a, at = np.arange(C), np.zeros((8, C), np.int64)
    for k in range(8):
        a = p[o[k], a]
        at[o[k], np.arange(C)] = a
    return at
def reference(x, u, v, pg, og, wc, ws):
    qu = [mx_ref.quantize(u[r]) for r in range(N)]
    lay = [pk(wc[r], ws[r]) for r in range(N)]
    p, o = [np.array(gentries(pg[r])) for r in range(N)], [np.array(gentries(og[r])) for r in range(N)]
    at = [walk(p[r], o[r]) for r in range(N)]
    now = [x[r] for r in range(N)]
    for t, step in enumerate(STEP):
        held, z = [], []
        for r in range(N):
            q = mx_ref.quantize(now[r])
            held.append(decode(q))
            s = mx_ref.matmul(qu[r], q)[::16]
            c = s[o[r], at[r][o[r], np.arange(C)]]
            for k in range(t % 2, 7, 2):
                turn = c[k] > c[k + 1]
                o[r][k], o[r][k + 1] = np.where(turn, o[r][k + 1], o[r][k]), np.where(turn, o[r][k], o[r][k + 1])
            at[r] = walk(p[r], o[r])
            z.append(mx_ref.quantize(gcols(held[r].astype(BF), at[r])))
        for r in range(N):
            e = np.take_along_axis(p[r], at[r], axis=1)
            now[r] = tile([held[r][:, b::4] + gpick(mx_ref.matmul(pick(lay[r], np.arange(128 * b, 128 * b + 128)), z[r ^ step]) * np.float32(0.03125), e) for b in range(4)])
    y, ol = np.zeros((N, 128, C), np.float32), np.zeros((N, 8, C), np.float32)
    oc, osc = np.zeros((N, 128, 4 * C), np.uint8), np.zeros((N, 16, C), np.uint8)
    for r in range(N):
        q = mx_ref.quantize(now[r])
        y[r] = mx_ref.matmul(mx_ref.quantize(v[r]), q)
        ol[r] = o[r]
        oc[r], osc[r] = emit(q)
    return {"y": y, "ol": ol, "oc": oc, "osc": osc}

@@ -1,0 +1,630 @@
+import numpy as np
+from concourse.mybir import dt, AluOpType, ActivationFunctionType
+
+C = 384
+HC = C // 2
+STEP = [2, 3, 1]
+NW = 512
+BASE = 8
+TW = BASE + 8 * NW
+OP = AluOpType
+COPY = ActivationFunctionType.Copy
+F32, BF, I32, U16, X4, U8 = "float32", "bfloat16", "int32", "uint16", "float8_e4m3fn_x4", "uint8"
+SMALL = {}
+for _n, _w in (("js", 4), ("jbm", 8), ("dd", 32), ("dd2", 32), ("d0", 8), ("mm", 32), ("mm2", 32), ("m0", 8), ("dv", 32), ("off0", 8), ("offsf", 8),
+               ("idxs", 8), ("y0", 8), ("y1", 8), ("yt", 8), ("yk", 8), ("t1", 8), ("t2", 8), ("t3", 8)):
+    SMALL[_n] = (sum(k[1] for k in SMALL.values()), _w)
+
+
+def _scratch():
+    s = {}
+
+    def sb(name, shape, d):
+        s[name] = ("sbuf", [128] + shape, d)
+    sb("pgi", [24], I32); sb("ogi", [24], I32); sb("pidx", [1], I32); sb("ti", [8], I32); sb("t24", [24], I32); sb("t24b", [24], I32)
+    sb("selu", [10], U16); sb("win", [16], F32); sb("wini", [16], I32)
+    sb("pgf", [32], F32); sb("pgt", [32], F32); sb("ogf", [32], F32); sb("ogt", [32], F32)
+    sb("cst", [16], F32); sb("one16", [16], F32); sb("mk8", [32], F32); sb("sm", [sum(k[1] for k in SMALL.values())], F32)
+    sb("ones", [512], BF); sb("ebt", [2048], BF); sb("ec", [512], X4); sb("ep", [512], U8)
+    sb("xb", [4 * C], BF); sb("ub", [512], BF); sb("vb16", [512], BF)
+    sb("uq0", [128], X4); sb("up0", [128], U8); sb("uc", [160], X4); sb("upl", [160], U8)
+    sb("vq", [128], X4); sb("vp", [128], U8); sb("wcod", [512], X4); sb("wpl", [512], U8)
+    sb("tab", [TW], F32); sb("sct", [8 * NW], F32)
+    for r in range(4):
+        sb("qc%d" % r, [C], X4); sb("qp%d" % r, [C], U8)
+        if r:
+            sb("xs%d" % r, [4 * C], BF)
+    for r in range(3):
+        sb("lc%d" % r, [C], X4); sb("lp%d" % r, [C], U8); sb("zl%d" % r, [24], U16); sb("al%d" % r, [24], U16)
+        sb("zc%d" % r, [C], X4); sb("zp%d" % r, [C], U8); sb("zt%d" % r, [4 * C], BF)
+    sb("fb", [3 * C], BF); sb("dp", [4 * C], BF); sb("rs", [4 * C], F32); sb("gs", [C], F32)
+    sb("oxd", [64], F32); sb("oxw", [256], F32); sb("ox", [4, 2, 32], F32)
+    sb("oe", [32], F32); sb("oo", [32], F32); sb("idxf", [64], F32); sb("idxu", [64], U16); sb("idxsu", [8], U16)
+    sb("offu", [64], U16); sb("wk", [1024], F32); sb("tt", [1024], F32); sb("rep", [1024], F32)
+    sb("vs", [32], F32); sb("vadr", [32], F32); sb("eb", [32], U16)
+    sb("ev", [512], F32); sb("bt", [256], BF); sb("bd", [16, 2, 16], BF); sb("btt", [512], BF)
+    sb("brep", [512], F32); sb("brt", [512], F32); sb("lb", [32], F32)
+    sb("zm", [192], F32); sb("offs", [16], U16); sb("reps", [128], F32); sb("wks", [256], F32); sb("tts", [256], F32)
+    for k in ("A", "B"):
+        sb("lt" + k, [32], F32); sb("xd" + k, [64], F32); sb("xw" + k, [192], F32); sb("xx" + k, [192], F32)
+        sb("cl" + k, [192], F32); sb("sc" + k, [192], F32)
+    sb("bl", [24], U16)
+    sb("olf", [32], F32); sb("olg", [32], F32); sb("olt", [32], F32); sb("ys", [C], F32)
+    s["ps"] = ("psum", [128, 4096], F32)
+    return s
+
+
+SCRATCH = _scratch()
+SEMAPHORES = (["qv", "qs", "qt", "qg", "loc", "d_pg", "d_og", "d_x", "d_u", "d_w", "d_v", "d_t", "d_o", "d_ol", "d_y0", "d_y1"]
+              + ["rq%d" % r for r in range(3)] + ["ra%d" % r for r in range(3)])
+
+
+def make_queue_tools(g, T):
+    eng = {"v": g.vector, "s": g.scalar, "t": g.tensor, "g": g, "y": g.sync}
+    own = {"v": "qv", "s": "qs", "t": "qt", "g": "qg"}
+    count = {k: 0 for k in SEMAPHORES}
+    known = {k: {} for k in eng}
+    clock = {}
+    hist = {}
+    bits = {}
+
+    def region(ref):
+        name, idx = ref
+        key = (name, str(idx))
+        if key not in bits:
+            if name == "ps":
+                bits[key] = (0, 128, 1 << idx)
+            else:
+                shape = SCRATCH[name][1][1:]
+                n = 1
+                for k in shape:
+                    n *= k
+                a = np.arange(n).reshape(shape)
+                sel = np.zeros(n, np.uint8)
+                sel[a[idx[1:]].reshape(-1)] = 1
+                m = int.from_bytes(np.packbits(sel, bitorder="little").tobytes(), "little")
+                bits[key] = (idx[0].start or 0, idx[0].stop or 128, m)
+        return bits[key]
+
+    def learn(q, ev):
+        k = known[q]
+        for s, n in clock[ev].items():
+            if k.get(s, 0) < n:
+                k[s] = n
+
+    def need(q, events):
+        todo = [e for e in set(events) if known[q].get(e[0], 0) < e[1]]
+        todo = [e for e in todo if not any(f != e and clock[f].get(e[0], 0) >= e[1] for f in todo)]
+        for e in sorted(todo):
+            if known[q].get(e[0], 0) < e[1]:
+                eng[q].wait_ge(T.sem[e[0]], e[1])
+                learn(q, e)
+
+    def deps(q, ins, outs):
+        ev = []
+        for refs, write in ((ins, False), (outs, True)):
+            for ref in refs:
+                p0, p1, m = region(ref)
+                for (h0, h1, hm, hw, hq, he) in hist.get(ref[0], ()):
+                    if (hw or write or ref[0] == "ps" and hq != q) and h0 < p1 and p0 < h1 and hm & m:
+                        if not hw and hq == q:
+                            continue
+                        ev.append(he)
+        return ev
+
+    def note(q, ev, ins, outs):
+        for refs, write in ((ins, False), (outs, True)):
+            for ref in refs:
+                p0, p1, m = region(ref)
+                lst = hist.setdefault(ref[0], [])
+                if write:
+                    lst[:] = [h for h in lst if not (p0 <= h[0] and h[1] <= p1 and (h[2] & ~m) == 0)]
+                lst.append((p0, p1, m, write, q, ev))
+
+    def op(q, call, outs, ins):
+        need(q, deps(q, ins, outs))
+        sem = own[q]
+        count[sem] += 1
+        ev = (sem, count[sem])
+        call().then_inc(T.sem[sem], 1)
+        clock[ev] = dict(known[q])
+        clock[ev][sem] = count[sem]
+        note(q, ev, ins, outs)
+
+    def dmas(sem, items):
+        count[sem] += 16 * len(items)
+        ev = (sem, count[sem])
+        clock[ev] = {sem: count[sem]}
+        for q, out, in_, outs, ins in items:
+            need(q, [e for e in deps(q, ins, outs) if e != ev])
+            eng[q].dma_start(out, in_).then_inc(T.sem[sem], 16)
+            for s, n in known[q].items():
+                if clock[ev].get(s, 0) < n:
+                    clock[ev][s] = n
+        for q, out, in_, outs, ins in items:
+            note("dma", ev, ins, outs)
+
+    def send(call, ins, n):
+        need("g", deps("g", ins, []))
+        call()
+        count["loc"] += n
+        clock[("loc", count["loc"])] = {"loc": count["loc"]}
+
+    def arrives(sem, n, outs):
+        count[sem] += n
+        ev = (sem, count[sem])
+        clock[ev] = {sem: count[sem]}
+        note("remote", ev, [], outs)
+
+    def finish():
+        for s in SEMAPHORES:
+            if count[s] and known["g"].get(s, 0) < count[s]:
+                g.wait_ge(T.sem[s], count[s])
+    return op, dmas, send, arrives, finish
+
+
+def rank_program(g, core, T, topo):
+    rank = T.rank_of(core)
+    if rank is None:
+        return
+    op, dmas, send, arrives, finish = make_queue_tools(g, T)
+    S_ = slice
+    ANY = slice(None)
+
+    def R(name, *idx, p=slice(0, 128)):
+        if name in SMALL:
+            o, n = SMALL[name]
+            i = idx[0] if idx else slice(0, n)
+            name, idx = "sm", (slice(o + i.start, o + i.stop, i.step),)
+        return (name, (p,) + tuple(idx)) if idx else (name, (p,) + tuple(ANY for _ in SCRATCH[name][1][1:]))
+
+    def V(ref):
+        return T[ref[0]][ref[1]]
+
+    def bank(k, n):
+        return T.ps[:, 512 * k:512 * k + n]
+
+    def cp(q, out, in_, scale=None):
+        if q == "v":
+            op(q, lambda: g.vector.tensor_copy(V(out), V(in_)), [out], [in_])
+        elif scale is None:
+            op(q, lambda: g.scalar.activation(V(out), V(in_), COPY), [out], [in_])
+        else:
+            op(q, lambda: g.scalar.activation(V(out), V(in_), COPY, scale=V(scale)), [out], [in_, scale])
+
+    def frombank(q, out, k, n=C, scale=None):
+        if q == "v" and scale is None:
+            op(q, lambda: g.vector.tensor_copy(V(out), bank(k, n)), [out], [("ps", k)])
+        elif q == "v":
+            op(q, lambda: g.vector.tensor_scalar(V(out), bank(k, n), scale, None, OP.mult), [out], [("ps", k)])
+        elif scale is None:
+            op(q, lambda: g.scalar.activation(V(out), bank(k, n), COPY), [out], [("ps", k)])
+        else:
+            op(q, lambda: g.scalar.activation(V(out), bank(k, n), COPY, scale=scale), [out], [("ps", k)])
+
+    def gather(q, out, win, off):
+        if q == "v":
+            op(q, lambda: g.vector.tensor_copy(V(out), V(win).indirect(V(off))), [out], [win, off])
+        else:
+            op(q, lambda: g.scalar.activation(V(out), V(win).indirect(V(off)), COPY), [out], [win, off])
+
+    def gather_add(out, win, off, in1):
+        op("v", lambda: g.vector.tensor_tensor(V(out), V(win).indirect(V(off)), V(in1), OP.add), [out], [win, off, in1])
+
+    def tt(out, a, b, o):
+        op("v", lambda: g.vector.tensor_tensor(V(out), V(a), V(b), o), [out], [a, b])
+
+    def ts(out, a, s1, s2, o0, o1=None):
+        v1 = V(s1) if isinstance(s1, tuple) else s1
+        v2 = V(s2) if isinstance(s2, tuple) else s2
+        ins = [a] + [s for s in (s1, s2) if isinstance(s, tuple)]
+        if o1 is None:
+            op("v", lambda: g.vector.tensor_scalar(V(out), V(a), v1, None, o0), [out], ins)
+        else:
+            op("v", lambda: g.vector.tensor_scalar(V(out), V(a), v1, v2, o0, o1), [out], ins)
+
+    def tr(out, in_):
+        op("v", lambda: g.vector.transpose(V(out), V(in_)), [out], [in_])
+
+    def ms(out, c):
+        op("v", lambda: g.vector.memset(V(out), c), [out], [])
+
+    def quant(oc_, op_, in_):
+        op("v", lambda: g.vector.quantize_mx(V(oc_), V(op_), V(in_)), [oc_, op_], [in_])
+
+    def mm(k, lc, lp, rc, rp, n=C):
+        op("t", lambda: g.tensor.matmul_mx(bank(k, n), V(lc), V(lp), V(rc), V(rp), True, True), [("ps", k)], [lc, lp, rc, rp])
+
+    def iota(out, pattern, base, cm, **kw):
+        op("g", lambda: g.iota(V(out), pattern, base, cm, **kw), [out], [])
+
+    def quadrant(a):
+        return slice(32 * a, 32 * a + 32)
+
+    def cols(name, a, n):
+        return R(name, S_(a, a + n))
+
+    def partner(r):
+        return T.cores[rank ^ STEP[r]]
+
+    def ways(src, dst):
+        return topo.engines(src, dst)[:8]
+
+    def remote(r, out, in_, sem, ins):
+        rid, pid, _ = topo.addr(partner(r))
+        e = ways(core, partner(r))
+        send(lambda: g.remote_dma(out, in_, T.sem[sem], T.sem.loc, pid, rid, sum(1 << k for k in e)), ins, len(e))
+
+    def q_of(r, a=0, n=C):
+        return cols("qc%d" % r, a, n), cols("qp%d" % r, a, n)
+
+    def send_state(r):
+        remote(r, T["lc%d" % r][:].bitcast(dt.uint8), T["qc%d" % r][:].bitcast(dt.uint8), "rq%d" % r, [R("qc%d" % r)])
+        remote(r, T["lp%d" % r][:], T["qp%d" % r][:], "rq%d" % r, [R("qp%d" % r)])
+
+    for r in range(3):
+        n = len(ways(partner(r), core))
+        arrives("rq%d" % r, 2 * n, [R("lc%d" % r), R("lp%d" % r)])
+        arrives("ra%d" % r, n, [R("zl%d" % r)])
+
+    dmas("d_pg", [("y", T.pgi[:], T.pg[:], [R("pgi")], [])])
+    dmas("d_og", [("s", T.ogi[:], T.og[:], [R("ogi")], [])])
+    dmas("d_x", [("y", T.xb[:], T.x[:], [R("xb")], [])])
+    dmas("d_u", [("s", T.ub[:], T.u[:], [R("ub")], [])])
+
+    def c1(k):
+        return cols("cst", k, 1)
+
+    def ti(k):
+        return cols("ti", k, 1)
+    iota(R("pidx"), [[0, 1]], 0, 1)
+    iota(R("wini"), [[NW, 16]], -8 * NW, 0)
+    ms(R("ones"), 1.0)
+    ms(cols("tab", 0, 1024), 0.0)
+    for k in (TW - 2048, TW - 1024):
+        cp("s", cols("tab", k, 1024), cols("tab", 0, 1024))
+    ms(cols("tab", 1024, TW - 3072), 0.0)
+    for b in range(4):
+        o = cols("ebt", 512 * b, 512)
+        op("g", lambda: g.affine_select(V(o), T.ones[:], [[-1, 512]], OP.is_equal, 0.0, b, 4), [o], [R("ones")])
+    ts(ti(0), R("pidx"), 4, 1, OP.arith_shift_right, OP.bitwise_and)
+    ts(ti(1), R("pidx"), 5, None, OP.arith_shift_right)
+    ms(R("pgf"), 0.0)
+    ts(c1(2), ti(0), 4.0, None, OP.mult)
+    ts(ti(2), R("pidx"), 15, None, OP.bitwise_and)
+    tt(c1(3), c1(2), ti(1), OP.add)
+    ms(R("ogf"), 0.0)
+    ts(c1(4), c1(3), float(NW), float(BASE), OP.mult, OP.add)
+
+    ts(cols("pgf", 0, 24), R("pgi"), c1(4), None, OP.add)
+    tr(R("pgt"), R("pgf"))
+    items = []
+    for G in range(6):
+        for h in range(2):
+            a, n = BASE + 4 * NW * h, 4 * NW
+            pr = slice(16 * G, 16 * G + 1)
+            items.append((("y", "s")[h], T.tab[pr, a:a + n], T.pgt[:, 16 * h:16 * h + 16],
+                          [R("tab", S_(a, a + n), p=pr)], [cols("pgt", 16 * h, 16)]))
+    dmas("d_t", items)
+    dmas("d_w", [("y", T.wcod[:].bitcast(dt.uint8), T.wc[:], [R("wcod")], []), ("y", T.wpl[:], T.ws[:], [R("wpl")], [])])
+    dmas("d_v", [("y", T.vb16[:], T.v[:], [R("vb16")], [])])
+
+    ts(R("t24"), R("ogi"), 1, None, OP.bitwise_and)
+    ts(R("t24b"), R("ogi"), 1, None, OP.arith_shift_right)
+    cp("v", c1(1), ti(0))
+    ts(c1(0), ti(0), -1.0, 1.0, OP.mult, OP.add)
+    ts(R("t24"), R("t24"), 4.0, None, OP.mult)
+    ms(R("one16"), 1.0)
+    ts(c1(7), ti(1), 128.0, None, OP.mult)
+    ts(c1(8), ti(0), 64.0, None, OP.mult)
+    tt(cols("ogf", 0, 24), R("t24"), R("t24b"), OP.add)
+    ts(ti(3), R("pidx"), 1, 3, OP.arith_shift_right, OP.bitwise_and)
+    cp("v", R("win"), R("wini"))
+    tt(c1(7), c1(7), c1(8), OP.add)
+    tr(R("ogt"), R("ogf"))
+    for h in range(2):
+        ts(R("mk8", S_(h, 32, 2)), R("one16"), c1(h), 8.0, OP.mult, OP.mult)
+    tt(c1(7), c1(7), ti(2), OP.add)
+    ms(cols("win", 0, 1), 0.0)
+
+    def spread(src, xd, xw, nsrc):
+        for H in range(2):
+            for h in range(2):
+                cp("vs"[H], cols(xd, 32 * h + 16 * H, 16), cols(src, 16 * h, 16))
+        k = 0
+        for a in range(nsrc):
+            for b in range(4):
+                cp("vs"[k % 2], R(xw, S_(64 * a, 64 * a + 64), p=quadrant(b)), R(xd, p=quadrant(a)))
+                k += 1
+
+    spread("ogt", "oxd", "oxw", 4)
+    for s in range(4):
+        ts(cols("js", s, 1), c1(7), 16.0 * s + BASE, None, OP.add)
+    cp("v", cols("idxf", 56, 8), cols("mk8", 0, 8))
+    for h in range(2):
+        ts(R("jbm", S_(h, 8, 2)), R("js"), c1(h), None, OP.mult)
+    ts(ti(4), R("pidx"), 3, 1, OP.arith_shift_right, OP.bitwise_and)
+    ts(c1(9), ti(3), 32.0, None, OP.mult)
+    ts(c1(10), ti(4), 16.0, None, OP.mult)
+    tr(R("ox"), R("oxw"))
+    tt(c1(9), c1(9), c1(10), OP.add)
+    ts(R("selu"), cols("one16", 0, 10), c1(9), None, OP.mult)
+    for par, name in ((0, "oe"), (1, "oo")):
+        for a in range(4):
+            for h in range(2):
+                o = R(name, S_(h, 32, 2), p=quadrant(a))
+                i = R("ox", ANY, par, S_(8 * a + 4 * h, 8 * a + 4 * h + 4), p=quadrant(a))
+                s = R("cst", S_(h, h + 1), p=quadrant(a))
+                if par:
+                    cp("s", o, i, s)
+                else:
+                    ts(o, i, s, None, OP.mult)
+    oe, oo, mk8 = R("oe"), R("oo"), R("mk8")
+    IE, IO = cols("idxf", 0, 32), cols("idxf", 32, 24)
+    tt(R("dd"), oo, oe, OP.subtract)
+    tt(IO, cols("oe", 8, 24), cols("oo", 0, 24), OP.subtract)
+    tt(IE, R("dd"), mk8, OP.add)
+    tt(IO, IO, cols("mk8", 0, 24), OP.add)
+    cp("v", R("idxu"), R("idxf"))
+    ts(R("off0"), cols("oe", 0, 8), float(NW), None, OP.mult)
+    tt(R("off0"), R("off0"), R("jbm"), OP.add)
+    cp("v", cols("offu", 0, 8), R("off0"))
+
+    KAP = [0, 4, 1, 5, 2, 6, 3, 7]
+
+    def rep(k):
+        gather("s", cols("rep", 128 * KAP[k], 128), R("win"), cols("idxu", 8 * KAP[k], 8))
+
+    def walk(first, fill):
+        for k in range(first, 8):
+            z = KAP[k]
+            blk, off = (128 * z, 128), cols("offu", 8 * z, 8)
+            if k < 7:
+                gather_add(cols("wk", *blk), R("tab"), off, cols("rep", *blk))
+                pause(fill)
+            else:
+                gather("v", cols("wk", *blk), R("tab"), off)
+                early_addresses(2)
+            tr(cols("tt", *blk), cols("wk", *blk))
+            if k < 6:
+                pause(fill)
+            elif k == 6:
+                early_addresses(0)
+            if k < 7:
+                cp("v", cols("offu", 8 * KAP[k + 1], 8), R("tt", S_(128 * z, 128 * z + 128, 16)))
+                if k == 6:
+                    early_addresses(1)
+                else:
+                    pause(fill)
+
+    def pause(fill):
+        if fill:
+            fill.pop(0)()
+
+    def differences():
+        return [lambda: tt(R("dv"), R("idxf", S_(0, 64, 2)), R("idxf", S_(1, 64, 2)), OP.add),
+                lambda: ts(R("dv"), R("dv"), -float(NW), 8.0 * NW, OP.mult, OP.add)]
+
+    def early_addresses(step):
+        if step == 0:
+            tt(cols("vs", 0, 28), R("tt", S_(0, 896, 32)), R("tt", S_(16, 896, 32)), OP.add)
+        elif step == 1:
+            tt(cols("vs", 0, 28), cols("vs", 0, 28), cols("dv", 0, 28), OP.add)
+        else:
+            for s in range(4):
+                cp("v", R("vadr", S_(8 * s, 8 * s + 7)), R("vs", S_(s, 28, 4)))
+
+    def last_address():
+        tt(R("vadr", S_(7, 32, 8)), R("tt", S_(896, 1024, 32)), R("tt", S_(912, 1024, 32)), OP.add)
+
+    def list_of_addresses():
+        ts(cols("eb", 0, 28), cols("vs", 0, 28), -float(BASE), None, OP.add)
+        ts(cols("eb", 28, 4), R("vadr", S_(7, 32, 8)), -float(BASE), None, OP.add)
+
+    def tt8(k):
+        return R("tt", S_(128 * KAP[k], 128 * KAP[k] + 128, 16))
+
+    def ahead(k, even):
+        w = 32 if even else 24
+        src = IE if even else IO
+        s0, s1 = R("tts", S_(0, 128, 16)), R("tts", S_(128, 256, 16))
+        nxt = cols("idxf", 8 * KAP[k + 1], 8)
+        return [
+            lambda: tt(cols("dd", 0, w), src, cols("mk8", 0, w), OP.subtract),
+            lambda: (ts(R("d0"), cols("dd", 0, 8), float(NW), None, OP.mult), tt(R("idxs"), cols("mk8", 0, 8), cols("dd", 0, 8), OP.subtract)),
+            lambda: (tt(R("offsf"), R("off0") if even else tt8(0), R("d0"), OP.add), cp("v", R("idxsu"), R("idxs"))),
+            lambda: (cp("v", cols("offs", 0, 8), R("offsf")), gather("s", R("reps"), R("win"), R("idxsu"))),
+            lambda: gather_add(cols("wks", 0, 128), R("tab"), cols("offs", 0, 8), R("reps")),
+            lambda: tr(cols("tts", 0, 128), cols("wks", 0, 128)),
+            lambda: cp("v", cols("offs", 8, 8), s0),
+            lambda: gather("v", cols("wks", 128, 128), R("tab"), cols("offs", 8, 8)),
+            lambda: tr(cols("tts", 128, 128), cols("wks", 128, 128)),
+            lambda: (tt(R("yk"), nxt, cols("mk8", 0, 8), OP.subtract), tt(R("yt"), s1, tt8(k + 1), OP.subtract),
+                     ts(cols("dd2", 0, w), cols("dd", 0, w), -2.0, None, OP.mult)),
+            lambda: (tt(R("yk"), R("yk"), cols("dd", 0, 8), OP.add), tt(R("y0"), s0, tt8(k), OP.subtract)),
+            lambda: (ts(R("yk"), R("yk"), float(NW), None, OP.mult), ts(R("t3"), cols("dd", 8, 8), float(NW), None, OP.mult)),
+            lambda: tt(R("y1"), R("yt"), R("yk"), OP.add),
+        ]
+
+    def select(k):
+        tr(R("xx" + k), R("xw" + k))
+        ts(R("cl" + k), R("xx" + k), c1(4), c1(5), OP.max, OP.min)
+
+    def totals(k):
+        op("v", lambda: g.vector.tensor_tensor_scan(V(R("sc" + k)), V(R("zm")), V(R("cl" + k)), 0.0, OP.mult, OP.add),
+           [R("sc" + k)], [R("zm"), R("cl" + k)])
+
+    def scores(r, x, a, n, q, k):
+        mm(k, cols("uc", 2 * x, 128), cols("upl", 2 * x, 128), *q_of(r, a, n), n)
+        frombank(q, cols("sct", NW * x + a, n), k, n)
+
+    def unpack(c, p, banks):
+        for b in range(4):
+            mm(banks + b, cols("ec", 128 * b, 128), cols("ep", 128 * b, 128), R(c), R(p))
+
+    for k in range(7):
+        rep(k)
+
+    def first_state():
+        quant(*q_of(0), R("xb"))
+        send_state(0)
+        for x in range(8):
+            iota(cols("sct", NW * x + C, NW - C), [[0, NW - C]], 0, 0, allow_small_or_imprecise_dtypes=True)
+
+    def scoring_columns():
+        op("v", lambda: g.vector.tensor_copy(T.uc[:].bitcast(dt.uint32), T.uq0[:].bitcast(dt.uint32).indirect(T.selu[:])),
+           [R("uc")], [R("uq0"), R("selu")])
+        op("s", lambda: g.scalar.activation(T.upl[:], T.up0[:].indirect(T.selu[:]), COPY), [R("upl")], [R("up0"), R("selu")])
+    aim = ahead(0, True)
+    fill = aim[:4] + [lambda: quant(R("uq0"), R("up0"), R("ub")), first_state, scoring_columns] + differences() + aim[4:] + [
+        lambda: ms(R("zm"), 1.0),
+        lambda: ms(R("zm", S_(0, 192, 8)), 0.0),
+        lambda: ts(c1(5), c1(4), float(NW), None, OP.add),
+        lambda: ts(c1(6), c1(3), 7.0 * NW, 7.0 * NW + 8 * BASE, OP.mult, OP.add)]
+    walk(0, fill)
+    for x in range(8):
+        scores(0, x, 0, C, "s", x)
+    last_address()
+    list_of_addresses()
+
+    for r in range(3):
+        odd = r == 1
+        for k in range(2):
+            gather("vs"[k], cols("ev", 256 * k, 256), R("sct"), cols("eb", 16 * k, 16))
+        while fill:
+            pause(fill)
+        if r == 0:
+            quant(R("ec"), R("ep"), R("ebt"))
+        unpack("qc%d" % r, "qp%d" % r, 0)
+        for b in range(3):
+            frombank("s", cols("fb", C * b, C), b)
+        n = 12 if odd else 16
+        if odd:
+            tt(cols("bt", 0, 192), cols("ev", 256, 192), cols("ev", 64, 192), OP.is_gt)
+        else:
+            tt(R("bt"), cols("ev", 0, 256), cols("ev", 256, 256), OP.is_gt)
+        for h in range(2):
+            ts(R("bd", S_(0, n), h, ANY), cols("bt", 0, 16 * n), c1(h), None, OP.mult)
+        tr(cols("btt", 0, 32 * n), R("bd", S_(0, n), ANY, ANY))
+        bm, bm0, bm1 = R("btt", S_(0, 32 * n, 16)), R("btt", S_(0, 128, 16)), R("btt", S_(128, 256, 16))
+        m, m2 = cols("mm", 0, 2 * n), cols("mm2", 0, 2 * n)
+        mine = IO if odd else IE
+        first = 1 if odd else 0
+        t0, t1, t2 = tt8(0), tt8(first), tt8(first + 1)
+        tt(m2, bm, cols("dd2", 0, 2 * n), OP.mult)
+        tt(R("t1"), bm0, R("y1"), OP.mult)
+        tt(R("t2"), bm1, R("t3"), OP.mult)
+        tt(mine, mine, m2, OP.add)
+        tt(t2, t2, R("t1"), OP.add)
+        tt(m, bm, cols("dd", 0, 2 * n), OP.mult)
+        if odd:
+            cp("v", cols("idxu", 32, 24), IO)
+        else:
+            cp("v", cols("idxu", 0, 32), IE)
+        tt(t2, t2, R("t2"), OP.add)
+        rep(first + 2)
+        a, k = (0, 32) if odd else (32, 24)
+        if odd:
+            tt(cols("idxf", 0, 24), cols("idxf", 0, 24), m, OP.add)
+        else:
+            tt(IO, IO, cols("mm", 8, 24), OP.add)
+        cp("v", cols("offu", 8 * KAP[first + 2], 8), t2)
+        if odd:
+            tt(cols("idxf", 8, 24), cols("idxf", 8, 24), m, OP.add)
+        else:
+            tt(IO, IO, cols("mm", 0, 24), OP.add)
+        tt(R("m0"), bm0, R("d0"), OP.mult)
+        cp("v", cols("idxu", a, k), cols("idxf", a, k))
+        for k in range(first + 3, 7):
+            rep(k)
+        up, dn = (OP.subtract, OP.add) if odd else (OP.add, OP.subtract)
+        E, O = (cols("oe", 8, 24), cols("oo", 0, 24)) if odd else (oe, oo)
+        f0 = t0 if odd else R("off0")
+        diff = differences()
+        fill = [lambda: (tt(R("y0"), bm0, R("y0"), OP.mult), tt(f0, f0, R("m0"), OP.add)), lambda: (tt(t1, t1, R("y0"), OP.add), diff[0]())]
+        fill += ahead(0 if odd else 1, odd) if r < 2 else []
+        orders = lambda: (tt(O, O, m, dn), tt(E, E, m, up))
+        fill.insert(3, lambda: (diff[1](), orders()))
+        if r == 0:
+            fill.append(lambda: quant(R("vq"), R("vp"), R("vb16")))
+        walk(first + 2, fill)
+        last_address()
+        tr(R("ltA"), R("vadr"))
+        list_of_addresses()
+        spread("ltA", "xdA", "xwA", 3)
+        gather("s", R("brep"), cols("tab", BASE, TW - BASE), R("eb"))
+        select("A")
+        totals("A")
+        ts(R("al%d" % r), R("scA", S_(7, 192, 8)), c1(6), None, OP.subtract)
+        remote(r, T["zl%d" % r][:], T["al%d" % r][:], "ra%d" % r, [R("al%d" % r)])
+        unpack("lc%d" % r, "lp%d" % r, 4)
+        for b in range(2):
+            frombank("s", cols("dp", C * b, C), 4 + b)
+        tr(R("brt"), R("brep"))
+        for k in range(4):
+            cp("v", cols("lb", 8 * k, 8), R("brt", S_(16 * k, 512, 64)))
+        tr(R("ltB"), R("lb"))
+        spread("ltB", "xdB", "xwB", 3)
+        for b in range(2, 4):
+            frombank("s", cols("dp", C * b, C), 4 + b)
+        select("B")
+        if r == 2:
+            tt(cols("olf", 0, 16), R("oe", S_(0, 32, 2)), R("oe", S_(1, 32, 2)), OP.add)
+            tt(cols("olf", 16, 16), R("oo", S_(0, 32, 2)), R("oo", S_(1, 32, 2)), OP.add)
+            ts(R("olg"), R("olf"), 4.0, -7.0, OP.is_ge, OP.mult)
+            tt(R("olf"), R("olf"), R("olf"), OP.add)
+            tt(R("olf"), R("olf"), R("olg"), OP.add)
+            tr(R("olt"), R("olf"))
+            items = []
+            for a in range(3):
+                for par in range(2):
+                    for h in range(2):
+                        p = slice(32 * a + 16 * par, 32 * a + 16 * par + 16)
+                        c = 128 * a + 64 * h
+                        items.append(("y", T.ol[par:8:2, c:c + 64], T.olt[p, 16 * h:16 * h + 16], [], [R("olt", S_(16 * h, 16 * h + 16), p=p)]))
+            dmas("d_ol", items)
+        zt, zc, zp = "zt%d" % r, "zc%d" % r, "zp%d" % r
+        for h in range(2):
+            for b in (0, 2, 1, 3):
+                gather("vs"[b // 2], R(zt, S_(4 * HC * h + b, 4 * HC * (h + 1), 4)), cols("dp", C * b, C), cols("zl%d" % r, 12 * h, 12))
+        totals("B")
+        for h in range(2):
+            quant(cols(zc, HC * h, HC), cols(zp, HC * h, HC), cols(zt, 4 * HC * h, 4 * HC))
+        for k in range(4):
+            for l in range(2):
+                ts(R("bl", S_(4 * (k & 1) + (k & 2) + l, 24, 8)), R("scB", S_(32 * l + 8 * k + 7, 192, 64)), c1(6), None, OP.subtract)
+        for h in range(2):
+            mm(h, cols("wcod", 0, 128), cols("wpl", 0, 128), cols(zc, HC * h, HC), cols(zp, HC * h, HC), HC)
+            frombank("sv"[h], cols("rs", HC * h, HC), h, HC, 0.03125)
+        nx = "xs%d" % (r + 1)
+        for b, k in ((1, 2), (3, 5), (2, 4)):
+            mm(k, cols("wcod", 128 * b, 128), cols("wpl", 128 * b, 128), R(zc), R(zp))
+            frombank("s", cols("rs", C * b, C), k, C, 0.03125)
+        for h in range(2):
+            gather("s", cols("gs", HC * h, HC), cols("rs", 3 * C, C), cols("bl", 12 * h, 12))
+        for h in range(2):
+            for b in range(3):
+                gather_add(R(nx, S_(4 * HC * h + b, 4 * HC * (h + 1), 4)), cols("rs", C * b, C), cols("bl", 12 * h, 12), cols("fb", C * b + HC * h, HC))
+            o, i = R(nx, S_(4 * HC * h + 3, 4 * HC * (h + 1), 4)), cols("gs", HC * h, HC)
+            op("v", lambda: g.vector.tensor_tensor(V(o), V(i), T.ps[:, 512 * 3 + HC * h:512 * 3 + HC * h + HC], OP.add), [o], [i, ("ps", 3)])
+            quant(*q_of(r + 1, HC * h, HC), cols(nx, 4 * HC * h, 4 * HC))
+            if r < 2:
+                for x in range(8):
+                    if h == 0:
+                        scores(r + 1, x, 0, HC, "s", (0, 1, 2, 6, 7, 5, 4, 0)[x])
+                    else:
+                        scores(r + 1, x, HC, HC, "sv"[x % 2], x)
+                        pause(fill)
+            else:
+                mm(h, R("vq"), R("vp"), *q_of(3, HC * h, HC), HC)
+                frombank("sv"[h], cols("ys", HC * h, HC), h, HC)
+                dmas("d_y%d" % h, [("y", T.y[:, HC * h:HC * h + HC], T.ys[:, HC * h:HC * h + HC], [], [cols("ys", HC * h, HC)])])
+        while fill:
+            pause(fill)
+        if r < 2:
+            send_state(r + 1)
+
+    qc, qp = q_of(3)
+    dmas("d_o", [("s", T.oc[:], T.qc3[:].bitcast(dt.uint8), [], [qc])]
+         + [(("s", "y")[k % 2], T.osc[4 * k:4 * k + 4, :], T.qp3[32 * k:32 * k + 4, :], [], [qp]) for k in range(4)])
+    finish()

@@ -2,17 +2,16 @@ import numpy as np
 from concourse.mybir import dt, AluOpType, ActivationFunctionType
 
 C = 384
-HC = C // 2
 STEP = [2, 3, 1]
-NW = 512
-BASE = 8
-TW = BASE + 8 * NW
+ZP = [(0, 192), (192, 192)]
+XP = [(0, 192), (192, 192)]
+SHARE = 104
 OP = AluOpType
 COPY = ActivationFunctionType.Copy
 F32, BF, I32, U16, X4, U8 = "float32", "bfloat16", "int32", "uint16", "float8_e4m3fn_x4", "uint8"
 SMALL = {}
-for _n, _w in (("js", 4), ("jbm", 8), ("dd", 32), ("dd2", 32), ("d0", 8), ("mm", 32), ("mm2", 32), ("m0", 8), ("dv", 32), ("off0", 8), ("offsf", 8),
-               ("idxs", 8), ("y0", 8), ("y1", 8), ("yt", 8), ("yk", 8), ("t1", 8), ("t2", 8), ("t3", 8)):
+for _n, _w in (("cq", 12), ("cg", 12), ("ca", 12), ("ce", 12), ("cb", 12), ("jb", 4), ("ci", 4), ("cf", 8), ("cst", 8), ("e", 12), ("qq", 12),
+               ("t1", 12), ("df", 12), ("co", 12), ("m", 12), ("pr", 12), ("yy", 4), ("a0", 4), ("s1", 4), ("pos", 24)):
     SMALL[_n] = (sum(k[1] for k in SMALL.values()), _w)
 
 
@@ -21,15 +20,18 @@ def _scratch():
 
     def sb(name, shape, d):
         s[name] = ("sbuf", [128] + shape, d)
-    sb("pgi", [24], I32); sb("ogi", [24], I32); sb("pidx", [1], I32); sb("ti", [8], I32); sb("t24", [24], I32); sb("t24b", [24], I32)
-    sb("selu", [10], U16); sb("win", [16], F32); sb("wini", [16], I32)
-    sb("pgf", [32], F32); sb("pgt", [32], F32); sb("ogf", [32], F32); sb("ogt", [32], F32)
-    sb("cst", [16], F32); sb("one16", [16], F32); sb("mk8", [32], F32); sb("sm", [sum(k[1] for k in SMALL.values())], F32)
+    sb("li", [96], I32); sb("rt", [400], F32); sb("pl", [192], U16); sb("pidx", [1], I32); sb("ti", [8], I32); sb("t12", [16], I32)
+    sb("sm", [sum(k[1] for k in SMALL.values())], F32)
+    sb("lp_", [12], U16); sb("lb", [12], U16); sb("la", [18], U16); sb("le", [6], U16); sb("ld", [6], U16)
+    sb("lo", [2], U16); sb("lu", [8], U16); sb("d", [12], F32)
+    sb("sg", [96], F32); sb("mv", [112], F32); sb("h1", [3, 32], F32); sb("h2", [24], F32)
+    sb("iw", [C], F32); sb("im", [C], BF); sb("dm", [C], BF); sb("gca", [192], F32); sb("gcb", [192], F32)
+    sb("z32", [96], BF); sb("z16", [C], BF); sb("z8", [192], BF); sb("wgt", [192], F32)
     sb("ones", [512], BF); sb("ebt", [2048], BF); sb("ec", [512], X4); sb("ep", [512], U8)
     sb("xb", [4 * C], BF); sb("ub", [512], BF); sb("vb16", [512], BF)
-    sb("uq0", [128], X4); sb("up0", [128], U8); sb("uc", [160], X4); sb("upl", [160], U8)
+    sb("uq0", [128], X4); sb("up0", [128], U8); sb("uc", [128], X4); sb("upl", [128], U8)
     sb("vq", [128], X4); sb("vp", [128], U8); sb("wcod", [512], X4); sb("wpl", [512], U8)
-    sb("tab", [TW], F32); sb("sct", [8 * NW], F32)
+    sb("tab", [8 * C], F32); sb("sct", [C], F32)
     for r in range(4):
         sb("qc%d" % r, [C], X4); sb("qp%d" % r, [C], U8)
         if r:
@@ -37,25 +39,20 @@ def _scratch():
     for r in range(3):
         sb("lc%d" % r, [C], X4); sb("lp%d" % r, [C], U8); sb("zl%d" % r, [24], U16); sb("al%d" % r, [24], U16)
         sb("zc%d" % r, [C], X4); sb("zp%d" % r, [C], U8); sb("zt%d" % r, [4 * C], BF)
-    sb("fb", [3 * C], BF); sb("dp", [4 * C], BF); sb("rs", [4 * C], F32); sb("gs", [C], F32)
-    sb("oxd", [64], F32); sb("oxw", [256], F32); sb("ox", [4, 2, 32], F32)
-    sb("oe", [32], F32); sb("oo", [32], F32); sb("idxf", [64], F32); sb("idxu", [64], U16); sb("idxsu", [8], U16)
-    sb("offu", [64], U16); sb("wk", [1024], F32); sb("tt", [1024], F32); sb("rep", [1024], F32)
-    sb("vs", [32], F32); sb("vadr", [32], F32); sb("eb", [32], U16)
-    sb("ev", [512], F32); sb("bt", [256], BF); sb("bd", [16, 2, 16], BF); sb("btt", [512], BF)
-    sb("brep", [512], F32); sb("brt", [512], F32); sb("lb", [32], F32)
-    sb("zm", [192], F32); sb("offs", [16], U16); sb("reps", [128], F32); sb("wks", [256], F32); sb("tts", [256], F32)
-    for k in ("A", "B"):
-        sb("lt" + k, [32], F32); sb("xd" + k, [64], F32); sb("xw" + k, [192], F32); sb("xx" + k, [192], F32)
-        sb("cl" + k, [192], F32); sb("sc" + k, [192], F32)
-    sb("bl", [24], U16)
-    sb("olf", [32], F32); sb("olg", [32], F32); sb("olt", [32], F32); sb("ys", [C], F32)
+    sb("fb", [2 * C], BF); sb("dp", [4 * C], BF); sb("rs", [4 * C], F32); sb("gs", [2 * C], F32)
+    sb("lab", [32], F32); sb("wk", [768], F32); sb("of", [8 * 96], F32); sb("offu", [32], U16)
+    sb("wks", [192], F32); sb("ofs", [192], F32); sb("offs", [8], U16)
+    sb("wa", [C], F32); sb("wo", [C], F32); sb("wt", [3, 8, 16], F32); sb("lf", [24], F32)
+    sb("eq", [192], F32); sb("iv", [192], F32); sb("inv", [24], U16); sb("oh", [192], F32)
+    sb("eb", [24], U16); sb("ef", [C], F32); sb("et", [C], F32); sb("sel", [96], F32); sb("es", [96], F32)
+    sb("ab", [24], U16); sb("bg", [C], F32); sb("bs", [C], F32); sb("bl", [24], U16)
+    sb("olf", [32], F32); sb("olt", [32], F32); sb("ys", [C], F32)
     s["ps"] = ("psum", [128, 4096], F32)
     return s
 
 
 SCRATCH = _scratch()
-SEMAPHORES = (["qv", "qs", "qt", "qg", "loc", "d_pg", "d_og", "d_x", "d_u", "d_w", "d_v", "d_t", "d_o", "d_ol", "d_y0", "d_y1"]
+SEMAPHORES = (["qv", "qs", "qt", "qg", "loc", "d_l", "d_x", "d_u", "d_w", "d_v", "d_o", "d_ol", "d_y0", "d_y1"]
               + ["rq%d" % r for r in range(3)] + ["ra%d" % r for r in range(3)])
 
 
@@ -181,16 +178,14 @@ def rank_program(g, core, T, topo):
     def V(ref):
         return T[ref[0]][ref[1]]
 
-    def bank(k, n):
-        return T.ps[:, 512 * k:512 * k + n]
+    def bank(k, n, a=0):
+        return T.ps[:, 512 * k + a:512 * k + a + n]
 
-    def cp(q, out, in_, scale=None):
+    def cp(q, out, in_):
         if q == "v":
             op(q, lambda: g.vector.tensor_copy(V(out), V(in_)), [out], [in_])
-        elif scale is None:
-            op(q, lambda: g.scalar.activation(V(out), V(in_), COPY), [out], [in_])
         else:
-            op(q, lambda: g.scalar.activation(V(out), V(in_), COPY, scale=V(scale)), [out], [in_, scale])
+            op(q, lambda: g.scalar.activation(V(out), V(in_), COPY), [out], [in_])
 
     def frombank(q, out, k, n=C, scale=None):
         if q == "v" and scale is None:
@@ -208,8 +203,8 @@ def rank_program(g, core, T, topo):
         else:
             op(q, lambda: g.scalar.activation(V(out), V(win).indirect(V(off)), COPY), [out], [win, off])
 
-    def gather_add(out, win, off, in1):
-        op("v", lambda: g.vector.tensor_tensor(V(out), V(win).indirect(V(off)), V(in1), OP.add), [out], [win, off, in1])
+    def gather_tt(out, win, off, in1, o):
+        op("v", lambda: g.vector.tensor_tensor(V(out), V(win).indirect(V(off)), V(in1), o), [out], [win, off, in1])
 
     def tt(out, a, b, o):
         op("v", lambda: g.vector.tensor_tensor(V(out), V(a), V(b), o), [out], [a, b])
@@ -226,6 +221,9 @@ def rank_program(g, core, T, topo):
     def tr(out, in_):
         op("v", lambda: g.vector.transpose(V(out), V(in_)), [out], [in_])
 
+    def scan(out, keep, in_):
+        op("v", lambda: g.vector.tensor_tensor_scan(V(out), V(keep), V(in_), 0.0, OP.mult, OP.add), [out], [keep, in_])
+
     def ms(out, c):
         op("v", lambda: g.vector.memset(V(out), c), [out], [])
 
@@ -235,8 +233,11 @@ def rank_program(g, core, T, topo):
     def mm(k, lc, lp, rc, rp, n=C):
         op("t", lambda: g.tensor.matmul_mx(bank(k, n), V(lc), V(lp), V(rc), V(rp), True, True), [("ps", k)], [lc, lp, rc, rp])
 
-    def iota(out, pattern, base, cm, **kw):
-        op("g", lambda: g.iota(V(out), pattern, base, cm, **kw), [out], [])
+    def iota(out, pattern, base, cm):
+        if SCRATCH[out[0]][2] == I32:
+            op("g", lambda: g.iota(V(out), pattern, base, cm), [out], [])
+        else:
+            op("g", lambda: g.iota(V(out), pattern, base, cm, allow_small_or_imprecise_dtypes=True), [out], [])
 
     def quadrant(a):
         return slice(32 * a, 32 * a + 32)
@@ -262,365 +263,341 @@ def rank_program(g, core, T, topo):
         remote(r, T["lc%d" % r][:].bitcast(dt.uint8), T["qc%d" % r][:].bitcast(dt.uint8), "rq%d" % r, [R("qc%d" % r)])
         remote(r, T["lp%d" % r][:], T["qp%d" % r][:], "rq%d" % r, [R("qp%d" % r)])
 
+    def pause(fill, n=1):
+        for _ in range(n):
+            if fill:
+                fill.pop(0)()
+
     for r in range(3):
         n = len(ways(partner(r), core))
         arrives("rq%d" % r, 2 * n, [R("lc%d" % r), R("lp%d" % r)])
         arrives("ra%d" % r, n, [R("zl%d" % r)])
 
-    dmas("d_pg", [("y", T.pgi[:], T.pg[:], [R("pgi")], [])])
-    dmas("d_og", [("s", T.ogi[:], T.og[:], [R("ogi")], [])])
+    items = []
+    for q, src, a in (("y", T.pg, 0), ("s", T.og, 24)):
+        items.append((q, T.li[:, a:a + 24], src[:], [cols("li", a, 24)], []))
+        items.append((q, T.li[0:112, 48 + a:72 + a], src[16:128, :], [cols("li", 48 + a, 24)], []))
+        items.append((q, T.li[112:128, 48 + a:72 + a], src[0:16, :], [], []))
+    dmas("d_l", items)
     dmas("d_x", [("y", T.xb[:], T.x[:], [R("xb")], [])])
     dmas("d_u", [("s", T.ub[:], T.u[:], [R("ub")], [])])
-
-    def c1(k):
-        return cols("cst", k, 1)
-
-    def ti(k):
-        return cols("ti", k, 1)
-    iota(R("pidx"), [[0, 1]], 0, 1)
-    iota(R("wini"), [[NW, 16]], -8 * NW, 0)
-    ms(R("ones"), 1.0)
-    ms(cols("tab", 0, 1024), 0.0)
-    for k in (TW - 2048, TW - 1024):
-        cp("s", cols("tab", k, 1024), cols("tab", 0, 1024))
-    ms(cols("tab", 1024, TW - 3072), 0.0)
-    for b in range(4):
-        o = cols("ebt", 512 * b, 512)
-        op("g", lambda: g.affine_select(V(o), T.ones[:], [[-1, 512]], OP.is_equal, 0.0, b, 4), [o], [R("ones")])
-    ts(ti(0), R("pidx"), 4, 1, OP.arith_shift_right, OP.bitwise_and)
-    ts(ti(1), R("pidx"), 5, None, OP.arith_shift_right)
-    ms(R("pgf"), 0.0)
-    ts(c1(2), ti(0), 4.0, None, OP.mult)
-    ts(ti(2), R("pidx"), 15, None, OP.bitwise_and)
-    tt(c1(3), c1(2), ti(1), OP.add)
-    ms(R("ogf"), 0.0)
-    ts(c1(4), c1(3), float(NW), float(BASE), OP.mult, OP.add)
-
-    ts(cols("pgf", 0, 24), R("pgi"), c1(4), None, OP.add)
-    tr(R("pgt"), R("pgf"))
-    items = []
-    for G in range(6):
-        for h in range(2):
-            a, n = BASE + 4 * NW * h, 4 * NW
-            pr = slice(16 * G, 16 * G + 1)
-            items.append((("y", "s")[h], T.tab[pr, a:a + n], T.pgt[:, 16 * h:16 * h + 16],
-                          [R("tab", S_(a, a + n), p=pr)], [cols("pgt", 16 * h, 16)]))
-    dmas("d_t", items)
     dmas("d_w", [("y", T.wcod[:].bitcast(dt.uint8), T.wc[:], [R("wcod")], []), ("y", T.wpl[:], T.ws[:], [R("wpl")], [])])
     dmas("d_v", [("y", T.vb16[:], T.v[:], [R("vb16")], [])])
 
-    ts(R("t24"), R("ogi"), 1, None, OP.bitwise_and)
-    ts(R("t24b"), R("ogi"), 1, None, OP.arith_shift_right)
-    cp("v", c1(1), ti(0))
-    ts(c1(0), ti(0), -1.0, 1.0, OP.mult, OP.add)
-    ts(R("t24"), R("t24"), 4.0, None, OP.mult)
-    ms(R("one16"), 1.0)
-    ts(c1(7), ti(1), 128.0, None, OP.mult)
-    ts(c1(8), ti(0), 64.0, None, OP.mult)
-    tt(cols("ogf", 0, 24), R("t24"), R("t24b"), OP.add)
-    ts(ti(3), R("pidx"), 1, 3, OP.arith_shift_right, OP.bitwise_and)
-    cp("v", R("win"), R("wini"))
-    tt(c1(7), c1(7), c1(8), OP.add)
-    tr(R("ogt"), R("ogf"))
+    def ti(k):
+        return cols("ti", k, 1)
+
+    def cf(k):
+        return cols("cf", k, 1)
+
+    def c1(k):
+        return cols("cst", k, 1)
+    iota(R("pidx"), [[0, 1]], 0, 1)
+    iota(R("cq"), [[0, 4], [16, 3]], 0, 0)
+    iota(R("cg"), [[2, 4], [0, 3]], 8, 0)
+    iota(R("ca"), [[2, 12]], 0, 0)
+    iota(R("iw"), [[1, C]], 0, 0)
+    iota(cols("jb", 0, 3), [[32, 3]], 0, 1)
+    iota(R("im"), [[0, 24], [1, 16]], 0, 0)
+    iota(cols("ce", 0, 6), [[128, 3], [0, 2]], 0, 0)
+    iota(R("cb"), [[8, 3], [0, 4]], 0, 0)
+    iota(R("gcb"), [[0, 3], [C, 8], [0, 8]], 0, 0)
+    iota(R("gca"), [[0, 24], [C, 8]], 0, 0)
+    ms(R("ones"), 1.0)
+    ms(cols("rt", C, 16), 0.0)
+    for name, a, n in (("wk", 0, C), ("wk", C, C), ("wks", 0, 192)):
+        o, i = cols(name, a, n), cols("ones", 0, n)
+        op("s", lambda: g.scalar.activation(V(o), V(i), COPY, scale=0.0), [o], [i])
+    I, M7, HI, G, A = range(5)
+    ts(ti(I), R("pidx"), 15, None, OP.bitwise_and)
+    ts(ti(M7), R("pidx"), 7, None, OP.bitwise_and)
+    ts(ti(HI), R("pidx"), 3, 1, OP.arith_shift_right, OP.bitwise_and)
+    ts(ti(G), R("pidx"), 4, None, OP.arith_shift_right)
+    ts(ti(A), R("pidx"), 5, None, OP.arith_shift_right)
+    cp("v", cols("cf", 0, 5), cols("ti", 0, 5))
+    tt(ti(5), R("pidx"), ti(G), OP.subtract)
+    ts(R("e"), R("cq"), cf(I), 24.0, OP.add, OP.is_ge)
+    ts(R("qq"), R("cq"), cf(I), None, OP.add)
+    ts(ti(6), ti(5), 7, None, OP.bitwise_and)
+    tt(R("t1"), R("e"), R("cg"), OP.add)
+    ts(R("e"), R("e"), -24.0, None, OP.mult)
+    ts(c1(0), ti(6), 48.0, 24.0, OP.mult, OP.add)
+    ts(cols("t12", 0, 12), R("t1"), cf(G), None, OP.subtract)
+    tt(R("qq"), R("qq"), R("e"), OP.add)
+    ts(c1(0), cf(A), 4.0, c1(0), OP.mult, OP.add)
+    ts(cols("t12", 0, 12), cols("t12", 0, 12), 7, None, OP.bitwise_and)
+    cp("v", cols("rt", 0, 96), R("li"))
+    ts(c1(0), cf(HI), 2.0, c1(0), OP.mult, OP.add)
+    ts(R("t1"), cols("t12", 0, 12), 48.0, None, OP.mult)
+
+    for a in range(4):
+        cp("vs"[a % 2], R("rt", S_(96, 192), p=quadrant(a)), R("rt", S_(0, 96), p=quadrant((a + 1) % 4)))
+    tt(R("t1"), R("t1"), R("qq"), OP.add)
+    ts(R("lo"), R("ca", S_(0, 4, 2)), c1(0), cf(G), OP.add, OP.add)
     for h in range(2):
-        ts(R("mk8", S_(h, 32, 2)), R("one16"), c1(h), 8.0, OP.mult, OP.mult)
-    tt(c1(7), c1(7), ti(2), OP.add)
-    ms(cols("win", 0, 1), 0.0)
+        cp("vs"[h], R("rt", S_(192, 384), p=S_(64 * h, 64 * h + 64)), R("rt", S_(0, 192), p=S_(64 - 64 * h, 128 - 64 * h)))
+    cp("v", R("lp_"), R("t1"))
+    ts(c1(4), cf(A), 64.0, None, OP.mult)
+    gather("v", cols("pl", 0, 96), R("rt"), cols("lp_", 0, 6))
+    gather("v", cols("pl", 96, 96), R("rt"), cols("lp_", 6, 6))
+    gather("s", cols("tab", 0, 16 * 96), R("iw"), cols("pl", 0, 96))
+    gather("s", cols("tab", 16 * 96, 16 * (SHARE - 96)), R("iw"), cols("pl", 96, SHARE - 96))
+    op("v", lambda: g.vector.tensor_scalar(T.lab[:], T.rt[:].indirect(T.lo[:]), float(C), None, OP.mult), [R("lab")], [R("rt"), R("lo")])
+    ts(cols("jb", 0, 3), cols("jb", 0, 3), c1(4), None, OP.add)
+    ms(R("z32"), 1.0)
 
-    def spread(src, xd, xw, nsrc):
-        for H in range(2):
-            for h in range(2):
-                cp("vs"[H], cols(xd, 32 * h + 16 * H, 16), cols(src, 16 * h, 16))
-        k = 0
-        for a in range(nsrc):
-            for b in range(4):
-                cp("vs"[k % 2], R(xw, S_(64 * a, 64 * a + 64), p=quadrant(b)), R(xd, p=quadrant(a)))
-                k += 1
+    def unit_tile(b):
+        o = cols("ebt", 512 * b, 512)
+        op("g", lambda: g.affine_select(V(o), T.ones[:], [[-1, 512]], OP.is_equal, 0.0, b, 4), [o], [R("ones")])
+    for b in range(3):
+        unit_tile(b)
 
-    spread("ogt", "oxd", "oxw", 4)
-    for s in range(4):
-        ts(cols("js", s, 1), c1(7), 16.0 * s + BASE, None, OP.add)
-    cp("v", cols("idxf", 56, 8), cols("mk8", 0, 8))
-    for h in range(2):
-        ts(R("jbm", S_(h, 8, 2)), R("js"), c1(h), None, OP.mult)
-    ts(ti(4), R("pidx"), 3, 1, OP.arith_shift_right, OP.bitwise_and)
-    ts(c1(9), ti(3), 32.0, None, OP.mult)
-    ts(c1(10), ti(4), 16.0, None, OP.mult)
-    tr(R("ox"), R("oxw"))
-    tt(c1(9), c1(9), c1(10), OP.add)
-    ts(R("selu"), cols("one16", 0, 10), c1(9), None, OP.mult)
-    for par, name in ((0, "oe"), (1, "oo")):
-        for a in range(4):
-            for h in range(2):
-                o = R(name, S_(h, 32, 2), p=quadrant(a))
-                i = R("ox", ANY, par, S_(8 * a + 4 * h, 8 * a + 4 * h + 4), p=quadrant(a))
-                s = R("cst", S_(h, h + 1), p=quadrant(a))
-                if par:
-                    cp("s", o, i, s)
-                else:
-                    ts(o, i, s, None, OP.mult)
-    oe, oo, mk8 = R("oe"), R("oo"), R("mk8")
-    IE, IO = cols("idxf", 0, 32), cols("idxf", 32, 24)
-    tt(R("dd"), oo, oe, OP.subtract)
-    tt(IO, cols("oe", 8, 24), cols("oo", 0, 24), OP.subtract)
-    tt(IE, R("dd"), mk8, OP.add)
-    tt(IO, IO, cols("mk8", 0, 24), OP.add)
-    cp("v", R("idxu"), R("idxf"))
-    ts(R("off0"), cols("oe", 0, 8), float(NW), None, OP.mult)
-    tt(R("off0"), R("off0"), R("jbm"), OP.add)
-    cp("v", cols("offu", 0, 8), R("off0"))
+    def OF(k):
+        return R("of", S_(96 * k + 31, 96 * k + 96, 32))
 
-    KAP = [0, 4, 1, 5, 2, 6, 3, 7]
+    def U(k):
+        return cols("offu", 4 * k, 3)
 
-    def rep(k):
-        gather("s", cols("rep", 128 * KAP[k], 128), R("win"), cols("idxu", 8 * KAP[k], 8))
+    def lay_labels():
+        for s in range(3):
+            cp("v", cols("wk", 256 * s, 8), cols("lab", 8 * s, 8))
+
+    lay_labels()
+    ms(R("z32", S_(0, 96, 32)), 0.0)
+    tt(OF(0), R("lab", S_(0, 24, 8)), cols("jb", 0, 3), OP.add)
+    ts(R("dm"), R("im"), cf(I), None, OP.is_equal)
+    cp("v", U(0), OF(0))
+    gather("v", cols("tab", 16 * SHARE, 16 * (192 - SHARE)), R("iw"), cols("pl", SHARE, 192 - SHARE))
+    dm = cols("dm", 0, 48)
+
+    def clean(q, k):
+        gather(q, cols("wa", 48 * k, 48), R("tab"), U(k))
 
     def walk(first, fill):
-        for k in range(first, 8):
-            z = KAP[k]
-            blk, off = (128 * z, 128), cols("offu", 8 * z, 8)
-            if k < 7:
-                gather_add(cols("wk", *blk), R("tab"), off, cols("rep", *blk))
-                pause(fill)
-            else:
-                gather("v", cols("wk", *blk), R("tab"), off)
-                early_addresses(2)
-            tr(cols("tt", *blk), cols("wk", *blk))
-            if k < 6:
-                pause(fill)
-            elif k == 6:
-                early_addresses(0)
-            if k < 7:
-                cp("v", cols("offu", 8 * KAP[k + 1], 8), R("tt", S_(128 * z, 128 * z + 128, 16)))
-                if k == 6:
-                    early_addresses(1)
-                else:
-                    pause(fill)
+        for k in range(first, 7):
+            gather_tt(R("wk", S_(k + 9, 768, 16)), R("tab"), U(k), dm, OP.mult)
+            clean("s", k)
+            pause(fill)
+            scan(cols("of", 96 * (k + 1), 96), R("z32"), R("wk", S_(k + 1, 768, 8)))
+            pause(fill)
+            cp("v", U(k + 1), OF(k + 1))
+            pause(fill)
+        clean("v", 7)
 
-    def pause(fill):
-        if fill:
-            fill.pop(0)()
+    def places():
+        return [lambda s=s: gather_tt(cols("eq", 64 * s, 64), R("lab"), cols("lb", 4 * s, 4), cols("gcb", 0, 64), OP.is_equal) for s in range(3)] + [
+            lambda: scan(R("iv"), R("wgt"), R("eq")),
+            lambda: [ts(cols("pos", 8 * s, 8), R("iv", S_(64 * s + 7, 64 * s + 64, 8)), -1.0, cols("ci", s, 1), OP.mult, OP.add) for s in range(3)],
+            place_offsets]
 
-    def differences():
-        return [lambda: tt(R("dv"), R("idxf", S_(0, 64, 2)), R("idxf", S_(1, 64, 2)), OP.add),
-                lambda: ts(R("dv"), R("dv"), -float(NW), 8.0 * NW, OP.mult, OP.add)]
+    def place_offsets():
+        ts(R("inv"), R("pos"), 48.0, C + 0.25, OP.mult, OP.add)
 
-    def early_addresses(step):
-        if step == 0:
-            tt(cols("vs", 0, 28), R("tt", S_(0, 896, 32)), R("tt", S_(16, 896, 32)), OP.add)
-        elif step == 1:
-            tt(cols("vs", 0, 28), cols("vs", 0, 28), cols("dv", 0, 28), OP.add)
-        else:
-            for s in range(4):
-                cp("v", R("vadr", S_(8 * s, 8 * s + 7)), R("vs", S_(s, 28, 4)))
+    def by_group(fill):
+        gather("v", cols("wo", 0, 192), R("wa"), cols("inv", 0, 12))
+        gather("s", cols("wo", 192, 192), R("wa"), cols("inv", 12, 12))
+        pause(fill)
+        tr(R("wt"), R("wo"))
+        pause(fill)
 
-    def last_address():
-        tt(R("vadr", S_(7, 32, 8)), R("tt", S_(896, 1024, 32)), R("tt", S_(912, 1024, 32)), OP.add)
+    def score_offsets():
+        cp("v", R("eb"), R("wt", ANY, ANY, 0))
 
-    def list_of_addresses():
-        ts(cols("eb", 0, 28), cols("vs", 0, 28), -float(BASE), None, OP.add)
-        ts(cols("eb", 28, 4), R("vadr", S_(7, 32, 8)), -float(BASE), None, OP.add)
+    def signs(k):
+        return [lambda: gather_tt(cols("oh", 0, 96), R("lab"), cols("la", 6 * k, 6), cols("gca", 0, 96), OP.is_equal),
+                lambda: gather_tt(cols("oh", 96, 96), R("lab"), cols("la", 6 * k + 6, 6), cols("gca", 0, 96), OP.is_equal),
+                lambda: tt(R("sg"), cols("oh", 0, 96), cols("oh", 96, 96), OP.subtract)]
 
-    def tt8(k):
-        return R("tt", S_(128 * KAP[k], 128 * KAP[k] + 128, 16))
+    def ahead(k):
+        n = 12 - k
+        calls = [lambda: tt(cols("df", 0, n), R("lab", S_(k + 1, 24, 2)), R("lab", S_(k, k + 2 * n, 2)), OP.subtract),
+                 lambda: [cp("v", R("wks", S_(t, 192, 64)), R("lab", S_(k + 2 * t, 24, 8))) for t in range(2)],
+                 lambda: (tt(cols("a0", 0, 3), OF(k), R("df", S_(0, n, 4)), OP.add), cp("v", R("co", S_(1, 12, 4)), R("df", S_(1, n, 4)))),
+                 lambda: cp("v", cols("offs", 0, 3), cols("a0", 0, 3))]
+        for t in range(2):
+            calls.append(lambda t=t: gather_tt(R("wks", S_(t + 2, 192, 4)), R("tab"), cols("offs", 4 * t, 3), dm, OP.mult))
+            calls.append(lambda t=t: scan(cols("ofs", 96 * t, 96), R("z32"), R("wks", S_(t, 192, 2))))
+            if t == 0:
+                calls.append(lambda: (cp("v", cols("offs", 4, 3), R("ofs", S_(31, 96, 32))),
+                                      tt(cols("yy", 0, 3), R("ofs", S_(31, 96, 32)), OF(k + 1), OP.subtract)))
+        calls.append(lambda: tt(R("co", S_(0, 12, 4)), R("ofs", S_(127, 192, 32)), OF(k + 2), OP.subtract))
+        return calls
 
-    def ahead(k, even):
-        w = 32 if even else 24
-        src = IE if even else IO
-        s0, s1 = R("tts", S_(0, 128, 16)), R("tts", S_(128, 256, 16))
-        nxt = cols("idxf", 8 * KAP[k + 1], 8)
-        return [
-            lambda: tt(cols("dd", 0, w), src, cols("mk8", 0, w), OP.subtract),
-            lambda: (ts(R("d0"), cols("dd", 0, 8), float(NW), None, OP.mult), tt(R("idxs"), cols("mk8", 0, 8), cols("dd", 0, 8), OP.subtract)),
-            lambda: (tt(R("offsf"), R("off0") if even else tt8(0), R("d0"), OP.add), cp("v", R("idxsu"), R("idxs"))),
-            lambda: (cp("v", cols("offs", 0, 8), R("offsf")), gather("s", R("reps"), R("win"), R("idxsu"))),
-            lambda: gather_add(cols("wks", 0, 128), R("tab"), cols("offs", 0, 8), R("reps")),
-            lambda: tr(cols("tts", 0, 128), cols("wks", 0, 128)),
-            lambda: cp("v", cols("offs", 8, 8), s0),
-            lambda: gather("v", cols("wks", 128, 128), R("tab"), cols("offs", 8, 8)),
-            lambda: tr(cols("tts", 128, 128), cols("wks", 128, 128)),
-            lambda: (tt(R("yk"), nxt, cols("mk8", 0, 8), OP.subtract), tt(R("yt"), s1, tt8(k + 1), OP.subtract),
-                     ts(cols("dd2", 0, w), cols("dd", 0, w), -2.0, None, OP.mult)),
-            lambda: (tt(R("yk"), R("yk"), cols("dd", 0, 8), OP.add), tt(R("y0"), s0, tt8(k), OP.subtract)),
-            lambda: (ts(R("yk"), R("yk"), float(NW), None, OP.mult), ts(R("t3"), cols("dd", 8, 8), float(NW), None, OP.mult)),
-            lambda: tt(R("y1"), R("yt"), R("yk"), OP.add),
-        ]
-
-    def select(k):
-        tr(R("xx" + k), R("xw" + k))
-        ts(R("cl" + k), R("xx" + k), c1(4), c1(5), OP.max, OP.min)
-
-    def totals(k):
-        op("v", lambda: g.vector.tensor_tensor_scan(V(R("sc" + k)), V(R("zm")), V(R("cl" + k)), 0.0, OP.mult, OP.add),
-           [R("sc" + k)], [R("zm"), R("cl" + k)])
-
-    def scores(r, x, a, n, q, k):
-        mm(k, cols("uc", 2 * x, 128), cols("upl", 2 * x, 128), *q_of(r, a, n), n)
-        frombank(q, cols("sct", NW * x + a, n), k, n)
+    def scores(r, a, n, q, k):
+        mm(k, R("uc"), R("upl"), *q_of(r, a, n), n)
+        frombank(q, cols("sct", a, n), k, n)
 
     def unpack(c, p, banks):
         for b in range(4):
-            mm(banks + b, cols("ec", 128 * b, 128), cols("ep", 128 * b, 128), R(c), R(p))
+            mm(banks[b], cols("ec", 128 * b, 128), cols("ep", 128 * b, 128), R(c), R(p))
 
-    for k in range(7):
-        rep(k)
+    def scoring_columns():
+        op("v", lambda: g.vector.tensor_copy(T.uc[:].bitcast(dt.uint32), T.uq0[:].bitcast(dt.uint32).indirect(T.lu[:])),
+           [R("uc")], [R("uq0"), R("lu")])
+        op("s", lambda: g.scalar.activation(T.upl[:], T.up0[:].indirect(T.lu[:]), COPY), [R("upl")], [R("up0"), R("lu")])
+
+    def weights(t):
+        for u in (t, t + 1):
+            ms(R("wgt", S_(u, 192, 8)), (9.0 - u) / (8.0 - u) if u else 0.0)
 
     def first_state():
         quant(*q_of(0), R("xb"))
         send_state(0)
-        for x in range(8):
-            iota(cols("sct", NW * x + C, NW - C), [[0, NW - C]], 0, 0, allow_small_or_imprecise_dtypes=True)
+        unit_tile(3)
 
-    def scoring_columns():
-        op("v", lambda: g.vector.tensor_copy(T.uc[:].bitcast(dt.uint32), T.uq0[:].bitcast(dt.uint32).indirect(T.selu[:])),
-           [R("uc")], [R("uq0"), R("selu")])
-        op("s", lambda: g.scalar.activation(T.upl[:], T.up0[:].indirect(T.selu[:]), COPY), [R("upl")], [R("up0"), R("selu")])
-    aim = ahead(0, True)
-    fill = aim[:4] + [lambda: quant(R("uq0"), R("up0"), R("ub")), first_state, scoring_columns] + differences() + aim[4:] + [
-        lambda: ms(R("zm"), 1.0),
-        lambda: ms(R("zm", S_(0, 192, 8)), 0.0),
-        lambda: ts(c1(5), c1(4), float(NW), None, OP.add),
-        lambda: ts(c1(6), c1(3), 7.0 * NW, 7.0 * NW + 8 * BASE, OP.mult, OP.add)]
+    def pair_lists():
+        ts(cols("la", 0, 6), cols("ca", 0, 6), cf(HI), 2.0, OP.add, OP.mult)
+        ts(cols("la", 6, 6), cols("la", 0, 6), 1.0, None, OP.add)
+        ts(R("la", S_(12, 18, 2)), R("la", S_(0, 6, 2)), 2.0, None, OP.add)
+        ts(R("la", S_(13, 18, 2)), R("la", S_(7, 12, 2)), cf(HI), 1.0, OP.subtract, OP.add)
+    aim, at, sg = ahead(0), places(), signs(0)
+    fill = [lambda: (ts(c1(2), cf(M7), 16.0, None, OP.mult), ts(R("lb"), R("cb"), cf(M7), None, OP.add)),
+            lambda: quant(R("uq0"), R("up0"), R("ub")),
+            lambda: (ts(R("lu"), cols("ca", 0, 8), 0.0, c1(2), OP.mult, OP.add), weights(0)),
+            first_state, at[0], scoring_columns, at[1],
+            lambda: (scores(0, 0, C, "s", 4), weights(2)), at[2],
+            lambda: (weights(4), weights(6)), pair_lists, at[3],
+            lambda: (ts(cols("ci", 0, 3), cols("cq", 0, 3), cf(I), 1.0 / 48, OP.add, OP.mult), aim[0](), aim[1]()),
+            lambda: (at[4](), aim[2]()), lambda: (aim[3](), ts(c1(1), cf(M7), 17.0, None, OP.mult)), lambda: (aim[4](), at[5]()),
+            lambda: (aim[5](), ts(R("le"), cols("ce", 0, 6), c1(1), None, OP.add)), sg[0], aim[6], aim[7], sg[1],
+            lambda: (aim[8](), ms(cols("z8", 0, 96), 1.0)), lambda: (sg[2](), ms(R("z8", S_(0, 96, 8)), 0.0)),
+            lambda: (aim[9](), ms(cols("mv", 96, 16), 0.0), ms(R("co", S_(2, 12, 4)), 0.0), ms(R("co", S_(3, 12, 4)), 0.0), ts(R("ld"), cols("ca", 0, 6), cf(HI), None, OP.add))]
     walk(0, fill)
-    for x in range(8):
-        scores(0, x, 0, C, "s", x)
-    last_address()
-    list_of_addresses()
+    by_group(fill)
+    score_offsets()
 
     for r in range(3):
-        odd = r == 1
-        for k in range(2):
-            gather("vs"[k], cols("ev", 256 * k, 256), R("sct"), cols("eb", 16 * k, 16))
-        while fill:
-            pause(fill)
+        k = r % 2
+        n = 12 - k
+        gather("v", cols("ef", 0, 192), R("sct"), cols("eb", 0, 12))
+        gather("s", cols("ef", 192, 192), R("sct"), cols("eb", 12, 12))
+        pause(fill, 99)
+        tr(R("et"), R("ef"))
         if r == 0:
-            quant(R("ec"), R("ep"), R("ebt"))
-        unpack("qc%d" % r, "qp%d" % r, 0)
-        for b in range(3):
-            frombank("s", cols("fb", C * b, C), b)
-        n = 12 if odd else 16
-        if odd:
-            tt(cols("bt", 0, 192), cols("ev", 256, 192), cols("ev", 64, 192), OP.is_gt)
-        else:
-            tt(R("bt"), cols("ev", 0, 256), cols("ev", 256, 256), OP.is_gt)
-        for h in range(2):
-            ts(R("bd", S_(0, n), h, ANY), cols("bt", 0, 16 * n), c1(h), None, OP.mult)
-        tr(cols("btt", 0, 32 * n), R("bd", S_(0, n), ANY, ANY))
-        bm, bm0, bm1 = R("btt", S_(0, 32 * n, 16)), R("btt", S_(0, 128, 16)), R("btt", S_(128, 256, 16))
-        m, m2 = cols("mm", 0, 2 * n), cols("mm2", 0, 2 * n)
-        mine = IO if odd else IE
-        first = 1 if odd else 0
-        t0, t1, t2 = tt8(0), tt8(first), tt8(first + 1)
-        tt(m2, bm, cols("dd2", 0, 2 * n), OP.mult)
-        tt(R("t1"), bm0, R("y1"), OP.mult)
-        tt(R("t2"), bm1, R("t3"), OP.mult)
-        tt(mine, mine, m2, OP.add)
-        tt(t2, t2, R("t1"), OP.add)
-        tt(m, bm, cols("dd", 0, 2 * n), OP.mult)
-        if odd:
-            cp("v", cols("idxu", 32, 24), IO)
-        else:
-            cp("v", cols("idxu", 0, 32), IE)
-        tt(t2, t2, R("t2"), OP.add)
-        rep(first + 2)
-        a, k = (0, 32) if odd else (32, 24)
-        if odd:
-            tt(cols("idxf", 0, 24), cols("idxf", 0, 24), m, OP.add)
-        else:
-            tt(IO, IO, cols("mm", 8, 24), OP.add)
-        cp("v", cols("offu", 8 * KAP[first + 2], 8), t2)
-        if odd:
-            tt(cols("idxf", 8, 24), cols("idxf", 8, 24), m, OP.add)
-        else:
-            tt(IO, IO, cols("mm", 0, 24), OP.add)
-        tt(R("m0"), bm0, R("d0"), OP.mult)
-        cp("v", cols("idxu", a, k), cols("idxf", a, k))
-        for k in range(first + 3, 7):
-            rep(k)
-        up, dn = (OP.subtract, OP.add) if odd else (OP.add, OP.subtract)
-        E, O = (cols("oe", 8, 24), cols("oo", 0, 24)) if odd else (oe, oo)
-        f0 = t0 if odd else R("off0")
-        diff = differences()
-        fill = [lambda: (tt(R("y0"), bm0, R("y0"), OP.mult), tt(f0, f0, R("m0"), OP.add)), lambda: (tt(t1, t1, R("y0"), OP.add), diff[0]())]
-        fill += ahead(0 if odd else 1, odd) if r < 2 else []
-        orders = lambda: (tt(O, O, m, dn), tt(E, E, m, up))
-        fill.insert(3, lambda: (diff[1](), orders()))
+            quant(cols("ec", 0, 128), cols("ep", 0, 128), cols("ebt", 0, 512))
+        gather_tt(R("sel"), R("et"), R("le"), R("sg"), OP.mult)
         if r == 0:
-            fill.append(lambda: quant(R("vq"), R("vp"), R("vb16")))
-        walk(first + 2, fill)
-        last_address()
-        tr(R("ltA"), R("vadr"))
-        list_of_addresses()
-        spread("ltA", "xdA", "xwA", 3)
-        gather("s", R("brep"), cols("tab", BASE, TW - BASE), R("eb"))
-        select("A")
-        totals("A")
-        ts(R("al%d" % r), R("scA", S_(7, 192, 8)), c1(6), None, OP.subtract)
+            quant(cols("ec", 128, 128), cols("ep", 128, 128), cols("ebt", 512, 512))
+        scan(R("es"), cols("z8", 0, 96), R("sel"))
+        if r == 0:
+            quant(cols("ec", 256, 128), cols("ep", 256, 128), cols("ebt", 1024, 512))
+        ts(R("d"), R("es", S_(7, 96, 8)), 0.0, None, OP.is_gt)
+        if r == 0:
+            quant(cols("ec", 384, 128), cols("ep", 384, 128), cols("ebt", 1536, 512))
+        m = cols("m", 0, n)
+        tt(R("pr"), R("d"), R("co"), OP.mult)
+        tt(m, cols("d", 0, n), cols("df", 0, n), OP.mult)
+        for s in range(3):
+            ts(cols("offu", 4 * (k + 2) + s, 1), cols("pr", 4 * s, 1), cols("pr", 4 * s + 1, 1), cols("of", 96 * (k + 2) + 32 * s + 31, 1), OP.add, OP.add)
+        tt(R("lab", S_(k + 1, 24, 2)), R("lab", S_(k + 1, 24, 2)), m, OP.subtract)
+        tt(R("lab", S_(k, k + 2 * n, 2)), R("lab", S_(k, k + 2 * n, 2)), m, OP.add)
+
+        def own_numbers():
+            unpack("qc%d" % r, "qp%d" % r, (0, 1, 6, 7))
+            for b in range(2):
+                frombank("s", cols("fb", C * b, C), b)
+            unpack("lc%d" % r, "lp%d" % r, (2, 3, 0, 1))
+        fill = [lambda: (lay_labels(), own_numbers()),
+                lambda: (tt(cols("s1", 0, 3), R("d", S_(0, n, 4)), cols("yy", 0, 3), OP.mult), tt(OF(k), OF(k), R("m", S_(0, n, 4)), OP.add)),
+                lambda: gather_tt(cols("mv", 0, 96), R("d"), R("ld"), R("sg"), OP.mult),
+                lambda: (tt(OF(k + 1), OF(k + 1), cols("s1", 0, 3), OP.add), cp("v", U(k), OF(k))),
+                lambda: tt(R("h1"), cols("mv", 0, 96), cols("mv", 16, 96), OP.add),
+                lambda: (cp("v", U(k + 1), OF(k + 1)), clean("s", k), clean("s", k + 1), tt(R("h2"), R("h1", ANY, S_(0, 8)), R("h1", ANY, S_(8, 16)), OP.add))]
+        if r < 2:
+            aim = ahead(1 - k)
+            fill += [lambda: (cp("v", OF(k + 2), U(k + 2)), aim[0]()), lambda: (tt(R("pos"), R("pos"), R("h2"), OP.add), aim[1]()),
+                     aim[2], lambda: (place_offsets(), aim[3]())] + aim[4:]
+        else:
+            fill += [lambda: (tt(R("pos"), R("pos"), R("h2"), OP.add), ms(cols("olf", 24, 8), 0.0)),
+                     lambda: [ts(R("olf", S_(s, 24, 3)), cols("lab", 8 * s, 8), 1.0 / C, None, OP.mult) for s in range(2)],
+                     lambda: (place_offsets(), ts(R("olf", S_(2, 24, 3)), cols("lab", 16, 8), 1.0 / C, None, OP.mult)), lambda: None,
+                     lambda: tr(R("olt"), R("olf")),
+                     lambda: dmas("d_ol", [("y", T.ol[:, 96 * a:96 * a + 96], T.olt[32 * a:32 * a + 24, :], [], [R("olt")]) for a in range(4)])]
+        if r == 0:
+            fill += [lambda: (ts(c1(3), cf(G), float(C), None, OP.mult), ms(R("z16"), 1.0))]
+        walk(k + 2, fill)
+        by_group(fill)
+        for a in range(4):
+            for c in range(4):
+                cp("vs"[c % 2], R("lf", S_(6 * a, 6 * a + 6), p=quadrant(c)), R("wt", ANY, S_(2 * c, 2 * c + 2), 0, p=quadrant(a)))
+        pause(fill)
+        cp("v", R("al%d" % r), R("lf"))
         remote(r, T["zl%d" % r][:], T["al%d" % r][:], "ra%d" % r, [R("al%d" % r)])
-        unpack("lc%d" % r, "lp%d" % r, 4)
-        for b in range(2):
-            frombank("s", cols("dp", C * b, C), 4 + b)
-        tr(R("brt"), R("brep"))
-        for k in range(4):
-            cp("v", cols("lb", 8 * k, 8), R("brt", S_(16 * k, 512, 64)))
-        tr(R("ltB"), R("lb"))
-        spread("ltB", "xdB", "xwB", 3)
-        for b in range(2, 4):
-            frombank("s", cols("dp", C * b, C), 4 + b)
-        select("B")
-        if r == 2:
-            tt(cols("olf", 0, 16), R("oe", S_(0, 32, 2)), R("oe", S_(1, 32, 2)), OP.add)
-            tt(cols("olf", 16, 16), R("oo", S_(0, 32, 2)), R("oo", S_(1, 32, 2)), OP.add)
-            ts(R("olg"), R("olf"), 4.0, -7.0, OP.is_ge, OP.mult)
-            tt(R("olf"), R("olf"), R("olf"), OP.add)
-            tt(R("olf"), R("olf"), R("olg"), OP.add)
-            tr(R("olt"), R("olf"))
-            items = []
-            for a in range(3):
-                for par in range(2):
-                    for h in range(2):
-                        p = slice(32 * a + 16 * par, 32 * a + 16 * par + 16)
-                        c = 128 * a + 64 * h
-                        items.append(("y", T.ol[par:8:2, c:c + 64], T.olt[p, 16 * h:16 * h + 16], [], [R("olt", S_(16 * h, 16 * h + 16), p=p)]))
-            dmas("d_ol", items)
-        zt, zc, zp = "zt%d" % r, "zc%d" % r, "zp%d" % r
-        for h in range(2):
-            for b in (0, 2, 1, 3):
-                gather("vs"[b // 2], R(zt, S_(4 * HC * h + b, 4 * HC * (h + 1), 4)), cols("dp", C * b, C), cols("zl%d" % r, 12 * h, 12))
-        totals("B")
-        for h in range(2):
-            quant(cols(zc, HC * h, HC), cols(zp, HC * h, HC), cols(zt, 4 * HC * h, 4 * HC))
-        for k in range(4):
-            for l in range(2):
-                ts(R("bl", S_(4 * (k & 1) + (k & 2) + l, 24, 8)), R("scB", S_(32 * l + 8 * k + 7, 192, 64)), c1(6), None, OP.subtract)
-        for h in range(2):
-            mm(h, cols("wcod", 0, 128), cols("wpl", 0, 128), cols(zc, HC * h, HC), cols(zp, HC * h, HC), HC)
-            frombank("sv"[h], cols("rs", HC * h, HC), h, HC, 0.03125)
+        for b in range(4):
+            frombank("s", cols("dp", C * b, C), (2, 3, 0, 1)[b])
+        pause(fill, 99)
+        ts(R("ab"), R("lf"), c1(3), None, OP.add)
+        fill = signs(1 - k) + [score_offsets] if r < 2 else []
+        if r == 0:
+            ms(R("z16", S_(0, C, 16)), 0.0)
+            fill.append(lambda: quant(R("vq"), R("vp"), R("vb16")))
+        pause(fill)
+        gather_tt(R("bg"), R("tab"), R("ab"), R("dm"), OP.mult)
+        pause(fill)
+        scan(R("bs"), R("z16"), R("bg"))
+        pause(fill)
+        cp("v", R("bl"), R("bs", S_(15, C, 16)))
+        pause(fill, 99)
+        zt, zc, zp, zl = "zt%d" % r, "zc%d" % r, "zp%d" % r, "zl%d" % r
+
+        def mosaic(h, b):
+            a, w = ZP[h]
+            gather("vs"[b // 2], R(zt, S_(4 * a + b, 4 * (a + w), 4)), cols("dp", C * b, C), cols(zl, a // 16, w // 16))
+
+        def layer(h, b, k):
+            a, w = ZP[h]
+            mm(k, cols("wcod", 128 * b, 128), cols("wpl", 128 * b, 128), cols(zc, a, w), cols(zp, a, w), w)
+
+        def products(q, h, b, k):
+            a, w = ZP[h]
+            frombank(q, cols("rs", C * b + a, w), k, w, 0.03125)
+
+        def quant_z(h):
+            a, w = ZP[h]
+            quant(cols(zc, a, w), cols(zp, a, w), cols(zt, 4 * a, 4 * w))
+        for h, b in ((0, 0), (0, 2), (0, 1), (0, 3), (1, 0), (1, 2), (1, 3)):
+            mosaic(h, b)
+        quant_z(0)
+        for b, kb in ((2, 0), (3, 1), (0, 2), (1, 3)):
+            layer(0, b, kb)
+            products("s", 0, b, kb)
+        mosaic(1, 1)
+        quant_z(1)
         nx = "xs%d" % (r + 1)
-        for b, k in ((1, 2), (3, 5), (2, 4)):
-            mm(k, cols("wcod", 128 * b, 128), cols("wpl", 128 * b, 128), R(zc), R(zp))
-            frombank("s", cols("rs", C * b, C), k, C, 0.03125)
-        for h in range(2):
-            gather("s", cols("gs", HC * h, HC), cols("rs", 3 * C, C), cols("bl", 12 * h, 12))
-        for h in range(2):
-            for b in range(3):
-                gather_add(R(nx, S_(4 * HC * h + b, 4 * HC * (h + 1), 4)), cols("rs", C * b, C), cols("bl", 12 * h, 12), cols("fb", C * b + HC * h, HC))
-            o, i = R(nx, S_(4 * HC * h + 3, 4 * HC * (h + 1), 4)), cols("gs", HC * h, HC)
-            op("v", lambda: g.vector.tensor_tensor(V(o), V(i), T.ps[:, 512 * 3 + HC * h:512 * 3 + HC * h + HC], OP.add), [o], [i, ("ps", 3)])
-            quant(*q_of(r + 1, HC * h, HC), cols(nx, 4 * HC * h, 4 * HC))
-            if r < 2:
-                for x in range(8):
-                    if h == 0:
-                        scores(r + 1, x, 0, HC, "s", (0, 1, 2, 6, 7, 5, 4, 0)[x])
-                    else:
-                        scores(r + 1, x, HC, HC, "sv"[x % 2], x)
-                        pause(fill)
+
+        def place(h, b):
+            a, w = XP[h]
+            return R(nx, S_(4 * a + b, 4 * (a + w), 4))
+
+        def pick(h, b):
+            a, w = XP[h]
+            if b < 2:
+                gather_tt(place(h, b), cols("rs", C * b, C), cols("bl", a // 16, w // 16), cols("fb", C * b + a, w), OP.add)
             else:
-                mm(h, R("vq"), R("vp"), *q_of(3, HC * h, HC), HC)
-                frombank("sv"[h], cols("ys", HC * h, HC), h, HC)
-                dmas("d_y%d" % h, [("y", T.y[:, HC * h:HC * h + HC], T.ys[:, HC * h:HC * h + HC], [], [cols("ys", HC * h, HC)])])
-        while fill:
-            pause(fill)
+                gather("s", cols("gs", C * (b - 2) + a, w), cols("rs", C * b, C), cols("bl", a // 16, w // 16))
+
+        def add(h, b):
+            a, w = XP[h]
+            o, i = place(h, b), cols("gs", C * (b - 2) + a, w)
+            op("v", lambda: g.vector.tensor_tensor(V(o), V(i), bank(4 + b, w, a), OP.add), [o], [i, ("ps", 4 + b)])
+        for b, kb in ((0, 4), (2, 5), (1, 0), (3, 1)):
+            layer(1, b, kb)
+            products("vs"[b // 2], 1, b, kb)
+        for h in range(2):
+            for b in range(4):
+                pick(h, b)
+        for h in range(2):
+            add(h, 2)
+            add(h, 3)
+        for h in range(2):
+            a, w = XP[h]
+            quant(*q_of(r + 1, a, w), cols(nx, 4 * a, 4 * w))
+            if r < 2:
+                scores(r + 1, a, w, "sv"[h], 4 + h)
+            else:
+                mm(4 + h, R("vq"), R("vp"), *q_of(3, a, w), w)
+                frombank("sv"[h], cols("ys", a, w), 4 + h, w)
+                dmas("d_y%d" % h, [("y", T.y[:, a:a + w], T.ys[:, a:a + w], [], [cols("ys", a, w)])])
         if r < 2:
             send_state(r + 1)
 

@@ -4,14 +4,19 @@ from concourse.mybir import dt, AluOpType, ActivationFunctionType
 C = 384
 STEP = [2, 3, 1]
 ZP = [(0, 192), (192, 192)]
-XP = [(0, 192), (192, 192)]
-SHARE = 104
+XP = [(0, 256), (256, 128)]
+SHARE = 106
+WAKE = 240
+SROOM = 0
+FOLLOW = (0, 2, 2, 4, 3, 2, 4, 4)
+SLACK = 40
+LANDS = {"d_l": 2200, "d_x": 4500, "d_u": 3500, "d_w": 4500, "d_v": 3500, "d_o": 0, "d_s": 0, "d_y": 0, "ra": 1300, "rq": 5500}
 OP = AluOpType
-COPY = ActivationFunctionType.Copy
+COPY, IDENT = ActivationFunctionType.Copy, ActivationFunctionType.Identity
 F32, BF, I32, U16, X4, U8 = "float32", "bfloat16", "int32", "uint16", "float8_e4m3fn_x4", "uint8"
 SMALL = {}
-for _n, _w in (("cq", 12), ("cg", 12), ("ca", 12), ("ce", 12), ("cb", 12), ("jb", 4), ("ci", 4), ("cf", 8), ("cst", 8), ("e", 12), ("qq", 12),
-               ("t1", 12), ("df", 12), ("co", 12), ("m", 12), ("pr", 12), ("yy", 4), ("a0", 4), ("s1", 4), ("pos", 24)):
+for _n, _w in (("cj", 12), ("cz", 12), ("ca", 12), ("ce", 12), ("cb", 12), ("jb", 4), ("ci", 4), ("cf", 8), ("cst", 12), ("t1", 12),
+               ("df", 12), ("m", 12), ("a0", 8), ("rr", 8), ("pos", 24)):
     SMALL[_n] = (sum(k[1] for k in SMALL.values()), _w)
 
 
@@ -20,13 +25,14 @@ def _scratch():
 
     def sb(name, shape, d):
         s[name] = ("sbuf", [128] + shape, d)
-    sb("li", [96], I32); sb("rt", [400], F32); sb("pl", [192], U16); sb("pidx", [1], I32); sb("ti", [8], I32); sb("t12", [16], I32)
+    sb("li", [96], I32); sb("rt", [400], F32); sb("pl", [192], U16); sb("pidx", [1], I32); sb("ti", [8], I32)
     sb("sm", [sum(k[1] for k in SMALL.values())], F32)
-    sb("lp_", [12], U16); sb("lb", [12], U16); sb("la", [18], U16); sb("le", [6], U16); sb("ld", [6], U16)
-    sb("lo", [2], U16); sb("lu", [8], U16); sb("d", [12], F32)
+    sb("lp_", [12], U16); sb("lb", [12], U16); sb("la", [18], U16); sb("le", [6], U16); sb("ld", [6], U16); sb("lh", [16], U16)
+    sb("lo", [2], U16); sb("lu", [8], U16); sb("d", [16], F32)
     sb("sg", [96], F32); sb("mv", [112], F32); sb("h1", [3, 32], F32); sb("h2", [24], F32)
-    sb("iw", [C], F32); sb("im", [C], BF); sb("dm", [C], BF); sb("gca", [192], F32); sb("gcb", [192], F32)
-    sb("z32", [96], BF); sb("z16", [C], BF); sb("z8", [192], BF); sb("wgt", [192], F32)
+    sb("co", [96], F32); sb("hz", [96], F32); sb("hv", [96], F32); sb("hs", [3 * 96], F32)
+    sb("iw", [C], F32); sb("im", [C], BF); sb("dm", [C], BF); sb("gca", [96], F32); sb("gcb", [64], F32)
+    sb("z32", [192], BF); sb("z16", [C], BF); sb("z8", [96], BF); sb("wgt", [192], F32)
     sb("ones", [512], BF); sb("ebt", [2048], BF); sb("ec", [512], X4); sb("ep", [512], U8)
     sb("xb", [4 * C], BF); sb("ub", [512], BF); sb("vb16", [512], BF)
     sb("uq0", [128], X4); sb("up0", [128], U8); sb("uc", [128], X4); sb("upl", [128], U8)
@@ -41,7 +47,7 @@ def _scratch():
         sb("zc%d" % r, [C], X4); sb("zp%d" % r, [C], U8); sb("zt%d" % r, [4 * C], BF)
     sb("fb", [2 * C], BF); sb("dp", [4 * C], BF); sb("rs", [4 * C], F32); sb("gs", [2 * C], F32)
     sb("lab", [32], F32); sb("wk", [768], F32); sb("of", [8 * 96], F32); sb("offu", [32], U16)
-    sb("wks", [192], F32); sb("ofs", [192], F32); sb("offs", [8], U16)
+    sb("wks", [1024], F32); sb("ofs", [768], F32); sb("offs", [24], U16)
     sb("wa", [C], F32); sb("wo", [C], F32); sb("wt", [3, 8, 16], F32); sb("lf", [24], F32)
     sb("eq", [192], F32); sb("iv", [192], F32); sb("inv", [24], U16); sb("oh", [192], F32)
     sb("eb", [24], U16); sb("ef", [C], F32); sb("et", [C], F32); sb("sel", [96], F32); sb("es", [96], F32)
@@ -52,7 +58,7 @@ def _scratch():
 
 
 SCRATCH = _scratch()
-SEMAPHORES = (["qv", "qs", "qt", "qg", "loc", "d_l", "d_x", "d_u", "d_w", "d_v", "d_o", "d_ol", "d_y0", "d_y1"]
+SEMAPHORES = (["qv", "qs", "qt", "qg", "loc", "d_l", "d_x", "d_u", "d_w", "d_v", "d_o0", "d_o1", "d_s", "d_ol", "d_y0", "d_y1"]
               + ["rq%d" % r for r in range(3)] + ["ra%d" % r for r in range(3)])
 
 
@@ -104,8 +110,6 @@ def make_queue_tools(g, T):
                 p0, p1, m = region(ref)
                 for (h0, h1, hm, hw, hq, he) in hist.get(ref[0], ()):
                     if (hw or write or ref[0] == "ps" and hq != q) and h0 < p1 and p0 < h1 and hm & m:
-                        if not hw and hq == q:
-                            continue
                         ev.append(he)
         return ev
 
@@ -118,32 +122,98 @@ def make_queue_tools(g, T):
                     lst[:] = [h for h in lst if not (p0 <= h[0] and h[1] <= p1 and (h[2] & ~m) == 0)]
                 lst.append((p0, p1, m, write, q, ev))
 
-    def op(q, call, outs, ins):
-        need(q, deps(q, ins, outs))
+    free = {k: 0.0 for k in eng}
+    fin = {}
+    streams, done, mode, probe = [], set(), ["chain"], [0.0, 0.0, 0.0]
+
+    def ready(ev):
+        return max([fin.get(e, 0.0) + WAKE for e in ev] + [0.0])
+
+    def run(st):
+        call, name, _ = st.pop(0)
+        was, mode[0] = mode[0], "step"
+        call()
+        mode[0] = was
+        done.add(name)
+
+    def fill(until):
+        return fill1(until, 10) or fill1(until, 80) or fill1(until, 1000)
+
+    def fill1(until, most):
+        for st in streams:
+            if st and done.issuperset(st[0][2]):
+                mode[0], probe[0], probe[1], probe[2] = "probe", 0.0, 0.0, 0.0
+                st[0][0]()
+                mode[0] = "chain"
+                late, cycles = max(probe[0] - free["v"], 0), probe[1]
+                room = until - free["v"]
+                if probe[2] > until + SROOM or cycles and late > most:
+                    continue
+                if cycles == 0 or late + cycles <= room + SLACK or late <= SLACK and cycles > WAKE and room >= WAKE - SLACK:
+                    run(st)
+                    return True
+        return False
+
+    def stream(*steps):
+        streams.append([s[1:] + ("", ())[len(s) - 2:] for s in steps])
+
+    def upto(*names):
+        for name in names:
+            while name not in done:
+                st = [s for s in streams if any(x[1] == name for x in s)][0]
+                upto(*st[0][2])
+                run(st)
+
+    def op(q, call, outs, ins, fixed=0, each=1.0):
+        n = bin(region(ins[-1] if outs[0][0] == "ps" else outs[0])[2]).count("1")
+        cycles = fixed + each * n if fixed else max(64, each * n)
+        if mode[0] == "probe":
+            if q == "v":
+                probe[0] = max(probe[0], ready(deps(q, ins, outs)) - probe[1])
+                probe[1] += cycles
+            elif q == "s":
+                probe[2] = probe[2] or max(free["s"], ready(deps(q, ins, outs)))
+            return
+        if q == "v" and mode[0] == "chain":
+            while fill(ready(deps(q, ins, outs))):
+                pass
+        before = deps(q, ins, outs)
+        need(q, before)
         sem = own[q]
         count[sem] += 1
         ev = (sem, count[sem])
         call().then_inc(T.sem[sem], 1)
         clock[ev] = dict(known[q])
         clock[ev][sem] = count[sem]
+        free[q] = fin[ev] = max(free[q], ready(before)) + cycles
         note(q, ev, ins, outs)
 
     def dmas(sem, items):
+        if mode[0] == "probe":
+            return
         count[sem] += 16 * len(items)
         ev = (sem, count[sem])
         clock[ev] = {sem: count[sem]}
         for q, out, in_, outs, ins in items:
-            need(q, [e for e in deps(q, ins, outs) if e != ev])
+            before = [e for e in deps(q, ins, outs) if e != ev]
+            need(q, before)
             eng[q].dma_start(out, in_).then_inc(T.sem[sem], 16)
+            free[q] = max(free[q], ready(before)) + 64
+            fin[ev] = free[q] + LANDS[sem[:3]]
             for s, n in known[q].items():
                 if clock[ev].get(s, 0) < n:
                     clock[ev][s] = n
         for q, out, in_, outs, ins in items:
             note("dma", ev, ins, outs)
 
-    def send(call, ins, n):
-        need("g", deps("g", ins, []))
+    def send(call, ins, n, sem):
+        if mode[0] == "probe":
+            return
+        before = deps("g", ins, [])
+        need("g", before)
         call()
+        free["g"] = max(free["g"], ready(before)) + 300
+        fin[(sem, count[sem])] = free["g"] + LANDS[sem[:2]]
         count["loc"] += n
         clock[("loc", count["loc"])] = {"loc": count["loc"]}
 
@@ -157,15 +227,19 @@ def make_queue_tools(g, T):
         for s in SEMAPHORES:
             if count[s] and known["g"].get(s, 0) < count[s]:
                 g.wait_ge(T.sem[s], count[s])
-    return op, dmas, send, arrives, finish
+    return op, dmas, send, arrives, finish, stream, upto, done.add
 
 
 def rank_program(g, core, T, topo):
     rank = T.rank_of(core)
     if rank is None:
         return
-    op, dmas, send, arrives, finish = make_queue_tools(g, T)
+    op, dmas, send, arrives, finish, stream, upto, mark = make_queue_tools(g, T)
     S_ = slice
+    ROOM = 0
+
+    def pause(k=0):
+        pass
     ANY = slice(None)
 
     def R(name, *idx, p=slice(0, 128)):
@@ -199,15 +273,15 @@ def rank_program(g, core, T, topo):
 
     def gather(q, out, win, off):
         if q == "v":
-            op(q, lambda: g.vector.tensor_copy(V(out), V(win).indirect(V(off))), [out], [win, off])
+            op(q, lambda: g.vector.tensor_copy(V(out), V(win).indirect(V(off))), [out], [win, off], 60, 1.56)
         else:
-            op(q, lambda: g.scalar.activation(V(out), V(win).indirect(V(off)), COPY), [out], [win, off])
+            op(q, lambda: g.scalar.activation(V(out), V(win).indirect(V(off)), COPY), [out], [win, off], 80, 1.56)
 
     def gather_tt(out, win, off, in1, o):
-        op("v", lambda: g.vector.tensor_tensor(V(out), V(win).indirect(V(off)), V(in1), o), [out], [win, off, in1])
+        op("v", lambda: g.vector.tensor_tensor(V(out), V(win).indirect(V(off)), V(in1), o), [out], [win, off, in1], 60, 1.56)
 
     def tt(out, a, b, o):
-        op("v", lambda: g.vector.tensor_tensor(V(out), V(a), V(b), o), [out], [a, b])
+        op("v", lambda: g.vector.tensor_tensor(V(out), V(a), V(b), o), [out], [a, b], 0, 2)
 
     def ts(out, a, s1, s2, o0, o1=None):
         v1 = V(s1) if isinstance(s1, tuple) else s1
@@ -227,17 +301,26 @@ def rank_program(g, core, T, topo):
     def ms(out, c):
         op("v", lambda: g.vector.memset(V(out), c), [out], [])
 
+    def affine(out, in_, scale, bias=0.0):
+        ins = [in_] + [s for s in (scale, bias) if isinstance(s, tuple)]
+        op("s", lambda: g.scalar.activation(V(out), V(in_), IDENT, bias=V(bias) if isinstance(bias, tuple) else bias,
+                                            scale=V(scale) if isinstance(scale, tuple) else scale), [out], ins)
+
+    def fill_s(out, c):
+        i = out[1][1]
+        affine(out, R("ones", S_(0, len(range(i.start or 0, i.stop or SCRATCH[out[0]][1][1], i.step or 1)))), float(c))
+
     def quant(oc_, op_, in_):
-        op("v", lambda: g.vector.quantize_mx(V(oc_), V(op_), V(in_)), [oc_, op_], [in_])
+        op("v", lambda: g.vector.quantize_mx(V(oc_), V(op_), V(in_)), [oc_, op_], [in_], 15, 1.06)
 
     def mm(k, lc, lp, rc, rp, n=C):
-        op("t", lambda: g.tensor.matmul_mx(bank(k, n), V(lc), V(lp), V(rc), V(rp), True, True), [("ps", k)], [lc, lp, rc, rp])
+        op("t", lambda: g.tensor.matmul_mx(bank(k, n), V(lc), V(lp), V(rc), V(rp), True, True), [("ps", k)], [lc, lp, rc, rp], 12, 0.75)
 
     def iota(out, pattern, base, cm):
         if SCRATCH[out[0]][2] == I32:
-            op("g", lambda: g.iota(V(out), pattern, base, cm), [out], [])
+            op("g", lambda: g.iota(V(out), pattern, base, cm), [out], [], 160, 2)
         else:
-            op("g", lambda: g.iota(V(out), pattern, base, cm, allow_small_or_imprecise_dtypes=True), [out], [])
+            op("g", lambda: g.iota(V(out), pattern, base, cm, allow_small_or_imprecise_dtypes=True), [out], [], 160, 2)
 
     def quadrant(a):
         return slice(32 * a, 32 * a + 32)
@@ -248,13 +331,10 @@ def rank_program(g, core, T, topo):
     def partner(r):
         return T.cores[rank ^ STEP[r]]
 
-    def ways(src, dst):
-        return topo.engines(src, dst)[:8]
-
     def remote(r, out, in_, sem, ins):
         rid, pid, _ = topo.addr(partner(r))
-        e = ways(core, partner(r))
-        send(lambda: g.remote_dma(out, in_, T.sem[sem], T.sem.loc, pid, rid, sum(1 << k for k in e)), ins, len(e))
+        send(lambda: g.remote_dma(out, in_, T.sem[sem], T.sem.loc, pid, rid, topo.mask(core, partner(r))), ins,
+             len(topo.engines(core, partner(r))), sem)
 
     def q_of(r, a=0, n=C):
         return cols("qc%d" % r, a, n), cols("qp%d" % r, a, n)
@@ -263,13 +343,8 @@ def rank_program(g, core, T, topo):
         remote(r, T["lc%d" % r][:].bitcast(dt.uint8), T["qc%d" % r][:].bitcast(dt.uint8), "rq%d" % r, [R("qc%d" % r)])
         remote(r, T["lp%d" % r][:], T["qp%d" % r][:], "rq%d" % r, [R("qp%d" % r)])
 
-    def pause(fill, n=1):
-        for _ in range(n):
-            if fill:
-                fill.pop(0)()
-
     for r in range(3):
-        n = len(ways(partner(r), core))
+        n = len(topo.engines(partner(r), core))
         arrives("rq%d" % r, 2 * n, [R("lc%d" % r), R("lp%d" % r)])
         arrives("ra%d" % r, n, [R("zl%d" % r)])
 
@@ -281,8 +356,6 @@ def rank_program(g, core, T, topo):
     dmas("d_l", items)
     dmas("d_x", [("y", T.xb[:], T.x[:], [R("xb")], [])])
     dmas("d_u", [("s", T.ub[:], T.u[:], [R("ub")], [])])
-    dmas("d_w", [("y", T.wcod[:].bitcast(dt.uint8), T.wc[:], [R("wcod")], []), ("y", T.wpl[:], T.ws[:], [R("wpl")], [])])
-    dmas("d_v", [("y", T.vb16[:], T.v[:], [R("vb16")], [])])
 
     def ti(k):
         return cols("ti", k, 1)
@@ -293,138 +366,181 @@ def rank_program(g, core, T, topo):
     def c1(k):
         return cols("cst", k, 1)
     iota(R("pidx"), [[0, 1]], 0, 1)
-    iota(R("cq"), [[0, 4], [16, 3]], 0, 0)
-    iota(R("cg"), [[2, 4], [0, 3]], 8, 0)
+    iota(R("cj"), [[16, 12]], 0, 0)
+    iota(R("cz"), [[96, 4], [16, 3]], 0, 0)
     iota(R("ca"), [[2, 12]], 0, 0)
-    iota(R("iw"), [[1, C]], 0, 0)
     iota(cols("jb", 0, 3), [[32, 3]], 0, 1)
+    iota(R("cb"), [[8, 3], [0, 4]], 0, 0)
+    iota(R("iw"), [[1, C]], 0, 0)
     iota(R("im"), [[0, 24], [1, 16]], 0, 0)
     iota(cols("ce", 0, 6), [[128, 3], [0, 2]], 0, 0)
-    iota(R("cb"), [[8, 3], [0, 4]], 0, 0)
-    iota(R("gcb"), [[0, 3], [C, 8], [0, 8]], 0, 0)
-    iota(R("gca"), [[0, 24], [C, 8]], 0, 0)
+    iota(R("gcb"), [[C, 8], [0, 8]], 0, 0)
+    iota(R("gca"), [[0, 12], [C, 8]], 0, 0)
     ms(R("ones"), 1.0)
-    ms(cols("rt", C, 16), 0.0)
-    for name, a, n in (("wk", 0, C), ("wk", C, C), ("wks", 0, 192)):
-        o, i = cols(name, a, n), cols("ones", 0, n)
-        op("s", lambda: g.scalar.activation(V(o), V(i), COPY, scale=0.0), [o], [i])
+    for name, a, n in (("rt", C, 16), ("wk", 0, C), ("wk", C, C), ("wks", 0, C), ("wks", C, C)):
+        fill_s(cols(name, a, n), 0.0)
+    fill_s(R("z32"), 1.0)
+    for u in range(8):
+        fill_s(R("wgt", S_(u, 192, 8)), (9.0 - u) / (8.0 - u) if u else 0.0)
+    fill_s(R("z32", S_(0, 192, 32)), 0.0)
     I, M7, HI, G, A = range(5)
     ts(ti(I), R("pidx"), 15, None, OP.bitwise_and)
+    ts(ti(G), R("pidx"), 4, None, OP.arith_shift_right)
     ts(ti(M7), R("pidx"), 7, None, OP.bitwise_and)
     ts(ti(HI), R("pidx"), 3, 1, OP.arith_shift_right, OP.bitwise_and)
-    ts(ti(G), R("pidx"), 4, None, OP.arith_shift_right)
     ts(ti(A), R("pidx"), 5, None, OP.arith_shift_right)
-    cp("v", cols("cf", 0, 5), cols("ti", 0, 5))
     tt(ti(5), R("pidx"), ti(G), OP.subtract)
-    ts(R("e"), R("cq"), cf(I), 24.0, OP.add, OP.is_ge)
-    ts(R("qq"), R("cq"), cf(I), None, OP.add)
+    cp("v", cols("cf", 0, 5), cols("ti", 0, 5))
     ts(ti(6), ti(5), 7, None, OP.bitwise_and)
-    tt(R("t1"), R("e"), R("cg"), OP.add)
-    ts(R("e"), R("e"), -24.0, None, OP.mult)
+    ts(c1(5), cf(G), 24.0, cf(I), OP.mult, OP.subtract)
+    ts(c1(6), cf(G), -48.0, cf(I), OP.mult, OP.add)
+    ts(c1(7), cf(A), 4.0, cf(G), OP.mult, OP.add)
     ts(c1(0), ti(6), 48.0, 24.0, OP.mult, OP.add)
-    ts(cols("t12", 0, 12), R("t1"), cf(G), None, OP.subtract)
-    tt(R("qq"), R("qq"), R("e"), OP.add)
-    ts(c1(0), cf(A), 4.0, c1(0), OP.mult, OP.add)
-    ts(cols("t12", 0, 12), cols("t12", 0, 12), 7, None, OP.bitwise_and)
-    cp("v", cols("rt", 0, 96), R("li"))
-    ts(c1(0), cf(HI), 2.0, c1(0), OP.mult, OP.add)
-    ts(R("t1"), cols("t12", 0, 12), 48.0, None, OP.mult)
+    ts(R("t1"), R("cj"), c1(5), float(C), OP.is_lt, OP.mult)
+    ts(c1(8), cf(HI), 24.0, c1(6), OP.mult, OP.add)
+    ts(c1(7), cf(HI), 2.0, c1(7), OP.mult, OP.add)
+    ts(c1(4), cf(A), 64.0, None, OP.mult)
+    tt(R("t1"), R("t1"), R("cz"), OP.add)
+    ts(c1(2), cf(M7), 16.0, None, OP.mult)
+    ts(R("lo"), R("ca", S_(0, 4, 2)), c1(0), c1(7), OP.add, OP.add)
+    ts(cols("jb", 0, 3), cols("jb", 0, 3), c1(4), None, OP.add)
+    for v, (k, more) in enumerate(((6, 0.0), (8, 0.0), (6, 24.0))):
+        ts(R("lp_", S_(v, 12, 3)), R("t1", S_(v, 12, 3)), c1(k), more, OP.add, OP.add)
 
+    cp("v", cols("rt", 0, 96), R("li"))
+    ts(R("lu"), cols("ca", 0, 8), 0.0, c1(2), OP.mult, OP.add)
+    ts(R("lb"), R("cb"), cf(M7), None, OP.add)
     for a in range(4):
         cp("vs"[a % 2], R("rt", S_(96, 192), p=quadrant(a)), R("rt", S_(0, 96), p=quadrant((a + 1) % 4)))
-    tt(R("t1"), R("t1"), R("qq"), OP.add)
-    ts(R("lo"), R("ca", S_(0, 4, 2)), c1(0), cf(G), OP.add, OP.add)
+    ts(cols("la", 0, 6), cols("ca", 0, 6), cf(HI), 2.0, OP.add, OP.mult)
+    ts(R("ld"), cols("ca", 0, 6), cf(HI), None, OP.add)
     for h in range(2):
         cp("vs"[h], R("rt", S_(192, 384), p=S_(64 * h, 64 * h + 64)), R("rt", S_(0, 192), p=S_(64 - 64 * h, 128 - 64 * h)))
-    cp("v", R("lp_"), R("t1"))
-    ts(c1(4), cf(A), 64.0, None, OP.mult)
+    ts(cols("la", 6, 6), cols("la", 0, 6), 1.0, None, OP.add)
+    ts(R("la", S_(12, 18, 2)), R("la", S_(0, 6, 2)), 2.0, None, OP.add)
     gather("v", cols("pl", 0, 96), R("rt"), cols("lp_", 0, 6))
     gather("v", cols("pl", 96, 96), R("rt"), cols("lp_", 6, 6))
     gather("s", cols("tab", 0, 16 * 96), R("iw"), cols("pl", 0, 96))
     gather("s", cols("tab", 16 * 96, 16 * (SHARE - 96)), R("iw"), cols("pl", 96, SHARE - 96))
-    op("v", lambda: g.vector.tensor_scalar(T.lab[:], T.rt[:].indirect(T.lo[:]), float(C), None, OP.mult), [R("lab")], [R("rt"), R("lo")])
-    ts(cols("jb", 0, 3), cols("jb", 0, 3), c1(4), None, OP.add)
-    ms(R("z32"), 1.0)
+    op("v", lambda: g.vector.tensor_scalar(T.lab[:], T.rt[:].indirect(T.lo[:]), float(C), None, OP.mult), [R("lab")], [R("rt"), R("lo")], 60, 1.56)
 
     def unit_tile(b):
         o = cols("ebt", 512 * b, 512)
-        op("g", lambda: g.affine_select(V(o), T.ones[:], [[-1, 512]], OP.is_equal, 0.0, b, 4), [o], [R("ones")])
+        op("g", lambda: g.affine_select(V(o), T.ones[:], [[-1, 512]], OP.is_equal, 0.0, b, 4), [o], [R("ones")], 200, 2)
     for b in range(3):
         unit_tile(b)
 
+    now = {}
+
     def OF(k):
-        return R("of", S_(96 * k + 31, 96 * k + 96, 32))
+        return now.get(k) or R("of", S_(96 * k + 31, 96 * k + 96, 32))
 
     def U(k):
         return cols("offu", 4 * k, 3)
 
-    def lay_labels():
+    def lay_labels(q, k):
         for s in range(3):
-            cp("v", cols("wk", 256 * s, 8), cols("lab", 8 * s, 8))
+            cp(q, cols("wk", 256 * s + k, 8 - k), cols("lab", 8 * s + k, 8 - k))
 
-    lay_labels()
-    ms(R("z32", S_(0, 96, 32)), 0.0)
+    ts(cols("dm", 0, 96), cols("im", 0, 96), cf(I), None, OP.is_equal)
+    ts(R("la", S_(13, 18, 2)), R("la", S_(7, 12, 2)), cf(HI), 1.0, OP.subtract, OP.add)
     tt(OF(0), R("lab", S_(0, 24, 8)), cols("jb", 0, 3), OP.add)
-    ts(R("dm"), R("im"), cf(I), None, OP.is_equal)
+    lay_labels("v", 1)
     cp("v", U(0), OF(0))
     gather("v", cols("tab", 16 * SHARE, 16 * (192 - SHARE)), R("iw"), cols("pl", SHARE, 192 - SHARE))
-    dm = cols("dm", 0, 48)
 
     def clean(q, k):
         gather(q, cols("wa", 48 * k, 48), R("tab"), U(k))
 
-    def walk(first, fill):
+    def walk(r, first):
         for k in range(first, 7):
-            gather_tt(R("wk", S_(k + 9, 768, 16)), R("tab"), U(k), dm, OP.mult)
+            gather_tt(R("wk", S_(k + 9, 768, 16)), R("tab"), U(k), cols("dm", 0, 48), OP.mult)
             clean("s", k)
-            pause(fill)
-            scan(cols("of", 96 * (k + 1), 96), R("z32"), R("wk", S_(k + 1, 768, 8)))
-            pause(fill)
+            pause()
+            scan(cols("of", 96 * (k + 1), 96), cols("z32", 0, 96), R("wk", S_(k + 1, 768, 8)))
+            now.pop(k + 1, None)
+            mark("of%d%d" % (r, k + 1))
+            pause()
             cp("v", U(k + 1), OF(k + 1))
-            pause(fill)
+            pause()
         clean("v", 7)
-
-    def places():
-        return [lambda s=s: gather_tt(cols("eq", 64 * s, 64), R("lab"), cols("lb", 4 * s, 4), cols("gcb", 0, 64), OP.is_equal) for s in range(3)] + [
-            lambda: scan(R("iv"), R("wgt"), R("eq")),
-            lambda: [ts(cols("pos", 8 * s, 8), R("iv", S_(64 * s + 7, 64 * s + 64, 8)), -1.0, cols("ci", s, 1), OP.mult, OP.add) for s in range(3)],
-            place_offsets]
+        pause()
 
     def place_offsets():
         ts(R("inv"), R("pos"), 48.0, C + 0.25, OP.mult, OP.add)
 
-    def by_group(fill):
+    def by_group():
         gather("v", cols("wo", 0, 192), R("wa"), cols("inv", 0, 12))
         gather("s", cols("wo", 192, 192), R("wa"), cols("inv", 12, 12))
-        pause(fill)
+        pause()
         tr(R("wt"), R("wo"))
-        pause(fill)
+        pause()
 
     def score_offsets():
         cp("v", R("eb"), R("wt", ANY, ANY, 0))
 
-    def signs(k):
-        return [lambda: gather_tt(cols("oh", 0, 96), R("lab"), cols("la", 6 * k, 6), cols("gca", 0, 96), OP.is_equal),
-                lambda: gather_tt(cols("oh", 96, 96), R("lab"), cols("la", 6 * k + 6, 6), cols("gca", 0, 96), OP.is_equal),
-                lambda: tt(R("sg"), cols("oh", 0, 96), cols("oh", 96, 96), OP.subtract)]
+    def signs(r, needs):
+        k = r % 2
+        stream((210, lambda: gather_tt(cols("oh", 0, 96), R("lab"), cols("la", 6 * k, 6), R("gca"), OP.is_equal), "", needs),
+               (210, lambda: gather_tt(cols("oh", 96, 96), R("lab"), cols("la", 6 * k + 6, 6), R("gca"), OP.is_equal)),
+               (192, lambda: tt(R("sg"), cols("oh", 0, 96), cols("oh", 96, 96), OP.subtract), "sg%d" % r))
 
-    def ahead(k):
+    def coef(x, t):
+        return R("co", S_(4 * x + t, 96, 32))
+
+    def ahead(r, needs):
+        k = r % 2
         n = 12 - k
-        calls = [lambda: tt(cols("df", 0, n), R("lab", S_(k + 1, 24, 2)), R("lab", S_(k, k + 2 * n, 2)), OP.subtract),
-                 lambda: [cp("v", R("wks", S_(t, 192, 64)), R("lab", S_(k + 2 * t, 24, 8))) for t in range(2)],
-                 lambda: (tt(cols("a0", 0, 3), OF(k), R("df", S_(0, n, 4)), OP.add), cp("v", R("co", S_(1, 12, 4)), R("df", S_(1, n, 4)))),
-                 lambda: cp("v", cols("offs", 0, 3), cols("a0", 0, 3))]
-        for t in range(2):
-            calls.append(lambda t=t: gather_tt(R("wks", S_(t + 2, 192, 4)), R("tab"), cols("offs", 4 * t, 3), dm, OP.mult))
-            calls.append(lambda t=t: scan(cols("ofs", 96 * t, 96), R("z32"), R("wks", S_(t, 192, 2))))
-            if t == 0:
-                calls.append(lambda: (cp("v", cols("offs", 4, 3), R("ofs", S_(31, 96, 32))),
-                                      tt(cols("yy", 0, 3), R("ofs", S_(31, 96, 32)), OF(k + 1), OP.subtract)))
-        calls.append(lambda: tt(R("co", S_(0, 12, 4)), R("ofs", S_(127, 192, 32)), OF(k + 2), OP.subtract))
-        return calls
+
+        def df(q):
+            return R("df", S_(q, n, 4))
+
+        def res(t, v):
+            return R("ofs", S_(192 * t + 96 * v + 31, 192 * t + 96 * v + 96, 32))
+
+        def look(t):
+            return [(210, lambda: gather_tt(R("wks", S_(192 * t + 1, 192 * t + 192, 2)), R("tab"), cols("offs", 6 * t, 6), cols("dm", 0, 96), OP.mult)),
+                    (192, lambda: scan(cols("ofs", 192 * t, 192), R("z32"), cols("wks", 192 * t, 192)), "l%d%d" % (r, t))]
+
+        def begin():
+            tt(cols("df", 0, n), R("lab", S_(k + 1, 24, 2)), R("lab", S_(k, k + 2 * n, 2)), OP.subtract)
+            if r:
+                gather("s", R("wks", S_(0, 1024, 32)), R("lab"), cols("lh", 12 + 2 * k, 2))
+            else:
+                for e, x in enumerate(FOLLOW):
+                    cp("s", R("wks", S_(96 * e, 96 * e + 96, 32)), R("lab", S_(x, 24, 8)))
+
+        def starts():
+            for v in range(2):
+                tt(cols("a0", 3 * v, 3), OF(k + 2 * v), df(v), OP.add)
+
+        def plain():
+            for q, (x, t) in enumerate(((0, 1), (2, 2), (4, 3))):
+                cp("s", coef(x, t), df(q))
+            for x in range(5):
+                cp("s", coef(x + x // 4, 3 * (x < 4)), OF(k + x))
+
+        def second():
+            cp("v", cols("offs", 12, 3), res(1, 0))
+            for s in range(3):
+                ts(cols("offs", 15 + s, 1), cols("ofs", 192 + 32 * s + 31, 1), cols("df", 4 * s + 1, 1), None, OP.add)
+
+        def less(x, t, a):
+            tt(coef(x, t), a, OF(k + x), OP.subtract)
+        stream((64, begin, "begun%d" % r, needs), (128, starts), (64, lambda: cp("v", cols("offs", 0, 6), cols("a0", 0, 6))), *look(0),
+               (64, lambda: cp("v", cols("offs", 6, 6), R("ofs", S_(31, 192, 32)))), *look(1), (256, second), *look(2),
+               (64, lambda: cp("v", cols("offs", 18, 6), R("ofs", S_(C + 31, C + 192, 32)))), *look(3),
+               (128, lambda: (less(4, 1, res(3, 0)), tt(cols("rr", 3, 3), res(3, 1), res(3, 0), OP.subtract))),
+               (64, lambda: tt(coef(4, 0), cols("rr", 3, 3), coef(4, 2), OP.subtract), "a%d" % r, ("b%d" % r,)))
+        stream((128, lambda: (less(1, 1, res(0, 0)), less(3, 2, res(0, 1))), "", ("l%d0" % r, "of%d%d" % (r - 1, k + 3))),
+               (128, lambda: (less(2, 1, res(1, 0)), less(4, 2, res(1, 1))), "", ("l%d1" % r, "of%d%d" % (r - 1, k + 4))),
+               (0, plain, "", ("sent%d" % (r - 1),)),
+               (128, lambda: (less(3, 1, res(2, 0)), tt(cols("rr", 0, 3), res(2, 1), res(2, 0), OP.subtract)), "", ("l%d2" % r,)),
+               (64, lambda: tt(coef(3, 0), cols("rr", 0, 3), coef(3, 2), OP.subtract), "b%d" % r))
 
     def scores(r, a, n, q, k):
         mm(k, R("uc"), R("upl"), *q_of(r, a, n), n)
+        pause(2 * ROOM)
         frombank(q, cols("sct", a, n), k, n)
 
     def unpack(c, p, banks):
@@ -433,111 +549,140 @@ def rank_program(g, core, T, topo):
 
     def scoring_columns():
         op("v", lambda: g.vector.tensor_copy(T.uc[:].bitcast(dt.uint32), T.uq0[:].bitcast(dt.uint32).indirect(T.lu[:])),
-           [R("uc")], [R("uq0"), R("lu")])
-        op("s", lambda: g.scalar.activation(T.upl[:], T.up0[:].indirect(T.lu[:]), COPY), [R("upl")], [R("up0"), R("lu")])
-
-    def weights(t):
-        for u in (t, t + 1):
-            ms(R("wgt", S_(u, 192, 8)), (9.0 - u) / (8.0 - u) if u else 0.0)
+           [R("uc")], [R("uq0"), R("lu")], 60, 1.56)
+        op("s", lambda: g.scalar.activation(T.upl[:], T.up0[:].indirect(T.lu[:]), COPY), [R("upl")], [R("up0"), R("lu")], 80, 1.56)
 
     def first_state():
         quant(*q_of(0), R("xb"))
         send_state(0)
         unit_tile(3)
+        dmas("d_v", [("y", T.vb16[:], T.v[:], [R("vb16")], [R("xb")])])
+        dmas("d_w", [("y", T.wcod[:].bitcast(dt.uint8), T.wc[:], [R("wcod")], []), ("y", T.wpl[:], T.ws[:], [R("wpl")], [])])
 
-    def pair_lists():
-        ts(cols("la", 0, 6), cols("ca", 0, 6), cf(HI), 2.0, OP.add, OP.mult)
-        ts(cols("la", 6, 6), cols("la", 0, 6), 1.0, None, OP.add)
-        ts(R("la", S_(12, 18, 2)), R("la", S_(0, 6, 2)), 2.0, None, OP.add)
-        ts(R("la", S_(13, 18, 2)), R("la", S_(7, 12, 2)), cf(HI), 1.0, OP.subtract, OP.add)
-    aim, at, sg = ahead(0), places(), signs(0)
-    fill = [lambda: (ts(c1(2), cf(M7), 16.0, None, OP.mult), ts(R("lb"), R("cb"), cf(M7), None, OP.add)),
-            lambda: quant(R("uq0"), R("up0"), R("ub")),
-            lambda: (ts(R("lu"), cols("ca", 0, 8), 0.0, c1(2), OP.mult, OP.add), weights(0)),
-            first_state, at[0], scoring_columns, at[1],
-            lambda: (scores(0, 0, C, "s", 4), weights(2)), at[2],
-            lambda: (weights(4), weights(6)), pair_lists, at[3],
-            lambda: (ts(cols("ci", 0, 3), cols("cq", 0, 3), cf(I), 1.0 / 48, OP.add, OP.mult), aim[0](), aim[1]()),
-            lambda: (at[4](), aim[2]()), lambda: (aim[3](), ts(c1(1), cf(M7), 17.0, None, OP.mult)), lambda: (aim[4](), at[5]()),
-            lambda: (aim[5](), ts(R("le"), cols("ce", 0, 6), c1(1), None, OP.add)), sg[0], aim[6], aim[7], sg[1],
-            lambda: (aim[8](), ms(cols("z8", 0, 96), 1.0)), lambda: (sg[2](), ms(R("z8", S_(0, 96, 8)), 0.0)),
-            lambda: (aim[9](), ms(cols("mv", 96, 16), 0.0), ms(R("co", S_(2, 12, 4)), 0.0), ms(R("co", S_(3, 12, 4)), 0.0), ts(R("ld"), cols("ca", 0, 6), cf(HI), None, OP.add))]
-    walk(0, fill)
-    by_group(fill)
+    def first_scores():
+        mm(4, R("uc"), R("upl"), *q_of(0))
+        frombank("s", R("sct"), 4)
+
+    def lists_of(a, n, name):
+        return [(0, lambda: tt(cols("ys", a, n), cols("bg", a, n), cols("dm", 0, n), OP.mult)),
+                (0, lambda: scan(cols("bs", a, n), cols("z16", 0, n), cols("ys", a, n))),
+                (0, lambda: cp("v", cols("lh", a // 16, n // 16), R("bs", S_(a + 15, a + n, 16))), name)]
+
+    def factors(a):
+        for s in range(3):
+            if a == 0:
+                fill_s(R("bg", S_(32 * s, 32 * s + 20, 4)), 12)
+                fill_s(R("bg", S_(32 * s + 1, 32 * s + 20, 4)), 4 * s + 1)
+                fill_s(R("bg", S_(32 * s + 2, 32 * s + 20, 4)), 4 * s)
+            else:
+                fill_s(R("bg", S_(32 * s + 98, 32 * s + 116, 4)), 4 * s + 1)
+                fill_s(cols("bg", 32 * s + 115, 1), 4 * s + 2)
+
+    def followers():
+        for e, x in enumerate(FOLLOW):
+            affine(cols("bg", 192 + 3 * e, 3), R("cb", S_(0, 12, 4)), 1.0, float(x))
+        fill_s(cols("bg", 216, 8), 0.0)
+    mark("sent-1")
+    ahead(0, ("of-12", "co"))
+    stream(*[(160, lambda s=s: gather_tt(cols("eq", 64 * s, 64), R("lab"), cols("lb", 4 * s, 4), R("gcb"), OP.is_equal)) for s in range(3)],
+           (192, lambda: scan(R("iv"), R("wgt"), R("eq"))),
+           (0, lambda: ts(cols("ci", 0, 3), cols("cj", 0, 3), cf(I), 1.0 / 48, OP.add, OP.mult)),
+           (0, lambda: [affine(cols("pos", 8 * s, 8), R("iv", S_(64 * s + 7, 64 * s + 64, 8)), -1.0, cols("ci", s, 1)) for s in range(3)]),
+           (64, place_offsets, "inv-1"))
+    stream((150, lambda: quant(R("uq0"), R("up0"), R("ub"))), (420, first_state), (260, scoring_columns), (0, first_scores, "s0"))
+    stream((0, lambda: (fill_s(R("co"), 0.0), fill_s(cols("bg", 0, 192), 13), fill_s(R("z8"), 1.0), fill_s(cols("d", 12, 4), 0.0)), "co"),
+           (0, lambda: fill_s(cols("z16", 0, C), 1.0), "", ("begun0",)), (0, lambda: factors(0)), (0, lambda: factors(1)),
+           (0, lambda: (fill_s(R("z16", S_(0, C, 16)), 0.0), fill_s(R("z8", S_(0, 96, 8)), 0.0), fill_s(cols("d", 13, 1), 1.0), affine(c1(1), cf(M7), 17.0))),
+           (0, lambda: ts(R("le"), cols("ce", 0, 6), c1(1), None, OP.add), "le"), *lists_of(0, 96, ""), *lists_of(96, 96, "lh"), (0, followers),
+           (0, lambda: (affine(cols("bg", 224, 32), cols("bg", 192, 32), 1.0, 1.0), affine(c1(3), cf(G), float(C)),
+                        fill_s(cols("mv", 96, 16), 0.0), fill_s(cols("olf", 24, 8), 0.0))), *lists_of(192, 64, "lf"))
+    signs(0, ())
+    stream(*[(150, lambda b=b: quant(cols("ec", 128 * b, 128), cols("ep", 128 * b, 128), cols("ebt", 512 * b, 512)), "e%d" % b, ("s0", "inv-1")) for b in range(4)],
+           (0, lambda: ts(cols("dm", 96, C - 96), cols("im", 96, C - 96), cf(I), None, OP.is_equal), "dm"))
+    walk(-1, 0)
+    upto("inv-1")
+    by_group()
+    upto("s0")
     score_offsets()
+
+    def own_numbers(r):
+        unpack("qc%d" % r, "qp%d" % r, (0, 1, 6, 7))
+        for b in range(2):
+            frombank("s", cols("fb", C * b, C), b)
+        unpack("lc%d" % r, "lp%d" % r, (2, 3, 0, 1))
 
     for r in range(3):
         k = r % 2
         n = 12 - k
         gather("v", cols("ef", 0, 192), R("sct"), cols("eb", 0, 12))
         gather("s", cols("ef", 192, 192), R("sct"), cols("eb", 12, 12))
-        pause(fill, 99)
+        stream((0, lambda r=r: own_numbers(r), "own%d" % r, ("e3",)))
         tr(R("et"), R("ef"))
-        if r == 0:
-            quant(cols("ec", 0, 128), cols("ep", 0, 128), cols("ebt", 0, 512))
+        pause()
+        upto("sg%d" % r, "le")
         gather_tt(R("sel"), R("et"), R("le"), R("sg"), OP.mult)
-        if r == 0:
-            quant(cols("ec", 128, 128), cols("ep", 128, 128), cols("ebt", 512, 512))
-        scan(R("es"), cols("z8", 0, 96), R("sel"))
-        if r == 0:
-            quant(cols("ec", 256, 128), cols("ep", 256, 128), cols("ebt", 1024, 512))
-        ts(R("d"), R("es", S_(7, 96, 8)), 0.0, None, OP.is_gt)
-        if r == 0:
-            quant(cols("ec", 384, 128), cols("ep", 384, 128), cols("ebt", 1536, 512))
+        pause()
+        scan(R("es"), R("z8"), R("sel"))
+        pause()
+        ts(cols("d", 0, 12), R("es", S_(7, 96, 8)), 0.0, None, OP.is_gt)
+        upto("a%d" % r, "lh")
         m = cols("m", 0, n)
-        tt(R("pr"), R("d"), R("co"), OP.mult)
+        gather_tt(R("hv"), R("d"), cols("lh", 6, 6), R("co"), OP.mult)
+        gather("s", R("hz"), R("d"), cols("lh", 0, 6))
         tt(m, cols("d", 0, n), cols("df", 0, n), OP.mult)
-        for s in range(3):
-            ts(cols("offu", 4 * (k + 2) + s, 1), cols("pr", 4 * s, 1), cols("pr", 4 * s + 1, 1), cols("of", 96 * (k + 2) + 32 * s + 31, 1), OP.add, OP.add)
-        tt(R("lab", S_(k + 1, 24, 2)), R("lab", S_(k + 1, 24, 2)), m, OP.subtract)
+        scan(cols("hs", 96 * r, 96), R("hz"), R("hv"))
+        tt(R("wk", S_(k + 5, 768, 256)), R("lab", S_(k + 5, 24, 8)), R("m", S_(2, n, 4)), OP.subtract)
         tt(R("lab", S_(k, k + 2 * n, 2)), R("lab", S_(k, k + 2 * n, 2)), m, OP.add)
 
-        def own_numbers():
-            unpack("qc%d" % r, "qp%d" % r, (0, 1, 6, 7))
-            for b in range(2):
-                frombank("s", cols("fb", C * b, C), b)
-            unpack("lc%d" % r, "lp%d" % r, (2, 3, 0, 1))
-        fill = [lambda: (lay_labels(), own_numbers()),
-                lambda: (tt(cols("s1", 0, 3), R("d", S_(0, n, 4)), cols("yy", 0, 3), OP.mult), tt(OF(k), OF(k), R("m", S_(0, n, 4)), OP.add)),
-                lambda: gather_tt(cols("mv", 0, 96), R("d"), R("ld"), R("sg"), OP.mult),
-                lambda: (tt(OF(k + 1), OF(k + 1), cols("s1", 0, 3), OP.add), cp("v", U(k), OF(k))),
-                lambda: tt(R("h1"), cols("mv", 0, 96), cols("mv", 16, 96), OP.add),
-                lambda: (cp("v", U(k + 1), OF(k + 1)), clean("s", k), clean("s", k + 1), tt(R("h2"), R("h1", ANY, S_(0, 8)), R("h1", ANY, S_(8, 16)), OP.add))]
+        for x in range(5):
+            now[k + x] = R("hs", S_(96 * r + 4 * x + 3 + 4 * (x // 4), 96 * r + 96, 32))
+        cp("v", U(k + 4), OF(k + 4))
+        tt(R("lab", S_(k + 1, 24, 2)), R("lab", S_(k + 1, 24, 2)), m, OP.subtract)
+        cp("v", U(k), OF(k))
+        cp("v", U(k + 1), OF(k + 1))
+        lay_labels("s", k + 6)
+
+        def kept(k=k):
+            for x in (2, 3):
+                cp("v", U(k + x), OF(k + x))
+            for x in range(4):
+                clean("s", k + x)
+        stream((210, lambda: gather_tt(cols("mv", 0, 96), R("d"), R("ld"), R("sg"), OP.mult), "mv%d" % r),
+               (0, lambda: None, "", ("lf",)),
+               (192, lambda: tt(R("h1"), cols("mv", 0, 96), cols("mv", 16, 96), OP.add)),
+               (64, lambda: tt(R("h2"), R("h1", ANY, S_(0, 8)), R("h1", ANY, S_(8, 16)), OP.add)),
+               (64, lambda: tt(R("pos"), R("pos"), R("h2"), OP.add)), (64, place_offsets, "inv%d" % r))
+        stream((128, kept, "kept%d" % r, ("mv%d" % r,)))
+        for x in range(k + 5):
+            mark("of%d%d" % (r, x))
         if r < 2:
-            aim = ahead(1 - k)
-            fill += [lambda: (cp("v", OF(k + 2), U(k + 2)), aim[0]()), lambda: (tt(R("pos"), R("pos"), R("h2"), OP.add), aim[1]()),
-                     aim[2], lambda: (place_offsets(), aim[3]())] + aim[4:]
+            ahead(r + 1, ("kept%d" % r, "lf"))
+            signs(r + 1, ("mv%d" % r,))
         else:
-            fill += [lambda: (tt(R("pos"), R("pos"), R("h2"), OP.add), ms(cols("olf", 24, 8), 0.0)),
-                     lambda: [ts(R("olf", S_(s, 24, 3)), cols("lab", 8 * s, 8), 1.0 / C, None, OP.mult) for s in range(2)],
-                     lambda: (place_offsets(), ts(R("olf", S_(2, 24, 3)), cols("lab", 16, 8), 1.0 / C, None, OP.mult)), lambda: None,
-                     lambda: tr(R("olt"), R("olf")),
-                     lambda: dmas("d_ol", [("y", T.ol[:, 96 * a:96 * a + 96], T.olt[32 * a:32 * a + 24, :], [], [R("olt")]) for a in range(4)])]
-        if r == 0:
-            fill += [lambda: (ts(c1(3), cf(G), float(C), None, OP.mult), ms(R("z16"), 1.0))]
-        walk(k + 2, fill)
-        by_group(fill)
+            stream((0, lambda: [affine(R("olf", S_(s, 24, 3)), cols("lab", 8 * s, 8), 1.0 / C) for s in range(3)], "", ("own2",)), (0, lambda: None),
+                   (64, lambda: tr(R("olt"), R("olf"))),
+                   (0, lambda: dmas("d_ol", [("y", T.ol[:, 96 * a:96 * a + 96], T.olt[32 * a:32 * a + 24, :], [], [R("olt")]) for a in range(4)])),
+                   (150, lambda: quant(R("vq"), R("vp"), R("vb16")), "v"))
+        walk(r, k + 4)
+        upto("inv%d" % r, "kept%d" % r, "own%d" % r, "dm")
+        by_group()
         for a in range(4):
             for c in range(4):
                 cp("vs"[c % 2], R("lf", S_(6 * a, 6 * a + 6), p=quadrant(c)), R("wt", ANY, S_(2 * c, 2 * c + 2), 0, p=quadrant(a)))
-        pause(fill)
+        pause()
         cp("v", R("al%d" % r), R("lf"))
         remote(r, T["zl%d" % r][:], T["al%d" % r][:], "ra%d" % r, [R("al%d" % r)])
-        for b in range(4):
+        for b in (0, 2, 3):
             frombank("s", cols("dp", C * b, C), (2, 3, 0, 1)[b])
-        pause(fill, 99)
+        mark("sent%d" % r)
         ts(R("ab"), R("lf"), c1(3), None, OP.add)
-        fill = signs(1 - k) + [score_offsets] if r < 2 else []
-        if r == 0:
-            ms(R("z16", S_(0, C, 16)), 0.0)
-            fill.append(lambda: quant(R("vq"), R("vp"), R("vb16")))
-        pause(fill)
+        if r < 2:
+            score_offsets()
+        pause()
         gather_tt(R("bg"), R("tab"), R("ab"), R("dm"), OP.mult)
-        pause(fill)
-        scan(R("bs"), R("z16"), R("bg"))
-        pause(fill)
-        cp("v", R("bl"), R("bs", S_(15, C, 16)))
-        pause(fill, 99)
+        pause()
+        frombank("v", cols("dp", C, C), 3)
+        pause()
         zt, zc, zp, zl = "zt%d" % r, "zc%d" % r, "zp%d" % r, "zl%d" % r
 
         def mosaic(h, b):
@@ -562,7 +707,9 @@ def rank_program(g, core, T, topo):
             layer(0, b, kb)
             products("s", 0, b, kb)
         mosaic(1, 1)
+        pause()
         quant_z(1)
+        scan(R("bs"), R("z16"), R("bg"))
         nx = "xs%d" % (r + 1)
 
         def place(h, b):
@@ -583,25 +730,34 @@ def rank_program(g, core, T, topo):
         for b, kb in ((0, 4), (2, 5), (1, 0), (3, 1)):
             layer(1, b, kb)
             products("vs"[b // 2], 1, b, kb)
+            if b == 0:
+                cp("v", R("bl"), R("bs", S_(15, C, 16)))
         for h in range(2):
             for b in range(4):
                 pick(h, b)
-        for h in range(2):
-            add(h, 2)
-            add(h, 3)
+        for h, b in ((0, 2), (0, 3), (1, 2), (1, 3))[:3 if r == 2 else 4]:
+            add(h, b)
         for h in range(2):
             a, w = XP[h]
+            if r == 2 and h:
+                add(1, 3)
             quant(*q_of(r + 1, a, w), cols(nx, 4 * a, 4 * w))
-            if r < 2:
-                scores(r + 1, a, w, "sv"[h], 4 + h)
-            else:
+            if r == 2:
+                upto("v")
                 mm(4 + h, R("vq"), R("vp"), *q_of(3, a, w), w)
-                frombank("sv"[h], cols("ys", a, w), 4 + h, w)
-                dmas("d_y%d" % h, [("y", T.y[:, a:a + w], T.ys[:, a:a + w], [], [cols("ys", a, w)])])
-        if r < 2:
-            send_state(r + 1)
+                dmas("d_o%d" % h, [("y", T.oc[:, 4 * a:4 * (a + w)], T.qc3[:, a:a + w].bitcast(dt.uint8), [], [q_of(3, a, w)[0]])])
+            elif h == 0:
+                mm(4, R("uc"), R("upl"), *q_of(r + 1, a, w), w)
+                frombank("s", cols("sct", a, w), 4, w)
+            else:
+                send_state(r + 1)
+                scores(r + 1, a, w, "v", 5)
+                pause()
 
-    qc, qp = q_of(3)
-    dmas("d_o", [("s", T.oc[:], T.qc3[:].bitcast(dt.uint8), [], [qc])]
-         + [(("s", "y")[k % 2], T.osc[4 * k:4 * k + 4, :], T.qp3[32 * k:32 * k + 4, :], [], [qp]) for k in range(4)])
+    for h in range(2):
+        a, w = XP[h]
+        frombank("sv"[h], cols("ys", a, w), 4 + h, w)
+        if h:
+            dmas("d_s", [("ys"[k % 2], T.osc[4 * k:4 * k + 4, :], T.qp3[32 * k:32 * k + 4, :], [], [R("qp3")]) for k in range(4)])
+        dmas("d_y%d" % h, [("sy"[h], T.y[:, a:a + w], T.ys[:, a:a + w], [], [cols("ys", a, w)])])
     finish()

@@ -3,11 +3,14 @@ from concourse.mybir import dt, AluOpType, ActivationFunctionType
 
 C = 384
 STEP = [2, 3, 1]
-ZP = [(0, 192), (192, 192)]
+ZP = [(0, 224), (224, 160)]
 XP = [(0, 256), (256, 128)]
-SHARE = 106
+SHARE = 138
 WAKE = 240
 SROOM = 0
+EARLY = [["oh0"]]
+DPS = 1
+RQ = "vvss"
 FOLLOW = (0, 2, 2, 4, 3, 2, 4, 4)
 SLACK = 40
 LANDS = {"d_l": 2200, "d_x": 4500, "d_u": 3500, "d_w": 4500, "d_v": 3500, "d_o": 0, "d_s": 0, "d_y": 0, "ra": 1300, "rq": 5500}
@@ -16,7 +19,7 @@ COPY, IDENT = ActivationFunctionType.Copy, ActivationFunctionType.Identity
 F32, BF, I32, U16, X4, U8 = "float32", "bfloat16", "int32", "uint16", "float8_e4m3fn_x4", "uint8"
 SMALL = {}
 for _n, _w in (("cj", 12), ("cz", 12), ("ca", 12), ("ce", 12), ("cb", 12), ("jb", 4), ("ci", 4), ("cf", 8), ("cst", 12), ("t1", 12),
-               ("df", 12), ("m", 12), ("a0", 8), ("rr", 8), ("pos", 24)):
+               ("df", 12), ("m", 12), ("a0", 8), ("rr", 8), ("pos", 24), ("pa", 24), ("pe", 24), ("os", 36)):
     SMALL[_n] = (sum(k[1] for k in SMALL.values()), _w)
 
 
@@ -25,19 +28,19 @@ def _scratch():
 
     def sb(name, shape, d):
         s[name] = ("sbuf", [128] + shape, d)
-    sb("li", [96], I32); sb("rt", [400], F32); sb("pl", [192], U16); sb("pidx", [1], I32); sb("ti", [8], I32)
+    sb("li", [96], I32); sb("rt", [208], F32); sb("pl", [192], U16); sb("pidx", [1], I32); sb("ti", [12], I32)
     sb("sm", [sum(k[1] for k in SMALL.values())], F32)
-    sb("lp_", [12], U16); sb("lb", [12], U16); sb("la", [18], U16); sb("le", [6], U16); sb("ld", [6], U16); sb("lh", [16], U16)
-    sb("lo", [2], U16); sb("lu", [8], U16); sb("d", [16], F32)
-    sb("sg", [96], F32); sb("mv", [112], F32); sb("h1", [3, 32], F32); sb("h2", [24], F32)
-    sb("co", [96], F32); sb("hz", [96], F32); sb("hv", [96], F32); sb("hs", [3 * 96], F32)
-    sb("iw", [C], F32); sb("im", [C], BF); sb("dm", [C], BF); sb("gca", [96], F32); sb("gcb", [64], F32)
-    sb("z32", [192], BF); sb("z16", [C], BF); sb("z8", [96], BF); sb("wgt", [192], F32)
+    sb("lb", [12], U16); sb("la", [18], U16); sb("le", [6], U16); sb("lh", [24], U16)
+    sb("lo", [2], U16); sb("lu", [8], U16); sb("d", [36], F32)
+    sb("sg", [112], F32); sb("mv", [128], F32); sb("cx", [128], F32); sb("wx", [128], F32); sb("px", [128], F32); sb("z5", [128], BF)
+    sb("co", [64], F32); sb("hz", [64], F32); sb("hs", [3 * 64], F32)
+    sb("iw", [C], F32); sb("im", [C], BF); sb("dm", [C], BF); sb("gc", [96], F32)
+    sb("z32", [192], BF); sb("z16", [C], BF); sb("z8", [192], BF); sb("wgt", [192], F32)
     sb("ones", [512], BF); sb("ebt", [2048], BF); sb("ec", [512], X4); sb("ep", [512], U8)
     sb("xb", [4 * C], BF); sb("ub", [512], BF); sb("vb16", [512], BF)
     sb("uq0", [128], X4); sb("up0", [128], U8); sb("uc", [128], X4); sb("upl", [128], U8)
     sb("vq", [128], X4); sb("vp", [128], U8); sb("wcod", [512], X4); sb("wpl", [512], U8)
-    sb("tab", [8 * C], F32); sb("sct", [C], F32)
+    sb("tab", [8 * C + 7 * 48], F32); sb("sct", [C], F32)
     for r in range(4):
         sb("qc%d" % r, [C], X4); sb("qp%d" % r, [C], U8)
         if r:
@@ -48,10 +51,10 @@ def _scratch():
     sb("fb", [2 * C], BF); sb("dp", [4 * C], BF); sb("rs", [4 * C], F32); sb("gs", [2 * C], F32)
     sb("lab", [32], F32); sb("wk", [768], F32); sb("of", [8 * 96], F32); sb("offu", [32], U16)
     sb("wks", [1024], F32); sb("ofs", [768], F32); sb("offs", [24], U16)
-    sb("wa", [C], F32); sb("wo", [C], F32); sb("wt", [3, 8, 16], F32); sb("lf", [24], F32)
+    sb("wo", [C], BF); sb("wt", [3, 8, 16], BF); sb("lf", [24], F32)
     sb("eq", [192], F32); sb("iv", [192], F32); sb("inv", [24], U16); sb("oh", [192], F32)
-    sb("eb", [24], U16); sb("ef", [C], F32); sb("et", [C], F32); sb("sel", [96], F32); sb("es", [96], F32)
-    sb("ab", [24], U16); sb("bg", [C], F32); sb("bs", [C], F32); sb("bl", [24], U16)
+    sb("eb", [24], U16); sb("ef", [C], F32); sb("et", [C], F32); sb("sel", [96], F32); sb("es", [112], F32)
+    sb("bg", [C], F32); sb("bs", [C], F32); sb("bl", [24], U16)
     sb("olf", [32], F32); sb("olt", [32], F32); sb("ys", [C], F32)
     s["ps"] = ("psum", [128, 4096], F32)
     return s
@@ -154,8 +157,8 @@ def make_queue_tools(g, T):
                     return True
         return False
 
-    def stream(*steps):
-        streams.append([s[1:] + ("", ())[len(s) - 2:] for s in steps])
+    def stream(*steps, first=False):
+        streams.insert(0 if first else len(streams), [s[1:] + ("", ())[len(s) - 2:] for s in steps])
 
     def upto(*names):
         for name in names:
@@ -349,10 +352,10 @@ def rank_program(g, core, T, topo):
         arrives("ra%d" % r, n, [R("zl%d" % r)])
 
     items = []
-    for q, src, a in (("y", T.pg, 0), ("s", T.og, 24)):
+    for q, src, a in (("y", T.pg, 0), ("s", T.og, 48)):
         items.append((q, T.li[:, a:a + 24], src[:], [cols("li", a, 24)], []))
-        items.append((q, T.li[0:112, 48 + a:72 + a], src[16:128, :], [cols("li", 48 + a, 24)], []))
-        items.append((q, T.li[112:128, 48 + a:72 + a], src[0:16, :], [], []))
+        items.append((q, T.li[0:112, 24 + a:48 + a], src[16:128, :], [cols("li", 24 + a, 24)], []))
+        items.append((q, T.li[112:128, 24 + a:48 + a], src[0:16, :], [], []))
     dmas("d_l", items)
     dmas("d_x", [("y", T.xb[:], T.x[:], [R("xb")], [])])
     dmas("d_u", [("s", T.ub[:], T.u[:], [R("ub")], [])])
@@ -366,71 +369,74 @@ def rank_program(g, core, T, topo):
     def c1(k):
         return cols("cst", k, 1)
     iota(R("pidx"), [[0, 1]], 0, 1)
-    iota(R("cj"), [[16, 12]], 0, 0)
-    iota(R("cz"), [[96, 4], [16, 3]], 0, 0)
     iota(R("ca"), [[2, 12]], 0, 0)
+    iota(R("gc"), [[0, 12], [1, 8]], 0, 0)
+    iota(R("cj"), [[32, 3], [2, 4]], 0, 0)
     iota(cols("jb", 0, 3), [[32, 3]], 0, 1)
     iota(R("cb"), [[8, 3], [0, 4]], 0, 0)
     iota(R("iw"), [[1, C]], 0, 0)
     iota(R("im"), [[0, 24], [1, 16]], 0, 0)
+    iota(R("wgt"), [[16, 3], [0, 8], [48, 8]], 8 * C, 0)
     iota(cols("ce", 0, 6), [[128, 3], [0, 2]], 0, 0)
-    iota(R("gcb"), [[C, 8], [0, 8]], 0, 0)
-    iota(R("gca"), [[0, 12], [C, 8]], 0, 0)
+    iota(cols("bg", 128, 120), [[4, 3], [0, 8], [1, 5]], 0, 0)
+    iota(cols("bg", 256, 120), [[32, 3], [1, 8], [8, 5]], 0, 0)
     ms(R("ones"), 1.0)
-    for name, a, n in (("rt", C, 16), ("wk", 0, C), ("wk", C, C), ("wks", 0, C), ("wks", C, C)):
+    for name, a, n in (("rt", 192, 16), ("wk", 0, C), ("wk", C, C), ("wks", 0, C), ("wks", C, C)):
         fill_s(cols(name, a, n), 0.0)
     fill_s(R("z32"), 1.0)
-    for u in range(8):
-        fill_s(R("wgt", S_(u, 192, 8)), (9.0 - u) / (8.0 - u) if u else 0.0)
+    fill_s(R("z8"), 1.0)
     fill_s(R("z32", S_(0, 192, 32)), 0.0)
+    fill_s(R("z8", S_(0, 192, 8)), 0.0)
     I, M7, HI, G, A = range(5)
     ts(ti(I), R("pidx"), 15, None, OP.bitwise_and)
     ts(ti(G), R("pidx"), 4, None, OP.arith_shift_right)
     ts(ti(M7), R("pidx"), 7, None, OP.bitwise_and)
     ts(ti(HI), R("pidx"), 3, 1, OP.arith_shift_right, OP.bitwise_and)
     ts(ti(A), R("pidx"), 5, None, OP.arith_shift_right)
-    tt(ti(5), R("pidx"), ti(G), OP.subtract)
-    cp("v", cols("cf", 0, 5), cols("ti", 0, 5))
-    ts(ti(6), ti(5), 7, None, OP.bitwise_and)
-    ts(c1(5), cf(G), 24.0, cf(I), OP.mult, OP.subtract)
-    ts(c1(6), cf(G), -48.0, cf(I), OP.mult, OP.add)
+    ts(ti(5), R("pidx"), 1, None, OP.bitwise_and)
+    ts(ti(6), R("pidx"), 1, 3, OP.arith_shift_right, OP.bitwise_and)
+    tt(ti(7), R("pidx"), ti(G), OP.subtract)
+    cp("v", cols("cf", 0, 7), cols("ti", 0, 7))
+    ts(ti(8), ti(7), 7, None, OP.bitwise_and)
     ts(c1(7), cf(A), 4.0, cf(G), OP.mult, OP.add)
-    ts(c1(0), ti(6), 48.0, 24.0, OP.mult, OP.add)
-    ts(R("t1"), R("cj"), c1(5), float(C), OP.is_lt, OP.mult)
-    ts(c1(8), cf(HI), 24.0, c1(6), OP.mult, OP.add)
-    ts(c1(7), cf(HI), 2.0, c1(7), OP.mult, OP.add)
+    ts(c1(0), ti(8), 24.0, None, OP.mult)
     ts(c1(4), cf(A), 64.0, None, OP.mult)
-    tt(R("t1"), R("t1"), R("cz"), OP.add)
     ts(c1(2), cf(M7), 16.0, None, OP.mult)
-    ts(R("lo"), R("ca", S_(0, 4, 2)), c1(0), c1(7), OP.add, OP.add)
+    ts(cols("eq", 0, 96), R("gc"), cf(G), 8.0 * C, OP.is_lt, OP.mult)
+    ts(c1(5), cf(5), 96.0, cf(HI), OP.mult, OP.add)
+    ts(c1(7), cf(HI), 2.0, c1(7), OP.mult, OP.add)
+    ts(R("gc"), R("gc"), cf(G), float(C), OP.subtract, OP.mult)
     ts(cols("jb", 0, 3), cols("jb", 0, 3), c1(4), None, OP.add)
-    for v, (k, more) in enumerate(((6, 0.0), (8, 0.0), (6, 24.0))):
-        ts(R("lp_", S_(v, 12, 3)), R("t1", S_(v, 12, 3)), c1(k), more, OP.add, OP.add)
-
-    cp("v", cols("rt", 0, 96), R("li"))
+    ts(R("lo"), R("ca", S_(0, 4, 2)), c1(0), c1(7), OP.add, OP.add)
     ts(R("lu"), cols("ca", 0, 8), 0.0, c1(2), OP.mult, OP.add)
-    ts(R("lb"), R("cb"), cf(M7), None, OP.add)
-    for a in range(4):
-        cp("vs"[a % 2], R("rt", S_(96, 192), p=quadrant(a)), R("rt", S_(0, 96), p=quadrant((a + 1) % 4)))
+    ts(c1(6), cf(6), 8.0, None, OP.mult)
+    tt(R("gc"), R("gc"), cols("eq", 0, 96), OP.add)
+
+    for name, a in (("pl", 0), ("rt", 48)):
+        cp("v", cols(name, 0, 48), cols("li", a, 48))
+    gather("s", cols("tab", 0, 2 * C), R("iw"), cols("pl", 0, 48))
+    for name, a0 in (("pl", 0), ("rt", 48)):
+        for a in range(4):
+            cp("v", R(name, S_(48, 96), p=quadrant(a)), R("li", S_(a0, a0 + 48), p=quadrant((a + 1) % 4)))
+    gather("s", cols("tab", 2 * C, 2 * C), R("iw"), cols("pl", 48, 48))
+    ts(R("lb"), R("cj"), c1(5), c1(6), OP.add, OP.add)
     ts(cols("la", 0, 6), cols("ca", 0, 6), cf(HI), 2.0, OP.add, OP.mult)
-    ts(R("ld"), cols("ca", 0, 6), cf(HI), None, OP.add)
-    for h in range(2):
-        cp("vs"[h], R("rt", S_(192, 384), p=S_(64 * h, 64 * h + 64)), R("rt", S_(0, 192), p=S_(64 - 64 * h, 128 - 64 * h)))
-    ts(cols("la", 6, 6), cols("la", 0, 6), 1.0, None, OP.add)
-    ts(R("la", S_(12, 18, 2)), R("la", S_(0, 6, 2)), 2.0, None, OP.add)
-    gather("v", cols("pl", 0, 96), R("rt"), cols("lp_", 0, 6))
-    gather("v", cols("pl", 96, 96), R("rt"), cols("lp_", 6, 6))
-    gather("s", cols("tab", 0, 16 * 96), R("iw"), cols("pl", 0, 96))
-    gather("s", cols("tab", 16 * 96, 16 * (SHARE - 96)), R("iw"), cols("pl", 96, SHARE - 96))
-    op("v", lambda: g.vector.tensor_scalar(T.lab[:], T.rt[:].indirect(T.lo[:]), float(C), None, OP.mult), [R("lab")], [R("rt"), R("lo")], 60, 1.56)
+    for name in ("pl", "rt"):
+        for h in range(2):
+            cp("v", R(name, S_(96, 192), p=S_(64 * h, 64 * h + 64)), R(name, S_(0, 96), p=S_(64 - 64 * h, 128 - 64 * h)))
+    gather("s", cols("tab", 4 * C, 16 * (SHARE - 96)), R("iw"), cols("pl", 96, SHARE - 96))
+    for out, k, o in (("olf", 8.0 * C, OP.is_lt), ("lab", float(C), OP.subtract)):
+        op("v", lambda: g.vector.tensor_scalar(T[out][:], T.rt[:].indirect(T.lo[:]), V(cf(G)), k, o, OP.mult), [R(out)], [R("rt"), R("lo"), cf(G)], 60, 1.56)
 
     def unit_tile(b):
         o = cols("ebt", 512 * b, 512)
         op("g", lambda: g.affine_select(V(o), T.ones[:], [[-1, 512]], OP.is_equal, 0.0, b, 4), [o], [R("ones")], 200, 2)
-    for b in range(3):
+    for b in range(4):
         unit_tile(b)
 
     now = {}
+
+    TAB = cols("tab", 0, 8 * C)
 
     def OF(k):
         return now.get(k) or R("of", S_(96 * k + 31, 96 * k + 96, 32))
@@ -442,51 +448,51 @@ def rank_program(g, core, T, topo):
         for s in range(3):
             cp(q, cols("wk", 256 * s + k, 8 - k), cols("lab", 8 * s + k, 8 - k))
 
-    ts(cols("dm", 0, 96), cols("im", 0, 96), cf(I), None, OP.is_equal)
-    ts(R("la", S_(13, 18, 2)), R("la", S_(7, 12, 2)), cf(HI), 1.0, OP.subtract, OP.add)
+    ts(cols("dm", 0, 128), cols("im", 0, 128), cf(I), None, OP.is_equal)
+    ts(cols("la", 6, 6), cols("la", 0, 6), 1.0, None, OP.add)
+    ts(R("la", S_(12, 18, 2)), R("la", S_(0, 6, 2)), 2.0, None, OP.add)
+    tt(R("lab"), R("lab"), R("olf"), OP.add)
+    gather("v", cols("tab", 16 * 182, 160), R("iw"), cols("pl", 182, 10))
     tt(OF(0), R("lab", S_(0, 24, 8)), cols("jb", 0, 3), OP.add)
     lay_labels("v", 1)
+    ts(R("la", S_(13, 18, 2)), R("la", S_(7, 12, 2)), cf(HI), 1.0, OP.subtract, OP.add)
     cp("v", U(0), OF(0))
-    gather("v", cols("tab", 16 * SHARE, 16 * (192 - SHARE)), R("iw"), cols("pl", SHARE, 192 - SHARE))
 
     def clean(q, k):
-        gather(q, cols("wa", 48 * k, 48), R("tab"), U(k))
+        gather(q, cols("tab", 8 * C + 48 * k, 48), TAB, U(k))
 
     def walk(r, first):
         for k in range(first, 7):
-            gather_tt(R("wk", S_(k + 9, 768, 16)), R("tab"), U(k), cols("dm", 0, 48), OP.mult)
+            gather_tt(R("wk", S_(k + 9, 768, 16)), TAB, U(k), cols("dm", 0, 48), OP.mult)
             clean("s", k)
-            pause()
+            upto("lab%d" % r)
             scan(cols("of", 96 * (k + 1), 96), cols("z32", 0, 96), R("wk", S_(k + 1, 768, 8)))
             now.pop(k + 1, None)
             mark("of%d%d" % (r, k + 1))
-            pause()
-            cp("v", U(k + 1), OF(k + 1))
-            pause()
-        clean("v", 7)
-        pause()
-
-    def place_offsets():
-        ts(R("inv"), R("pos"), 48.0, C + 0.25, OP.mult, OP.add)
+            if k < 6:
+                cp("v", U(k + 1), OF(k + 1))
 
     def by_group():
-        gather("v", cols("wo", 0, 192), R("wa"), cols("inv", 0, 12))
-        gather("s", cols("wo", 192, 192), R("wa"), cols("inv", 12, 12))
-        pause()
-        tr(R("wt"), R("wo"))
-        pause()
+        for s in range(3):
+            ts(cols("inv", 8 * s, 8), R("px", S_(40 * s + 4, 40 * s + 40, 5)), cols("of", 96 * 7 + 32 * s + 31, 1), None, OP.max)
+        op("v", lambda: g.vector.tensor_scalar(T.wo[:, 0:192], T.tab[:].indirect(T.inv[:, 0:12]), -192.0, None, OP.add),
+           [cols("wo", 0, 192)], [R("tab"), cols("inv", 0, 12)], 60, 1.56)
+        op("s", lambda: g.scalar.activation(T.wo[:, 192:384], T.tab[:].indirect(T.inv[:, 12:24]), IDENT, bias=-192.0),
+           [cols("wo", 192, 192)], [R("tab"), cols("inv", 12, 12)], 80, 1.56)
+        op("v", lambda: g.vector.transpose(T.wt[:], T.wo[:]), [R("wt")], [R("wo")], 0, 0.5)
 
     def score_offsets():
-        cp("v", R("eb"), R("wt", ANY, ANY, 0))
+        ts(R("eb"), R("wt", ANY, ANY, 0), 192.0, None, OP.add)
 
     def signs(r, needs):
         k = r % 2
-        stream((210, lambda: gather_tt(cols("oh", 0, 96), R("lab"), cols("la", 6 * k, 6), R("gca"), OP.is_equal), "", needs),
-               (210, lambda: gather_tt(cols("oh", 96, 96), R("lab"), cols("la", 6 * k + 6, 6), R("gca"), OP.is_equal)),
-               (192, lambda: tt(R("sg"), cols("oh", 0, 96), cols("oh", 96, 96), OP.subtract), "sg%d" % r))
+        stream((210, lambda: gather_tt(cols("oh", 0, 96), R("lab"), cols("la", 6 * k, 6), R("gc"), OP.is_equal), "", needs),
+               (210, lambda: gather_tt(cols("oh", 96, 96), R("lab"), cols("la", 6 * k + 6, 6), R("gc"), OP.is_equal), "oh%d" % r),
+               (192, lambda: tt(cols("sg", 0, 96), cols("oh", 0, 96), cols("oh", 96, 96), OP.subtract), "sg%d" % r),
+               (0, lambda: gather_tt(R("cx"), R("sg"), cols("lh", 16, 8), R("wx"), OP.mult), "cx%d" % r, ("lx",)))
 
     def coef(x, t):
-        return R("co", S_(4 * x + t, 96, 32))
+        return R("co", S_(((0, 0, 0, 1), (0, 2, 0, 3), (0, 4, 6, 7), (14, 15, 8, 9), (17, 18, 10, 11, 12))[x][t], 60, 20))
 
     def ahead(r, needs):
         k = r % 2
@@ -499,26 +505,23 @@ def rank_program(g, core, T, topo):
             return R("ofs", S_(192 * t + 96 * v + 31, 192 * t + 96 * v + 96, 32))
 
         def look(t):
-            return [(210, lambda: gather_tt(R("wks", S_(192 * t + 1, 192 * t + 192, 2)), R("tab"), cols("offs", 6 * t, 6), cols("dm", 0, 96), OP.mult)),
+            return [(210, lambda: gather_tt(R("wks", S_(192 * t + 1, 192 * t + 192, 2)), TAB, cols("offs", 6 * t, 6), cols("dm", 0, 96), OP.mult)),
                     (192, lambda: scan(cols("ofs", 192 * t, 192), R("z32"), cols("wks", 192 * t, 192)), "l%d%d" % (r, t))]
 
         def begin():
             tt(cols("df", 0, n), R("lab", S_(k + 1, 24, 2)), R("lab", S_(k, k + 2 * n, 2)), OP.subtract)
             if r:
-                gather("s", R("wks", S_(0, 1024, 32)), R("lab"), cols("lh", 12 + 2 * k, 2))
-            else:
-                for e, x in enumerate(FOLLOW):
-                    cp("s", R("wks", S_(96 * e, 96 * e + 96, 32)), R("lab", S_(x, 24, 8)))
+                gather("s", R("wks", S_(0, 1024, 32)), R("lab"), cols("lh", 4 + 2 * k, 2))
 
         def starts():
             for v in range(2):
                 tt(cols("a0", 3 * v, 3), OF(k + 2 * v), df(v), OP.add)
 
         def plain():
-            for q, (x, t) in enumerate(((0, 1), (2, 2), (4, 3))):
+            for q, (x, t) in enumerate(((0, 1), (2, 2), (4, 4))):
                 cp("s", coef(x, t), df(q))
             for x in range(5):
-                cp("s", coef(x + x // 4, 3 * (x < 4)), OF(k + x))
+                cp("s", coef(x, 3), OF(k + x))
 
         def second():
             cp("v", cols("offs", 12, 3), res(1, 0))
@@ -534,9 +537,9 @@ def rank_program(g, core, T, topo):
                (64, lambda: tt(coef(4, 0), cols("rr", 3, 3), coef(4, 2), OP.subtract), "a%d" % r, ("b%d" % r,)))
         stream((128, lambda: (less(1, 1, res(0, 0)), less(3, 2, res(0, 1))), "", ("l%d0" % r, "of%d%d" % (r - 1, k + 3))),
                (128, lambda: (less(2, 1, res(1, 0)), less(4, 2, res(1, 1))), "", ("l%d1" % r, "of%d%d" % (r - 1, k + 4))),
-               (0, plain, "", ("sent%d" % (r - 1),)),
                (128, lambda: (less(3, 1, res(2, 0)), tt(cols("rr", 0, 3), res(2, 1), res(2, 0), OP.subtract)), "", ("l%d2" % r,)),
                (64, lambda: tt(coef(3, 0), cols("rr", 0, 3), coef(3, 2), OP.subtract), "b%d" % r))
+        stream((0, plain, "plain%d" % r, ("sent%d" % (r - 1), "begun%d" % r, "of%d%d" % (r - 1, k + 4))))
 
     def scores(r, a, n, q, k):
         mm(k, R("uc"), R("upl"), *q_of(r, a, n), n)
@@ -555,7 +558,6 @@ def rank_program(g, core, T, topo):
     def first_state():
         quant(*q_of(0), R("xb"))
         send_state(0)
-        unit_tile(3)
         dmas("d_v", [("y", T.vb16[:], T.v[:], [R("vb16")], [R("xb")])])
         dmas("d_w", [("y", T.wcod[:].bitcast(dt.uint8), T.wc[:], [R("wcod")], []), ("y", T.wpl[:], T.ws[:], [R("wpl")], [])])
 
@@ -568,37 +570,57 @@ def rank_program(g, core, T, topo):
                 (0, lambda: scan(cols("bs", a, n), cols("z16", 0, n), cols("ys", a, n))),
                 (0, lambda: cp("v", cols("lh", a // 16, n // 16), R("bs", S_(a + 15, a + n, 16))), name)]
 
-    def factors(a):
-        for s in range(3):
-            if a == 0:
-                fill_s(R("bg", S_(32 * s, 32 * s + 20, 4)), 12)
-                fill_s(R("bg", S_(32 * s + 1, 32 * s + 20, 4)), 4 * s + 1)
-                fill_s(R("bg", S_(32 * s + 2, 32 * s + 20, 4)), 4 * s)
-            else:
-                fill_s(R("bg", S_(32 * s + 98, 32 * s + 116, 4)), 4 * s + 1)
-                fill_s(cols("bg", 32 * s + 115, 1), 4 * s + 2)
+    def factors(s):
+        for a, b, step, q in ((1, 6, 2, 0), (16, 20, 3, 0), (7, 12, 2, 1), (15, 19, 3, 1), (13, 14, 1, 2)):
+            fill_s(R("bg", S_(20 * s + a, 20 * s + b, step)), 32 * s + 8 * q + 7)
 
     def followers():
         for e, x in enumerate(FOLLOW):
-            affine(cols("bg", 192 + 3 * e, 3), R("cb", S_(0, 12, 4)), 1.0, float(x))
-        fill_s(cols("bg", 216, 8), 0.0)
+            affine(cols("bg", 64 + 3 * e, 3), R("cb", S_(0, 12, 4)), 1.0, float(x))
+        fill_s(cols("bg", 88, 8), 0.0)
     mark("sent-1")
-    ahead(0, ("of-12", "co"))
-    stream(*[(160, lambda s=s: gather_tt(cols("eq", 64 * s, 64), R("lab"), cols("lb", 4 * s, 4), R("gcb"), OP.is_equal)) for s in range(3)],
-           (192, lambda: scan(R("iv"), R("wgt"), R("eq"))),
-           (0, lambda: ts(cols("ci", 0, 3), cols("cj", 0, 3), cf(I), 1.0 / 48, OP.add, OP.mult)),
-           (0, lambda: [affine(cols("pos", 8 * s, 8), R("iv", S_(64 * s + 7, 64 * s + 64, 8)), -1.0, cols("ci", s, 1)) for s in range(3)]),
-           (64, place_offsets, "inv-1"))
-    stream((150, lambda: quant(R("uq0"), R("up0"), R("ub"))), (420, first_state), (260, scoring_columns), (0, first_scores, "s0"))
-    stream((0, lambda: (fill_s(R("co"), 0.0), fill_s(cols("bg", 0, 192), 13), fill_s(R("z8"), 1.0), fill_s(cols("d", 12, 4), 0.0)), "co"),
-           (0, lambda: fill_s(cols("z16", 0, C), 1.0), "", ("begun0",)), (0, lambda: factors(0)), (0, lambda: factors(1)),
-           (0, lambda: (fill_s(R("z16", S_(0, C, 16)), 0.0), fill_s(R("z8", S_(0, 96, 8)), 0.0), fill_s(cols("d", 13, 1), 1.0), affine(c1(1), cf(M7), 17.0))),
-           (0, lambda: ts(R("le"), cols("ce", 0, 6), c1(1), None, OP.add), "le"), *lists_of(0, 96, ""), *lists_of(96, 96, "lh"), (0, followers),
-           (0, lambda: (affine(cols("bg", 224, 32), cols("bg", 192, 32), 1.0, 1.0), affine(c1(3), cf(G), float(C)),
-                        fill_s(cols("mv", 96, 16), 0.0), fill_s(cols("olf", 24, 8), 0.0))), *lists_of(192, 64, "lf"))
+    mark("lab-1")
+    affine(R("wgt"), R("wgt"), 1.0, cf(I))
+    ahead(0, ("of-12",))
     signs(0, ())
-    stream(*[(150, lambda b=b: quant(cols("ec", 128 * b, 128), cols("ep", 128 * b, 128), cols("ebt", 512 * b, 512)), "e%d" % b, ("s0", "inv-1")) for b in range(4)],
-           (0, lambda: ts(cols("dm", 96, C - 96), cols("im", 96, C - 96), cf(I), None, OP.is_equal), "dm"))
+    stream(*[(0, lambda h=h: gather_tt(cols("eq", 96 * h, 96), R("oh"), cols("lb", 6 * h, 6), cols("wgt", 96 * h, 96), OP.mult), "", ("oh0",)) for h in range(2)],
+           (0, lambda: scan(R("iv"), R("z8"), R("eq")), "iv"),
+           (0, lambda: (cp("v", R("px", S_(4, 120, 5)), R("iv", S_(7, 192, 8))), cp("s", cols("d", 12, 24), R("iv", S_(7, 192, 8)))), "inv-1"))
+    mark("px-1")
+
+    def move_lists():
+        affine(c1(9), cf(I), -1.0)
+        affine(R("bg", S_(132, 248, 5)), cols("iw", 0, 24), 1.0, 12.0)
+        fill_s(R("bg", S_(260, 376, 5)), 96)
+        fill_s(R("wx", S_(4, 120, 5)), 1.0)
+        fill_s(R("z5", S_(0, 128, 5)), 0.0)
+        for s in range(3):
+            affine(R("wx", S_(40 * s + 3, 40 * s + 40, 5)), cols("ones", 0, 8), c1(9), -(8.0 * C + 6 * 48 + 16 * s))
+    stream((150, lambda: quant(R("uq0"), R("up0"), R("ub")), "uq"), (420, first_state, "q0"), (260, scoring_columns, "uc"), (0, first_scores, "s0"))
+    for e, x in enumerate(FOLLOW):
+        cp("s", R("wks", S_(96 * e, 96 * e + 96, 32)), R("lab", S_(x, 24, 8)))
+    for name, a, n, c in (("co", 0, 64, 0), ("bg", 0, 64, 96), ("z16", 0, C, 1), ("wx", 0, 128, 48), ("z5", 0, 128, 1), ("bg", 248, 8, 0), ("bg", 376, 8, 0)):
+        fill_s(cols(name, a, n), c)
+    fill_s(R("wgt", S_(7, 192, 8)), 0.0)
+    for s in range(3):
+        factors(s)
+    followers()
+    fill_s(R("z16", S_(0, C, 16)), 0.0)
+    move_lists()
+    affine(cols("bg", 96, 32), cols("bg", 64, 32), 1.0, 1.0)
+    for name, a, n, c in (("es", 96, 16, 0), ("sg", 96, 16, 1)):
+        fill_s(cols(name, a, n), c)
+    affine(c1(1), cf(M7), 17.0)
+    stream((0, lambda: ts(R("le"), cols("ce", 0, 6), c1(1), None, OP.add), "le"), *lists_of(0, 128, "lh"))
+    stream(*lists_of(256, 128, "lx"))
+    stream(*lists_of(128, 128, "l1"))
+    mark("lf")
+    stream((0, lambda: ts(cols("dm", 128, C - 128), cols("im", 128, C - 128), cf(I), None, OP.is_equal), "dm"),
+           *[(150, lambda b=b: quant(cols("ec", 128 * b, 128), cols("ep", 128 * b, 128), cols("ebt", 512 * b, 512)), "e%d" % b, ("lx",)) for b in range(4)])
+    cuts = [SHARE + 2 * ((182 - SHARE) * x // (2 * len(EARLY))) for x in range(len(EARLY))] + [182]
+    for x, names in enumerate(EARLY):
+        upto(*names)
+        gather("v", cols("tab", 16 * cuts[x], 16 * (cuts[x + 1] - cuts[x])), R("iw"), cols("pl", cuts[x], cuts[x + 1] - cuts[x]))
     walk(-1, 0)
     upto("inv-1")
     by_group()
@@ -620,46 +642,53 @@ def rank_program(g, core, T, topo):
         tr(R("et"), R("ef"))
         pause()
         upto("sg%d" % r, "le")
-        gather_tt(R("sel"), R("et"), R("le"), R("sg"), OP.mult)
+        gather_tt(R("sel"), R("et"), R("le"), cols("sg", 0, 96), OP.mult)
         pause()
-        scan(R("es"), R("z8"), R("sel"))
-        pause()
-        ts(cols("d", 0, 12), R("es", S_(7, 96, 8)), 0.0, None, OP.is_gt)
-        upto("a%d" % r, "lh")
+        scan(cols("es", 0, 96), cols("z8", 0, 96), R("sel"))
+        upto("a%d" % r, "plain%d" % r, "lh")
         m = cols("m", 0, n)
-        gather_tt(R("hv"), R("d"), cols("lh", 6, 6), R("co"), OP.mult)
-        gather("s", R("hz"), R("d"), cols("lh", 0, 6))
+        op("v", lambda: g.vector.tensor_scalar(T.hz[:], T.es[:].indirect(T.lh[:, 0:4]), 0.0, None, OP.is_gt), [R("hz")], [R("es"), cols("lh", 0, 4)], 60, 1.56)
+        upto("px%d" % (r - 1))
+        ts(cols("d", 0, 12), R("es", S_(7, 96, 8)), 0.0, None, OP.is_gt)
+        scan(cols("hs", 64 * r, 64), R("hz"), R("co"))
         tt(m, cols("d", 0, n), cols("df", 0, n), OP.mult)
-        scan(cols("hs", 96 * r, 96), R("hz"), R("hv"))
+
+        def term(t, s=None, r=r):
+            return R("hs", S_(64 * r + t, 64 * r + 60, 20)) if s is None else cols("hs", 64 * r + 20 * s + t, 1)
+        for s in range(3):
+            ts(cols("offu", 4 * (k + 4) + s, 1), term(19, s), term(11, s), term(13, s), OP.add, OP.add)
         tt(R("wk", S_(k + 5, 768, 256)), R("lab", S_(k + 5, 24, 8)), R("m", S_(2, n, 4)), OP.subtract)
         tt(R("lab", S_(k, k + 2 * n, 2)), R("lab", S_(k, k + 2 * n, 2)), m, OP.add)
+        now.update({k: term(1), k + 1: term(3)})
+        now.update({k + x: cols("os", 12 * r + 3 * (x - 2), 3) for x in (2, 3, 4)})
 
-        for x in range(5):
-            now[k + x] = R("hs", S_(96 * r + 4 * x + 3 + 4 * (x // 4), 96 * r + 96, 32))
-        cp("v", U(k + 4), OF(k + 4))
-        tt(R("lab", S_(k + 1, 24, 2)), R("lab", S_(k + 1, 24, 2)), m, OP.subtract)
-        cp("v", U(k), OF(k))
-        cp("v", U(k + 1), OF(k + 1))
-        lay_labels("s", k + 6)
+        def labels(k=k, m=m):
+            tt(R("lab", S_(k + 1, 24, 2)), R("lab", S_(k + 1, 24, 2)), m, OP.subtract)
+            lay_labels("s", k + 6)
 
-        def kept(k=k):
-            for x in (2, 3):
-                cp("v", U(k + x), OF(k + x))
-            for x in range(4):
-                clean("s", k + x)
-        stream((210, lambda: gather_tt(cols("mv", 0, 96), R("d"), R("ld"), R("sg"), OP.mult), "mv%d" % r),
-               (0, lambda: None, "", ("lf",)),
-               (192, lambda: tt(R("h1"), cols("mv", 0, 96), cols("mv", 16, 96), OP.add)),
-               (64, lambda: tt(R("h2"), R("h1", ANY, S_(0, 8)), R("h1", ANY, S_(8, 16)), OP.add)),
-               (64, lambda: tt(R("pos"), R("pos"), R("h2"), OP.add)), (64, place_offsets, "inv%d" % r))
-        stream((128, kept, "kept%d" % r, ("mv%d" % r,)))
+        def sums(k=k, term=term):
+            tt(OF(k + 2), term(5), term(7), OP.add)
+            tt(OF(k + 3), term(16), term(9), OP.add)
+
+        def kept(k, x):
+            for y in (x, x + 1):
+                cp("v", U(k + y), OF(k + y))
+            for y in (x, x + 1):
+                clean("s", k + y)
+        stream((0, lambda: gather_tt(R("mv"), R("d"), cols("lh", 8, 8), R("cx"), OP.mult), "mv%d" % r, ("cx%d" % r, "l1")),
+               (0, lambda: scan(R("px"), R("z5"), R("mv")), "inv%d" % r),
+               (0, lambda: cp("s", cols("d", 12, 24), R("px", S_(4, 120, 5))), "px%d" % r, ("kept%d" % r,)), first=True)
+        stream((0, labels, "lab%d" % r), (0, sums), (0, lambda k=k: kept(k, 0)), (0, lambda k=k: kept(k, 2)),
+               (0, lambda k=k: cp("v", OF(k + 4), U(k + 4)), "kept%d" % r), first=True)
         for x in range(k + 5):
             mark("of%d%d" % (r, x))
         if r < 2:
             ahead(r + 1, ("kept%d" % r, "lf"))
-            signs(r + 1, ("mv%d" % r,))
+            signs(r + 1, ("mv%d" % r, "lab%d" % r))
         else:
-            stream((0, lambda: [affine(R("olf", S_(s, 24, 3)), cols("lab", 8 * s, 8), 1.0 / C) for s in range(3)], "", ("own2",)), (0, lambda: None),
+            stream((0, lambda: ts(R("pa"), cols("lab", 0, 24), 1.0 / C, cf(G), OP.mult, OP.add), "", ("kept2",)),
+                   (0, lambda: ts(R("pe"), R("pa"), 8.0, -8.0, OP.is_ge, OP.mult)),
+                   (0, lambda: [tt(R("olf", S_(s, 24, 3)), cols("pa", 8 * s, 8), cols("pe", 8 * s, 8), OP.add) for s in range(3)]),
                    (64, lambda: tr(R("olt"), R("olf"))),
                    (0, lambda: dmas("d_ol", [("y", T.ol[:, 96 * a:96 * a + 96], T.olt[32 * a:32 * a + 24, :], [], [R("olt")]) for a in range(4)])),
                    (150, lambda: quant(R("vq"), R("vp"), R("vb16")), "v"))
@@ -670,18 +699,20 @@ def rank_program(g, core, T, topo):
             for c in range(4):
                 cp("vs"[c % 2], R("lf", S_(6 * a, 6 * a + 6), p=quadrant(c)), R("wt", ANY, S_(2 * c, 2 * c + 2), 0, p=quadrant(a)))
         pause()
-        cp("v", R("al%d" % r), R("lf"))
+        ts(R("al%d" % r), R("lf"), 192.0, None, OP.add)
         remote(r, T["zl%d" % r][:], T["al%d" % r][:], "ra%d" % r, [R("al%d" % r)])
-        for b in (0, 2, 3):
+        for b in range(4) if DPS else (0, 2, 3):
             frombank("s", cols("dp", C * b, C), (2, 3, 0, 1)[b])
         mark("sent%d" % r)
-        ts(R("ab"), R("lf"), c1(3), None, OP.add)
+        if r < 2:
+            upto("plain%d" % (r + 1))
         if r < 2:
             score_offsets()
         pause()
-        gather_tt(R("bg"), R("tab"), R("ab"), R("dm"), OP.mult)
+        gather_tt(R("bg"), TAB, R("al%d" % r), R("dm"), OP.mult)
         pause()
-        frombank("v", cols("dp", C, C), 3)
+        if not DPS:
+            frombank("v", cols("dp", C, C), 3)
         pause()
         zt, zc, zp, zl = "zt%d" % r, "zc%d" % r, "zp%d" % r, "zl%d" % r
 
@@ -729,7 +760,7 @@ def rank_program(g, core, T, topo):
             op("v", lambda: g.vector.tensor_tensor(V(o), V(i), bank(4 + b, w, a), OP.add), [o], [i, ("ps", 4 + b)])
         for b, kb in ((0, 4), (2, 5), (1, 0), (3, 1)):
             layer(1, b, kb)
-            products("vs"[b // 2], 1, b, kb)
+            products(RQ[b], 1, b, kb)
             if b == 0:
                 cp("v", R("bl"), R("bs", S_(15, C, 16)))
         for h in range(2):

import numpy as np
from concourse.mybir import dt, AluOpType, ActivationFunctionType

C = 384
STEP = [2, 3, 1]
ZP = [(0, 224), (224, 160)]
XP = [(0, 256), (256, 128)]
SHARE = 138
WAKE = 240
SROOM = 0
EARLY = [["oh0"]]
DPS = 1
RQ = "vvss"
FOLLOW = (0, 2, 2, 4, 3, 2, 4, 4)
SLACK = 40
LANDS = {"d_l": 2200, "d_x": 4500, "d_u": 3500, "d_w": 4500, "d_v": 3500, "d_o": 0, "d_s": 0, "d_y": 0, "ra": 1300, "rq": 5500}
OP = AluOpType
COPY, IDENT = ActivationFunctionType.Copy, ActivationFunctionType.Identity
F32, BF, I32, U16, X4, U8 = "float32", "bfloat16", "int32", "uint16", "float8_e4m3fn_x4", "uint8"
SMALL = {}
for _n, _w in (("cj", 12), ("cz", 12), ("ca", 12), ("ce", 12), ("cb", 12), ("jb", 4), ("ci", 4), ("cf", 8), ("cst", 12), ("t1", 12),
               ("df", 12), ("m", 12), ("a0", 8), ("rr", 8), ("pos", 24), ("pa", 24), ("pe", 24), ("os", 36)):
    SMALL[_n] = (sum(k[1] for k in SMALL.values()), _w)


def _scratch():
    s = {}

    def sb(name, shape, d):
        s[name] = ("sbuf", [128] + shape, d)
    sb("li", [96], I32); sb("rt", [208], F32); sb("pl", [192], U16); sb("pidx", [1], I32); sb("ti", [12], I32)
    sb("sm", [sum(k[1] for k in SMALL.values())], F32)
    sb("lb", [12], U16); sb("la", [18], U16); sb("le", [6], U16); sb("lh", [24], U16)
    sb("lo", [2], U16); sb("lu", [8], U16); sb("d", [36], F32)
    sb("sg", [112], F32); sb("mv", [128], F32); sb("cx", [128], F32); sb("wx", [128], F32); sb("px", [128], F32); sb("z5", [128], BF)
    sb("co", [64], F32); sb("hz", [64], F32); sb("hs", [3 * 64], F32)
    sb("iw", [C], F32); sb("im", [C], BF); sb("dm", [C], BF); sb("gc", [96], F32)
    sb("z32", [192], BF); sb("z16", [C], BF); sb("z8", [192], BF); sb("wgt", [192], F32)
    sb("ones", [512], BF); sb("ebt", [2048], BF); sb("ec", [512], X4); sb("ep", [512], U8)
    sb("xb", [4 * C], BF); sb("ub", [512], BF); sb("vb16", [512], BF)
    sb("uq0", [128], X4); sb("up0", [128], U8); sb("uc", [128], X4); sb("upl", [128], U8)
    sb("vq", [128], X4); sb("vp", [128], U8); sb("wcod", [512], X4); sb("wpl", [512], U8)
    sb("tab", [8 * C + 7 * 48], F32); sb("sct", [C], F32)
    for r in range(4):
        sb("qc%d" % r, [C], X4); sb("qp%d" % r, [C], U8)
        if r:
            sb("xs%d" % r, [4 * C], BF)
    for r in range(3):
        sb("lc%d" % r, [C], X4); sb("lp%d" % r, [C], U8); sb("zl%d" % r, [24], U16); sb("al%d" % r, [24], U16)
        sb("zc%d" % r, [C], X4); sb("zp%d" % r, [C], U8); sb("zt%d" % r, [4 * C], BF)
    sb("fb", [2 * C], BF); sb("dp", [4 * C], BF); sb("rs", [4 * C], F32); sb("gs", [2 * C], F32)
    sb("lab", [32], F32); sb("wk", [768], F32); sb("of", [8 * 96], F32); sb("offu", [32], U16)
    sb("wks", [1024], F32); sb("ofs", [768], F32); sb("offs", [24], U16)
    sb("wo", [C], BF); sb("wt", [3, 8, 16], BF); sb("lf", [24], F32)
    sb("eq", [192], F32); sb("iv", [192], F32); sb("inv", [24], U16); sb("oh", [192], F32)
    sb("eb", [24], U16); sb("ef", [C], F32); sb("et", [C], F32); sb("sel", [96], F32); sb("es", [112], F32)
    sb("bg", [C], F32); sb("bs", [C], F32); sb("bl", [24], U16)
    sb("olf", [32], F32); sb("olt", [32], F32); sb("ys", [C], F32)
    s["ps"] = ("psum", [128, 4096], F32)
    return s


SCRATCH = _scratch()
SEMAPHORES = (["qv", "qs", "qt", "qg", "loc", "d_l", "d_x", "d_u", "d_w", "d_v", "d_o0", "d_o1", "d_s", "d_ol", "d_y0", "d_y1"]
              + ["rq%d" % r for r in range(3)] + ["ra%d" % r for r in range(3)])


def make_queue_tools(g, T):
    eng = {"v": g.vector, "s": g.scalar, "t": g.tensor, "g": g, "y": g.sync}
    own = {"v": "qv", "s": "qs", "t": "qt", "g": "qg"}
    count = {k: 0 for k in SEMAPHORES}
    known = {k: {} for k in eng}
    clock = {}
    hist = {}
    bits = {}

    def region(ref):
        name, idx = ref
        key = (name, str(idx))
        if key not in bits:
            if name == "ps":
                bits[key] = (0, 128, 1 << idx)
            else:
                shape = SCRATCH[name][1][1:]
                n = 1
                for k in shape:
                    n *= k
                a = np.arange(n).reshape(shape)
                sel = np.zeros(n, np.uint8)
                sel[a[idx[1:]].reshape(-1)] = 1
                m = int.from_bytes(np.packbits(sel, bitorder="little").tobytes(), "little")
                bits[key] = (idx[0].start or 0, idx[0].stop or 128, m)
        return bits[key]

    def learn(q, ev):
        k = known[q]
        for s, n in clock[ev].items():
            if k.get(s, 0) < n:
                k[s] = n

    def need(q, events):
        todo = [e for e in set(events) if known[q].get(e[0], 0) < e[1]]
        todo = [e for e in todo if not any(f != e and clock[f].get(e[0], 0) >= e[1] for f in todo)]
        for e in sorted(todo):
            if known[q].get(e[0], 0) < e[1]:
                eng[q].wait_ge(T.sem[e[0]], e[1])
                learn(q, e)

    def deps(q, ins, outs):
        ev = []
        for refs, write in ((ins, False), (outs, True)):
            for ref in refs:
                p0, p1, m = region(ref)
                for (h0, h1, hm, hw, hq, he) in hist.get(ref[0], ()):
                    if (hw or write or ref[0] == "ps" and hq != q) and h0 < p1 and p0 < h1 and hm & m:
                        ev.append(he)
        return ev

    def note(q, ev, ins, outs):
        for refs, write in ((ins, False), (outs, True)):
            for ref in refs:
                p0, p1, m = region(ref)
                lst = hist.setdefault(ref[0], [])
                if write:
                    lst[:] = [h for h in lst if not (p0 <= h[0] and h[1] <= p1 and (h[2] & ~m) == 0)]
                lst.append((p0, p1, m, write, q, ev))

    free = {k: 0.0 for k in eng}
    fin = {}
    streams, done, mode, probe = [], set(), ["chain"], [0.0, 0.0, 0.0]

    def ready(ev):
        return max([fin.get(e, 0.0) + WAKE for e in ev] + [0.0])

    def run(st):
        call, name, _ = st.pop(0)
        was, mode[0] = mode[0], "step"
        call()
        mode[0] = was
        done.add(name)

    def fill(until):
        return fill1(until, 10) or fill1(until, 80) or fill1(until, 1000)

    def fill1(until, most):
        for st in streams:
            if st and done.issuperset(st[0][2]):
                mode[0], probe[0], probe[1], probe[2] = "probe", 0.0, 0.0, 0.0
                st[0][0]()
                mode[0] = "chain"
                late, cycles = max(probe[0] - free["v"], 0), probe[1]
                room = until - free["v"]
                if probe[2] > until + SROOM or cycles and late > most:
                    continue
                if cycles == 0 or late + cycles <= room + SLACK or late <= SLACK and cycles > WAKE and room >= WAKE - SLACK:
                    run(st)
                    return True
        return False

    def stream(*steps, first=False):
        streams.insert(0 if first else len(streams), [s[1:] + ("", ())[len(s) - 2:] for s in steps])

    def upto(*names):
        for name in names:
            while name not in done:
                st = [s for s in streams if any(x[1] == name for x in s)][0]
                upto(*st[0][2])
                run(st)

    def op(q, call, outs, ins, fixed=0, each=1.0):
        n = bin(region(ins[-1] if outs[0][0] == "ps" else outs[0])[2]).count("1")
        cycles = fixed + each * n if fixed else max(64, each * n)
        if mode[0] == "probe":
            if q == "v":
                probe[0] = max(probe[0], ready(deps(q, ins, outs)) - probe[1])
                probe[1] += cycles
            elif q == "s":
                probe[2] = probe[2] or max(free["s"], ready(deps(q, ins, outs)))
            return
        if q == "v" and mode[0] == "chain":
            while fill(ready(deps(q, ins, outs))):
                pass
        before = deps(q, ins, outs)
        need(q, before)
        sem = own[q]
        count[sem] += 1
        ev = (sem, count[sem])
        call().then_inc(T.sem[sem], 1)
        clock[ev] = dict(known[q])
        clock[ev][sem] = count[sem]
        free[q] = fin[ev] = max(free[q], ready(before)) + cycles
        note(q, ev, ins, outs)

    def dmas(sem, items):
        if mode[0] == "probe":
            return
        count[sem] += 16 * len(items)
        ev = (sem, count[sem])
        clock[ev] = {sem: count[sem]}
        for q, out, in_, outs, ins in items:
            before = [e for e in deps(q, ins, outs) if e != ev]
            need(q, before)
            eng[q].dma_start(out, in_).then_inc(T.sem[sem], 16)
            free[q] = max(free[q], ready(before)) + 64
            fin[ev] = free[q] + LANDS[sem[:3]]
            for s, n in known[q].items():
                if clock[ev].get(s, 0) < n:
                    clock[ev][s] = n
        for q, out, in_, outs, ins in items:
            note("dma", ev, ins, outs)

    def send(call, ins, n, sem):
        if mode[0] == "probe":
            return
        before = deps("g", ins, [])
        need("g", before)
        call()
        free["g"] = max(free["g"], ready(before)) + 300
        fin[(sem, count[sem])] = free["g"] + LANDS[sem[:2]]
        count["loc"] += n
        clock[("loc", count["loc"])] = {"loc": count["loc"]}

    def arrives(sem, n, outs):
        count[sem] += n
        ev = (sem, count[sem])
        clock[ev] = {sem: count[sem]}
        note("remote", ev, [], outs)

    def finish():
        for s in SEMAPHORES:
            if count[s] and known["g"].get(s, 0) < count[s]:
                g.wait_ge(T.sem[s], count[s])
    return op, dmas, send, arrives, finish, stream, upto, done.add


def rank_program(g, core, T, topo):
    rank = T.rank_of(core)
    if rank is None:
        return
    op, dmas, send, arrives, finish, stream, upto, mark = make_queue_tools(g, T)
    S_ = slice
    ROOM = 0

    def pause(k=0):
        pass
    ANY = slice(None)

    def R(name, *idx, p=slice(0, 128)):
        if name in SMALL:
            o, n = SMALL[name]
            i = idx[0] if idx else slice(0, n)
            name, idx = "sm", (slice(o + i.start, o + i.stop, i.step),)
        return (name, (p,) + tuple(idx)) if idx else (name, (p,) + tuple(ANY for _ in SCRATCH[name][1][1:]))

    def V(ref):
        return T[ref[0]][ref[1]]

    def bank(k, n, a=0):
        return T.ps[:, 512 * k + a:512 * k + a + n]

    def cp(q, out, in_):
        if q == "v":
            op(q, lambda: g.vector.tensor_copy(V(out), V(in_)), [out], [in_])
        else:
            op(q, lambda: g.scalar.activation(V(out), V(in_), COPY), [out], [in_])

    def frombank(q, out, k, n=C, scale=None):
        if q == "v" and scale is None:
            op(q, lambda: g.vector.tensor_copy(V(out), bank(k, n)), [out], [("ps", k)])
        elif q == "v":
            op(q, lambda: g.vector.tensor_scalar(V(out), bank(k, n), scale, None, OP.mult), [out], [("ps", k)])
        elif scale is None:
            op(q, lambda: g.scalar.activation(V(out), bank(k, n), COPY), [out], [("ps", k)])
        else:
            op(q, lambda: g.scalar.activation(V(out), bank(k, n), COPY, scale=scale), [out], [("ps", k)])

    def gather(q, out, win, off):
        if q == "v":
            op(q, lambda: g.vector.tensor_copy(V(out), V(win).indirect(V(off))), [out], [win, off], 60, 1.56)
        else:
            op(q, lambda: g.scalar.activation(V(out), V(win).indirect(V(off)), COPY), [out], [win, off], 80, 1.56)

    def gather_tt(out, win, off, in1, o):
        op("v", lambda: g.vector.tensor_tensor(V(out), V(win).indirect(V(off)), V(in1), o), [out], [win, off, in1], 60, 1.56)

    def tt(out, a, b, o):
        op("v", lambda: g.vector.tensor_tensor(V(out), V(a), V(b), o), [out], [a, b], 0, 2)

    def ts(out, a, s1, s2, o0, o1=None):
        v1 = V(s1) if isinstance(s1, tuple) else s1
        v2 = V(s2) if isinstance(s2, tuple) else s2
        ins = [a] + [s for s in (s1, s2) if isinstance(s, tuple)]
        if o1 is None:
            op("v", lambda: g.vector.tensor_scalar(V(out), V(a), v1, None, o0), [out], ins)
        else:
            op("v", lambda: g.vector.tensor_scalar(V(out), V(a), v1, v2, o0, o1), [out], ins)

    def tr(out, in_):
        op("v", lambda: g.vector.transpose(V(out), V(in_)), [out], [in_])

    def scan(out, keep, in_):
        op("v", lambda: g.vector.tensor_tensor_scan(V(out), V(keep), V(in_), 0.0, OP.mult, OP.add), [out], [keep, in_])

    def ms(out, c):
        op("v", lambda: g.vector.memset(V(out), c), [out], [])

    def affine(out, in_, scale, bias=0.0):
        ins = [in_] + [s for s in (scale, bias) if isinstance(s, tuple)]
        op("s", lambda: g.scalar.activation(V(out), V(in_), IDENT, bias=V(bias) if isinstance(bias, tuple) else bias,
                                            scale=V(scale) if isinstance(scale, tuple) else scale), [out], ins)

    def fill_s(out, c):
        i = out[1][1]
        affine(out, R("ones", S_(0, len(range(i.start or 0, i.stop or SCRATCH[out[0]][1][1], i.step or 1)))), float(c))

    def quant(oc_, op_, in_):
        op("v", lambda: g.vector.quantize_mx(V(oc_), V(op_), V(in_)), [oc_, op_], [in_], 15, 1.06)

    def mm(k, lc, lp, rc, rp, n=C):
        op("t", lambda: g.tensor.matmul_mx(bank(k, n), V(lc), V(lp), V(rc), V(rp), True, True), [("ps", k)], [lc, lp, rc, rp], 12, 0.75)

    def iota(out, pattern, base, cm):
        if SCRATCH[out[0]][2] == I32:
            op("g", lambda: g.iota(V(out), pattern, base, cm), [out], [], 160, 2)
        else:
            op("g", lambda: g.iota(V(out), pattern, base, cm, allow_small_or_imprecise_dtypes=True), [out], [], 160, 2)

    def quadrant(a):
        return slice(32 * a, 32 * a + 32)

    def cols(name, a, n):
        return R(name, S_(a, a + n))

    def partner(r):
        return T.cores[rank ^ STEP[r]]

    def remote(r, out, in_, sem, ins):
        rid, pid, _ = topo.addr(partner(r))
        send(lambda: g.remote_dma(out, in_, T.sem[sem], T.sem.loc, pid, rid, topo.mask(core, partner(r))), ins,
             len(topo.engines(core, partner(r))), sem)

    def q_of(r, a=0, n=C):
        return cols("qc%d" % r, a, n), cols("qp%d" % r, a, n)

    def send_state(r):
        remote(r, T["lc%d" % r][:].bitcast(dt.uint8), T["qc%d" % r][:].bitcast(dt.uint8), "rq%d" % r, [R("qc%d" % r)])
        remote(r, T["lp%d" % r][:], T["qp%d" % r][:], "rq%d" % r, [R("qp%d" % r)])

    for r in range(3):
        n = len(topo.engines(partner(r), core))
        arrives("rq%d" % r, 2 * n, [R("lc%d" % r), R("lp%d" % r)])
        arrives("ra%d" % r, n, [R("zl%d" % r)])

    items = []
    for q, src, a in (("y", T.pg, 0), ("s", T.og, 48)):
        items.append((q, T.li[:, a:a + 24], src[:], [cols("li", a, 24)], []))
        items.append((q, T.li[0:112, 24 + a:48 + a], src[16:128, :], [cols("li", 24 + a, 24)], []))
        items.append((q, T.li[112:128, 24 + a:48 + a], src[0:16, :], [], []))
    dmas("d_l", items)
    dmas("d_x", [("y", T.xb[:], T.x[:], [R("xb")], [])])
    dmas("d_u", [("s", T.ub[:], T.u[:], [R("ub")], [])])

    def ti(k):
        return cols("ti", k, 1)

    def cf(k):
        return cols("cf", k, 1)

    def c1(k):
        return cols("cst", k, 1)
    iota(R("pidx"), [[0, 1]], 0, 1)
    iota(R("ca"), [[2, 12]], 0, 0)
    iota(R("gc"), [[0, 12], [1, 8]], 0, 0)
    iota(R("cj"), [[32, 3], [2, 4]], 0, 0)
    iota(cols("jb", 0, 3), [[32, 3]], 0, 1)
    iota(R("cb"), [[8, 3], [0, 4]], 0, 0)
    iota(R("iw"), [[1, C]], 0, 0)
    iota(R("im"), [[0, 24], [1, 16]], 0, 0)
    iota(R("wgt"), [[16, 3], [0, 8], [48, 8]], 8 * C, 0)
    iota(cols("ce", 0, 6), [[128, 3], [0, 2]], 0, 0)
    iota(cols("bg", 128, 120), [[4, 3], [0, 8], [1, 5]], 0, 0)
    iota(cols("bg", 256, 120), [[32, 3], [1, 8], [8, 5]], 0, 0)
    ms(R("ones"), 1.0)
    for name, a, n in (("rt", 192, 16), ("wk", 0, C), ("wk", C, C), ("wks", 0, C), ("wks", C, C)):
        fill_s(cols(name, a, n), 0.0)
    fill_s(R("z32"), 1.0)
    fill_s(R("z8"), 1.0)
    fill_s(R("z32", S_(0, 192, 32)), 0.0)
    fill_s(R("z8", S_(0, 192, 8)), 0.0)
    I, M7, HI, G, A = range(5)
    ts(ti(I), R("pidx"), 15, None, OP.bitwise_and)
    ts(ti(G), R("pidx"), 4, None, OP.arith_shift_right)
    ts(ti(M7), R("pidx"), 7, None, OP.bitwise_and)
    ts(ti(HI), R("pidx"), 3, 1, OP.arith_shift_right, OP.bitwise_and)
    ts(ti(A), R("pidx"), 5, None, OP.arith_shift_right)
    ts(ti(5), R("pidx"), 1, None, OP.bitwise_and)
    ts(ti(6), R("pidx"), 1, 3, OP.arith_shift_right, OP.bitwise_and)
    tt(ti(7), R("pidx"), ti(G), OP.subtract)
    cp("v", cols("cf", 0, 7), cols("ti", 0, 7))
    ts(ti(8), ti(7), 7, None, OP.bitwise_and)
    ts(c1(7), cf(A), 4.0, cf(G), OP.mult, OP.add)
    ts(c1(0), ti(8), 24.0, None, OP.mult)
    ts(c1(4), cf(A), 64.0, None, OP.mult)
    ts(c1(2), cf(M7), 16.0, None, OP.mult)
    ts(cols("eq", 0, 96), R("gc"), cf(G), 8.0 * C, OP.is_lt, OP.mult)
    ts(c1(5), cf(5), 96.0, cf(HI), OP.mult, OP.add)
    ts(c1(7), cf(HI), 2.0, c1(7), OP.mult, OP.add)
    ts(R("gc"), R("gc"), cf(G), float(C), OP.subtract, OP.mult)
    ts(cols("jb", 0, 3), cols("jb", 0, 3), c1(4), None, OP.add)
    ts(R("lo"), R("ca", S_(0, 4, 2)), c1(0), c1(7), OP.add, OP.add)
    ts(R("lu"), cols("ca", 0, 8), 0.0, c1(2), OP.mult, OP.add)
    ts(c1(6), cf(6), 8.0, None, OP.mult)
    tt(R("gc"), R("gc"), cols("eq", 0, 96), OP.add)

    for name, a in (("pl", 0), ("rt", 48)):
        cp("v", cols(name, 0, 48), cols("li", a, 48))
    gather("s", cols("tab", 0, 2 * C), R("iw"), cols("pl", 0, 48))
    for name, a0 in (("pl", 0), ("rt", 48)):
        for a in range(4):
            cp("v", R(name, S_(48, 96), p=quadrant(a)), R("li", S_(a0, a0 + 48), p=quadrant((a + 1) % 4)))
    gather("s", cols("tab", 2 * C, 2 * C), R("iw"), cols("pl", 48, 48))
    ts(R("lb"), R("cj"), c1(5), c1(6), OP.add, OP.add)
    ts(cols("la", 0, 6), cols("ca", 0, 6), cf(HI), 2.0, OP.add, OP.mult)
    for name in ("pl", "rt"):
        for h in range(2):
            cp("v", R(name, S_(96, 192), p=S_(64 * h, 64 * h + 64)), R(name, S_(0, 96), p=S_(64 - 64 * h, 128 - 64 * h)))
    gather("s", cols("tab", 4 * C, 16 * (SHARE - 96)), R("iw"), cols("pl", 96, SHARE - 96))
    for out, k, o in (("olf", 8.0 * C, OP.is_lt), ("lab", float(C), OP.subtract)):
        op("v", lambda: g.vector.tensor_scalar(T[out][:], T.rt[:].indirect(T.lo[:]), V(cf(G)), k, o, OP.mult), [R(out)], [R("rt"), R("lo"), cf(G)], 60, 1.56)

    def unit_tile(b):
        o = cols("ebt", 512 * b, 512)
        op("g", lambda: g.affine_select(V(o), T.ones[:], [[-1, 512]], OP.is_equal, 0.0, b, 4), [o], [R("ones")], 200, 2)
    for b in range(4):
        unit_tile(b)

    now = {}

    TAB = cols("tab", 0, 8 * C)

    def OF(k):
        return now.get(k) or R("of", S_(96 * k + 31, 96 * k + 96, 32))

    def U(k):
        return cols("offu", 4 * k, 3)

    def lay_labels(q, k):
        for s in range(3):
            cp(q, cols("wk", 256 * s + k, 8 - k), cols("lab", 8 * s + k, 8 - k))

    ts(cols("dm", 0, 128), cols("im", 0, 128), cf(I), None, OP.is_equal)
    ts(cols("la", 6, 6), cols("la", 0, 6), 1.0, None, OP.add)
    ts(R("la", S_(12, 18, 2)), R("la", S_(0, 6, 2)), 2.0, None, OP.add)
    tt(R("lab"), R("lab"), R("olf"), OP.add)
    gather("v", cols("tab", 16 * 182, 160), R("iw"), cols("pl", 182, 10))
    tt(OF(0), R("lab", S_(0, 24, 8)), cols("jb", 0, 3), OP.add)
    lay_labels("v", 1)
    ts(R("la", S_(13, 18, 2)), R("la", S_(7, 12, 2)), cf(HI), 1.0, OP.subtract, OP.add)
    cp("v", U(0), OF(0))

    def clean(q, k):
        gather(q, cols("tab", 8 * C + 48 * k, 48), TAB, U(k))

    def walk(r, first):
        for k in range(first, 7):
            gather_tt(R("wk", S_(k + 9, 768, 16)), TAB, U(k), cols("dm", 0, 48), OP.mult)
            clean("s", k)
            upto("lab%d" % r)
            scan(cols("of", 96 * (k + 1), 96), cols("z32", 0, 96), R("wk", S_(k + 1, 768, 8)))
            now.pop(k + 1, None)
            mark("of%d%d" % (r, k + 1))
            if k < 6:
                cp("v", U(k + 1), OF(k + 1))

    def by_group():
        for s in range(3):
            ts(cols("inv", 8 * s, 8), R("px", S_(40 * s + 4, 40 * s + 40, 5)), cols("of", 96 * 7 + 32 * s + 31, 1), None, OP.max)
        op("v", lambda: g.vector.tensor_scalar(T.wo[:, 0:192], T.tab[:].indirect(T.inv[:, 0:12]), -192.0, None, OP.add),
           [cols("wo", 0, 192)], [R("tab"), cols("inv", 0, 12)], 60, 1.56)
        op("s", lambda: g.scalar.activation(T.wo[:, 192:384], T.tab[:].indirect(T.inv[:, 12:24]), IDENT, bias=-192.0),
           [cols("wo", 192, 192)], [R("tab"), cols("inv", 12, 12)], 80, 1.56)
        op("v", lambda: g.vector.transpose(T.wt[:], T.wo[:]), [R("wt")], [R("wo")], 0, 0.5)

    def score_offsets():
        ts(R("eb"), R("wt", ANY, ANY, 0), 192.0, None, OP.add)

    def signs(r, needs):
        k = r % 2
        stream((210, lambda: gather_tt(cols("oh", 0, 96), R("lab"), cols("la", 6 * k, 6), R("gc"), OP.is_equal), "", needs),
               (210, lambda: gather_tt(cols("oh", 96, 96), R("lab"), cols("la", 6 * k + 6, 6), R("gc"), OP.is_equal), "oh%d" % r),
               (192, lambda: tt(cols("sg", 0, 96), cols("oh", 0, 96), cols("oh", 96, 96), OP.subtract), "sg%d" % r),
               (0, lambda: gather_tt(R("cx"), R("sg"), cols("lh", 16, 8), R("wx"), OP.mult), "cx%d" % r, ("lx",)))

    def coef(x, t):
        return R("co", S_(((0, 0, 0, 1), (0, 2, 0, 3), (0, 4, 6, 7), (14, 15, 8, 9), (17, 18, 10, 11, 12))[x][t], 60, 20))

    def ahead(r, needs):
        k = r % 2
        n = 12 - k

        def df(q):
            return R("df", S_(q, n, 4))

        def res(t, v):
            return R("ofs", S_(192 * t + 96 * v + 31, 192 * t + 96 * v + 96, 32))

        def look(t):
            return [(210, lambda: gather_tt(R("wks", S_(192 * t + 1, 192 * t + 192, 2)), TAB, cols("offs", 6 * t, 6), cols("dm", 0, 96), OP.mult)),
                    (192, lambda: scan(cols("ofs", 192 * t, 192), R("z32"), cols("wks", 192 * t, 192)), "l%d%d" % (r, t))]

        def begin():
            tt(cols("df", 0, n), R("lab", S_(k + 1, 24, 2)), R("lab", S_(k, k + 2 * n, 2)), OP.subtract)
            if r:
                gather("s", R("wks", S_(0, 1024, 32)), R("lab"), cols("lh", 4 + 2 * k, 2))

        def starts():
            for v in range(2):
                tt(cols("a0", 3 * v, 3), OF(k + 2 * v), df(v), OP.add)

        def plain():
            for q, (x, t) in enumerate(((0, 1), (2, 2), (4, 4))):
                cp("s", coef(x, t), df(q))
            for x in range(5):
                cp("s", coef(x, 3), OF(k + x))

        def second():
            cp("v", cols("offs", 12, 3), res(1, 0))
            for s in range(3):
                ts(cols("offs", 15 + s, 1), cols("ofs", 192 + 32 * s + 31, 1), cols("df", 4 * s + 1, 1), None, OP.add)

        def less(x, t, a):
            tt(coef(x, t), a, OF(k + x), OP.subtract)
        stream((64, begin, "begun%d" % r, needs), (128, starts), (64, lambda: cp("v", cols("offs", 0, 6), cols("a0", 0, 6))), *look(0),
               (64, lambda: cp("v", cols("offs", 6, 6), R("ofs", S_(31, 192, 32)))), *look(1), (256, second), *look(2),
               (64, lambda: cp("v", cols("offs", 18, 6), R("ofs", S_(C + 31, C + 192, 32)))), *look(3),
               (128, lambda: (less(4, 1, res(3, 0)), tt(cols("rr", 3, 3), res(3, 1), res(3, 0), OP.subtract))),
               (64, lambda: tt(coef(4, 0), cols("rr", 3, 3), coef(4, 2), OP.subtract), "a%d" % r, ("b%d" % r,)))
        stream((128, lambda: (less(1, 1, res(0, 0)), less(3, 2, res(0, 1))), "", ("l%d0" % r, "of%d%d" % (r - 1, k + 3))),
               (128, lambda: (less(2, 1, res(1, 0)), less(4, 2, res(1, 1))), "", ("l%d1" % r, "of%d%d" % (r - 1, k + 4))),
               (128, lambda: (less(3, 1, res(2, 0)), tt(cols("rr", 0, 3), res(2, 1), res(2, 0), OP.subtract)), "", ("l%d2" % r,)),
               (64, lambda: tt(coef(3, 0), cols("rr", 0, 3), coef(3, 2), OP.subtract), "b%d" % r))
        stream((0, plain, "plain%d" % r, ("sent%d" % (r - 1), "begun%d" % r, "of%d%d" % (r - 1, k + 4))))

    def scores(r, a, n, q, k):
        mm(k, R("uc"), R("upl"), *q_of(r, a, n), n)
        pause(2 * ROOM)
        frombank(q, cols("sct", a, n), k, n)

    def unpack(c, p, banks):
        for b in range(4):
            mm(banks[b], cols("ec", 128 * b, 128), cols("ep", 128 * b, 128), R(c), R(p))

    def scoring_columns():
        op("v", lambda: g.vector.tensor_copy(T.uc[:].bitcast(dt.uint32), T.uq0[:].bitcast(dt.uint32).indirect(T.lu[:])),
           [R("uc")], [R("uq0"), R("lu")], 60, 1.56)
        op("s", lambda: g.scalar.activation(T.upl[:], T.up0[:].indirect(T.lu[:]), COPY), [R("upl")], [R("up0"), R("lu")], 80, 1.56)

    def first_state():
        quant(*q_of(0), R("xb"))
        send_state(0)
        dmas("d_v", [("y", T.vb16[:], T.v[:], [R("vb16")], [R("xb")])])
        dmas("d_w", [("y", T.wcod[:].bitcast(dt.uint8), T.wc[:], [R("wcod")], []), ("y", T.wpl[:], T.ws[:], [R("wpl")], [])])

    def first_scores():
        mm(4, R("uc"), R("upl"), *q_of(0))
        frombank("s", R("sct"), 4)

    def lists_of(a, n, name):
        return [(0, lambda: tt(cols("ys", a, n), cols("bg", a, n), cols("dm", 0, n), OP.mult)),
                (0, lambda: scan(cols("bs", a, n), cols("z16", 0, n), cols("ys", a, n))),
                (0, lambda: cp("v", cols("lh", a // 16, n // 16), R("bs", S_(a + 15, a + n, 16))), name)]

    def factors(s):
        for a, b, step, q in ((1, 6, 2, 0), (16, 20, 3, 0), (7, 12, 2, 1), (15, 19, 3, 1), (13, 14, 1, 2)):
            fill_s(R("bg", S_(20 * s + a, 20 * s + b, step)), 32 * s + 8 * q + 7)

    def followers():
        for e, x in enumerate(FOLLOW):
            affine(cols("bg", 64 + 3 * e, 3), R("cb", S_(0, 12, 4)), 1.0, float(x))
        fill_s(cols("bg", 88, 8), 0.0)
    mark("sent-1")
    mark("lab-1")
    affine(R("wgt"), R("wgt"), 1.0, cf(I))
    ahead(0, ("of-12",))
    signs(0, ())
    stream(*[(0, lambda h=h: gather_tt(cols("eq", 96 * h, 96), R("oh"), cols("lb", 6 * h, 6), cols("wgt", 96 * h, 96), OP.mult), "", ("oh0",)) for h in range(2)],
           (0, lambda: scan(R("iv"), R("z8"), R("eq")), "iv"),
           (0, lambda: (cp("v", R("px", S_(4, 120, 5)), R("iv", S_(7, 192, 8))), cp("s", cols("d", 12, 24), R("iv", S_(7, 192, 8)))), "inv-1"))
    mark("px-1")

    def move_lists():
        affine(c1(9), cf(I), -1.0)
        affine(R("bg", S_(132, 248, 5)), cols("iw", 0, 24), 1.0, 12.0)
        fill_s(R("bg", S_(260, 376, 5)), 96)
        fill_s(R("wx", S_(4, 120, 5)), 1.0)
        fill_s(R("z5", S_(0, 128, 5)), 0.0)
        for s in range(3):
            affine(R("wx", S_(40 * s + 3, 40 * s + 40, 5)), cols("ones", 0, 8), c1(9), -(8.0 * C + 6 * 48 + 16 * s))
    stream((150, lambda: quant(R("uq0"), R("up0"), R("ub")), "uq"), (420, first_state, "q0"), (260, scoring_columns, "uc"), (0, first_scores, "s0"))
    for e, x in enumerate(FOLLOW):
        cp("s", R("wks", S_(96 * e, 96 * e + 96, 32)), R("lab", S_(x, 24, 8)))
    for name, a, n, c in (("co", 0, 64, 0), ("bg", 0, 64, 96), ("z16", 0, C, 1), ("wx", 0, 128, 48), ("z5", 0, 128, 1), ("bg", 248, 8, 0), ("bg", 376, 8, 0)):
        fill_s(cols(name, a, n), c)
    fill_s(R("wgt", S_(7, 192, 8)), 0.0)
    for s in range(3):
        factors(s)
    followers()
    fill_s(R("z16", S_(0, C, 16)), 0.0)
    move_lists()
    affine(cols("bg", 96, 32), cols("bg", 64, 32), 1.0, 1.0)
    for name, a, n, c in (("es", 96, 16, 0), ("sg", 96, 16, 1)):
        fill_s(cols(name, a, n), c)
    affine(c1(1), cf(M7), 17.0)
    stream((0, lambda: ts(R("le"), cols("ce", 0, 6), c1(1), None, OP.add), "le"), *lists_of(0, 128, "lh"))
    stream(*lists_of(256, 128, "lx"))
    stream(*lists_of(128, 128, "l1"))
    mark("lf")
    stream((0, lambda: ts(cols("dm", 128, C - 128), cols("im", 128, C - 128), cf(I), None, OP.is_equal), "dm"),
           *[(150, lambda b=b: quant(cols("ec", 128 * b, 128), cols("ep", 128 * b, 128), cols("ebt", 512 * b, 512)), "e%d" % b, ("lx",)) for b in range(4)])
    cuts = [SHARE + 2 * ((182 - SHARE) * x // (2 * len(EARLY))) for x in range(len(EARLY))] + [182]
    for x, names in enumerate(EARLY):
        upto(*names)
        gather("v", cols("tab", 16 * cuts[x], 16 * (cuts[x + 1] - cuts[x])), R("iw"), cols("pl", cuts[x], cuts[x + 1] - cuts[x]))
    walk(-1, 0)
    upto("inv-1")
    by_group()
    upto("s0")
    score_offsets()

    def own_numbers(r):
        unpack("qc%d" % r, "qp%d" % r, (0, 1, 6, 7))
        for b in range(2):
            frombank("s", cols("fb", C * b, C), b)
        unpack("lc%d" % r, "lp%d" % r, (2, 3, 0, 1))

    for r in range(3):
        k = r % 2
        n = 12 - k
        gather("v", cols("ef", 0, 192), R("sct"), cols("eb", 0, 12))
        gather("s", cols("ef", 192, 192), R("sct"), cols("eb", 12, 12))
        stream((0, lambda r=r: own_numbers(r), "own%d" % r, ("e3",)))
        tr(R("et"), R("ef"))
        pause()
        upto("sg%d" % r, "le")
        gather_tt(R("sel"), R("et"), R("le"), cols("sg", 0, 96), OP.mult)
        pause()
        scan(cols("es", 0, 96), cols("z8", 0, 96), R("sel"))
        upto("a%d" % r, "plain%d" % r, "lh")
        m = cols("m", 0, n)
        op("v", lambda: g.vector.tensor_scalar(T.hz[:], T.es[:].indirect(T.lh[:, 0:4]), 0.0, None, OP.is_gt), [R("hz")], [R("es"), cols("lh", 0, 4)], 60, 1.56)
        upto("px%d" % (r - 1))
        ts(cols("d", 0, 12), R("es", S_(7, 96, 8)), 0.0, None, OP.is_gt)
        scan(cols("hs", 64 * r, 64), R("hz"), R("co"))
        tt(m, cols("d", 0, n), cols("df", 0, n), OP.mult)

        def term(t, s=None, r=r):
            return R("hs", S_(64 * r + t, 64 * r + 60, 20)) if s is None else cols("hs", 64 * r + 20 * s + t, 1)
        for s in range(3):
            ts(cols("offu", 4 * (k + 4) + s, 1), term(19, s), term(11, s), term(13, s), OP.add, OP.add)
        tt(R("wk", S_(k + 5, 768, 256)), R("lab", S_(k + 5, 24, 8)), R("m", S_(2, n, 4)), OP.subtract)
        tt(R("lab", S_(k, k + 2 * n, 2)), R("lab", S_(k, k + 2 * n, 2)), m, OP.add)
        now.update({k: term(1), k + 1: term(3)})
        now.update({k + x: cols("os", 12 * r + 3 * (x - 2), 3) for x in (2, 3, 4)})

        def labels(k=k, m=m):
            tt(R("lab", S_(k + 1, 24, 2)), R("lab", S_(k + 1, 24, 2)), m, OP.subtract)
            lay_labels("s", k + 6)

        def sums(k=k, term=term):
            tt(OF(k + 2), term(5), term(7), OP.add)
            tt(OF(k + 3), term(16), term(9), OP.add)

        def kept(k, x):
            for y in (x, x + 1):
                cp("v", U(k + y), OF(k + y))
            for y in (x, x + 1):
                clean("s", k + y)
        stream((0, lambda: gather_tt(R("mv"), R("d"), cols("lh", 8, 8), R("cx"), OP.mult), "mv%d" % r, ("cx%d" % r, "l1")),
               (0, lambda: scan(R("px"), R("z5"), R("mv")), "inv%d" % r),
               (0, lambda: cp("s", cols("d", 12, 24), R("px", S_(4, 120, 5))), "px%d" % r, ("kept%d" % r,)), first=True)
        stream((0, labels, "lab%d" % r), (0, sums), (0, lambda k=k: kept(k, 0)), (0, lambda k=k: kept(k, 2)),
               (0, lambda k=k: cp("v", OF(k + 4), U(k + 4)), "kept%d" % r), first=True)
        for x in range(k + 5):
            mark("of%d%d" % (r, x))
        if r < 2:
            ahead(r + 1, ("kept%d" % r, "lf"))
            signs(r + 1, ("mv%d" % r, "lab%d" % r))
        else:
            stream((0, lambda: ts(R("pa"), cols("lab", 0, 24), 1.0 / C, cf(G), OP.mult, OP.add), "", ("kept2",)),
                   (0, lambda: ts(R("pe"), R("pa"), 8.0, -8.0, OP.is_ge, OP.mult)),
                   (0, lambda: [tt(R("olf", S_(s, 24, 3)), cols("pa", 8 * s, 8), cols("pe", 8 * s, 8), OP.add) for s in range(3)]),
                   (64, lambda: tr(R("olt"), R("olf"))),
                   (0, lambda: dmas("d_ol", [("y", T.ol[:, 96 * a:96 * a + 96], T.olt[32 * a:32 * a + 24, :], [], [R("olt")]) for a in range(4)])),
                   (150, lambda: quant(R("vq"), R("vp"), R("vb16")), "v"))
        walk(r, k + 4)
        upto("inv%d" % r, "kept%d" % r, "own%d" % r, "dm")
        by_group()
        for a in range(4):
            for c in range(4):
                cp("vs"[c % 2], R("lf", S_(6 * a, 6 * a + 6), p=quadrant(c)), R("wt", ANY, S_(2 * c, 2 * c + 2), 0, p=quadrant(a)))
        pause()
        ts(R("al%d" % r), R("lf"), 192.0, None, OP.add)
        remote(r, T["zl%d" % r][:], T["al%d" % r][:], "ra%d" % r, [R("al%d" % r)])
        for b in range(4) if DPS else (0, 2, 3):
            frombank("s", cols("dp", C * b, C), (2, 3, 0, 1)[b])
        mark("sent%d" % r)
        if r < 2:
            upto("plain%d" % (r + 1))
        if r < 2:
            score_offsets()
        pause()
        gather_tt(R("bg"), TAB, R("al%d" % r), R("dm"), OP.mult)
        pause()
        if not DPS:
            frombank("v", cols("dp", C, C), 3)
        pause()
        zt, zc, zp, zl = "zt%d" % r, "zc%d" % r, "zp%d" % r, "zl%d" % r

        def mosaic(h, b):
            a, w = ZP[h]
            gather("vs"[b // 2], R(zt, S_(4 * a + b, 4 * (a + w), 4)), cols("dp", C * b, C), cols(zl, a // 16, w // 16))

        def layer(h, b, k):
            a, w = ZP[h]
            mm(k, cols("wcod", 128 * b, 128), cols("wpl", 128 * b, 128), cols(zc, a, w), cols(zp, a, w), w)

        def products(q, h, b, k):
            a, w = ZP[h]
            frombank(q, cols("rs", C * b + a, w), k, w, 0.03125)

        def quant_z(h):
            a, w = ZP[h]
            quant(cols(zc, a, w), cols(zp, a, w), cols(zt, 4 * a, 4 * w))
        for h, b in ((0, 0), (0, 2), (0, 1), (0, 3), (1, 0), (1, 2), (1, 3)):
            mosaic(h, b)
        quant_z(0)
        for b, kb in ((2, 0), (3, 1), (0, 2), (1, 3)):
            layer(0, b, kb)
            products("s", 0, b, kb)
        mosaic(1, 1)
        pause()
        quant_z(1)
        scan(R("bs"), R("z16"), R("bg"))
        nx = "xs%d" % (r + 1)

        def place(h, b):
            a, w = XP[h]
            return R(nx, S_(4 * a + b, 4 * (a + w), 4))

        def pick(h, b):
            a, w = XP[h]
            if b < 2:
                gather_tt(place(h, b), cols("rs", C * b, C), cols("bl", a // 16, w // 16), cols("fb", C * b + a, w), OP.add)
            else:
                gather("s", cols("gs", C * (b - 2) + a, w), cols("rs", C * b, C), cols("bl", a // 16, w // 16))

        def add(h, b):
            a, w = XP[h]
            o, i = place(h, b), cols("gs", C * (b - 2) + a, w)
            op("v", lambda: g.vector.tensor_tensor(V(o), V(i), bank(4 + b, w, a), OP.add), [o], [i, ("ps", 4 + b)])
        for b, kb in ((0, 4), (2, 5), (1, 0), (3, 1)):
            layer(1, b, kb)
            products(RQ[b], 1, b, kb)
            if b == 0:
                cp("v", R("bl"), R("bs", S_(15, C, 16)))
        for h in range(2):
            for b in range(4):
                pick(h, b)
        for h, b in ((0, 2), (0, 3), (1, 2), (1, 3))[:3 if r == 2 else 4]:
            add(h, b)
        for h in range(2):
            a, w = XP[h]
            if r == 2 and h:
                add(1, 3)
            quant(*q_of(r + 1, a, w), cols(nx, 4 * a, 4 * w))
            if r == 2:
                upto("v")
                mm(4 + h, R("vq"), R("vp"), *q_of(3, a, w), w)
                dmas("d_o%d" % h, [("y", T.oc[:, 4 * a:4 * (a + w)], T.qc3[:, a:a + w].bitcast(dt.uint8), [], [q_of(3, a, w)[0]])])
            elif h == 0:
                mm(4, R("uc"), R("upl"), *q_of(r + 1, a, w), w)
                frombank("s", cols("sct", a, w), 4, w)
            else:
                send_state(r + 1)
                scores(r + 1, a, w, "v", 5)
                pause()

    for h in range(2):
        a, w = XP[h]
        frombank("sv"[h], cols("ys", a, w), 4 + h, w)
        if h:
            dmas("d_s", [("ys"[k % 2], T.osc[4 * k:4 * k + 4, :], T.qp3[32 * k:32 * k + 4, :], [], [R("qp3")]) for k in range(4)])
        dmas("d_y%d" % h, [("sy"[h], T.y[:, a:a + w], T.ys[:, a:a + w], [], [cols("ys", a, w)])])
    finish()
